import numpy as np
import ml_dtypes


def mxq(x, axis, fmt="e4m3"):
    dtype, down = {"e4m3": (ml_dtypes.float8_e4m3fn, 7), "e5m2": (ml_dtypes.float8_e5m2, 14)}[fmt]
    v = np.moveaxis(np.asarray(x, np.float32).astype(ml_dtypes.bfloat16).astype(np.float64), axis, -1)
    blocks = v.reshape(v.shape[:-1] + (-1, 32))
    amax = np.abs(blocks).max(-1, keepdims=True)
    byte = np.maximum(np.where(amax > 0, np.frexp(amax)[1] - 1 + 127, 0) - down, 1)
    scale = np.exp2(byte - 127.0)
    codes = (blocks / scale).astype(np.float32).astype(dtype).astype(np.float64)
    return np.moveaxis((codes * scale).reshape(v.shape), -1, axis)


WIDE = False


def mx_kscale(k):
    if not WIDE:
        return np.ones(k)
    levels = np.array([30, -30])
    if k % 512:
        return np.exp2(np.random.permutation(np.resize(levels, k // 32))).repeat(32)
    a = np.empty((k // 512, 16))
    for p in range(k // 512):
        a[p, :8] = np.random.permutation(np.resize(levels, 8))
        for g in range(8):
            far = levels[np.abs(levels - a[p, g]) >= 10]
            a[p, g + 8] = far[np.random.randint(len(far))]
    return np.exp2(a.ravel()).repeat(32)


def f64(x):
    return np.asarray(x).astype(np.float64)


K, N, T = 1024, 1024, 512


def setup_inputs():
    n = np.random.standard_normal
    s = mx_kscale(K)[:, None]
    m = np.exp(0.5 * n((1, T)))
    return {
        "g": (m * n((K, T)) * s).astype(np.float32),
        "w": (n((K, N)) / np.sqrt(K) / s).astype(np.float32),
    }


def reference(g, w):
    g_q_ = mxq(f64(g), 0, "e5m2")
    g_r_ = mxq(f64(g) - g_q_, 0, "e4m3")
    w_ = mxq(f64(w), 0, "e4m3")
    dx = w_.T @ g_q_ + w_.T @ g_r_
    return dx

@@ -1,0 +1,214 @@
+from contextlib import ExitStack
+
+import concourse.mybir as mybir
+from concourse.masks import make_identity
+
+K, N, T = 1024, 1024, 512
+FLOPS = 2 * 2 * K * N * T
+
+F32 = mybir.dt.float32
+BF16 = mybir.dt.bfloat16
+U32 = mybir.dt.uint32
+U8 = mybir.dt.uint8
+E4M3 = mybir.dt.float8_e4m3fn_x4
+E5M2 = mybir.dt.float8_e5m2_x4
+
+P = 128
+PACK = 4
+K_PASS = P * PACK
+PASSES = K // K_PASS
+HALF = T // 2
+W_COLS = 256
+QUARTERS = N // W_COLS
+RUN = 4
+
+
+def tile_mix_tierg_none_kernel(tc, g, w, out):
+    nc = tc.nc
+    with ExitStack() as ctx:
+        sb = ctx.enter_context(tc.tile_pool(name="sb", bufs=1))
+        ps = ctx.enter_context(tc.psum_pool(name="ps", bufs=1))
+        ctx.enter_context(tc.manual_schedule())
+
+        def tiles(label, count, shape, dtype):
+            return [sb.tile(shape, dtype, name=label + str(i), align_bytes=64) for i in range(count)]
+
+        g_flat = tiles("g_raw", PASSES, [P, 2 * PACK * HALF], F32)
+
+        def g_half(c, h):
+            return g_flat[c][:, h * PACK * HALF : (h + 1) * PACK * HALF].rearrange("p (j t) -> p j t", j=PACK)
+
+        g_bf = tiles("g_bf", PASSES, [P, T, PACK], BF16)
+        gq_codes = tiles("gq_codes", PASSES, [P, T], U32)
+        gq_scales = tiles("gq_scales", PASSES, [P, T], U8)
+        r_rows = tiles("r_rows", PASSES, [P, PACK, T], BF16)
+        r_bf = tiles("r_bf", PASSES, [P, T, PACK], BF16)
+        gr_codes = tiles("gr_codes", PASSES, [P, T], U32)
+        gr_scales = tiles("gr_scales", PASSES, [P, T], U8)
+        pieces = PASSES * QUARTERS
+        w_raw = tiles("w_raw", pieces, [P, PACK, W_COLS], F32)
+        w_bf = tiles("w_bf", pieces, [P, W_COLS, PACK], BF16)
+        w_codes = tiles("w_codes", pieces, [P, W_COLS], U32)
+        w_scales = tiles("w_scales", pieces, [P, W_COLS], U8)
+        result = tiles("result", N // P, [P, T], F32)
+        eye = sb.tile([P, P], BF16, align_bytes=64)
+        eye_bf = sb.tile([P, PACK * (K_PASS + 1)], BF16, align_bytes=64)
+        eye_codes = sb.tile([P, K_PASS], U32, align_bytes=64)
+        eye_scales = sb.tile([P, K_PASS], U8, align_bytes=64)
+
+        def bank(b, label):
+            return ps.tile([P, T], F32, name=label, tag="bank" + str(b))
+
+        def interleave(engine, dst, src):
+            d = dst.rearrange("p (c i) j -> p c j i", i=RUN)
+            s = src.rearrange("p j (c i) -> p c j i", i=RUN)
+            if engine == "v":
+                nc.vector.tensor_copy(out=d, in_=s)
+            else:
+                nc.scalar.copy(out=d, in_=s)
+
+        def quantize(codes, scales, values, fmt):
+            nc.vector.quantize_mx(out=codes.bitcast(fmt), scales=scales, in_=values.rearrange("p c j -> p (c j)"))
+
+        def cast_g(engine, c, h, lo, hi):
+            interleave(engine, g_bf[c][:, h * HALF + lo : h * HALF + hi, :], g_half(c, h)[:, :, lo:hi])
+
+        def quant_g(c, lo, hi):
+            quantize(gq_codes[c][:, lo:hi], gq_scales[c][:, lo:hi], g_bf[c][:, lo:hi, :], E5M2)
+
+        back = {}
+
+        def dequant(c):
+            for j in range(PACK):
+                back[c, j] = bank(PACK * c + j, "back")
+                cols = slice(j * P, (j + 1) * P)
+                nc.tensor.matmul_mx(
+                    out=back[c, j][:], lhsT=eye_codes[:, cols].bitcast(E4M3), lhsT_scale=eye_scales[:, cols],
+                    rhs=gq_codes[c][:].bitcast(E5M2), rhs_scale=gq_scales[c][:], start=True, stop=True,
+                )
+
+        def subtract(c, j):
+            nc.vector.tensor_tensor(
+                out=r_rows[c][:, j, :].rearrange("p (h t) -> p h t", h=2),
+                in0=g_flat[c][:].rearrange("p (h j t) -> p h j t", h=2, j=PACK)[:, :, j, :],
+                in1=back[c, j][:].rearrange("p (h t) -> p h t", h=2),
+                op=mybir.AluOpType.subtract,
+            )
+
+        def pack_r(engine, c, lo, hi):
+            interleave(engine, r_bf[c][:, lo:hi, :], r_rows[c][:, :, lo:hi])
+
+        def quant_r(c):
+            quantize(gr_codes[c][:], gr_scales[c][:], r_bf[c][:], E4M3)
+
+        def cast_w(engine, c, q, lo=0, hi=W_COLS):
+            i = PASSES * q + c
+            interleave(engine, w_bf[i][:, lo:hi, :], w_raw[i][:, :, lo:hi])
+
+        def quant_w(c, q):
+            i = PASSES * q + c
+            quantize(w_codes[i][:], w_scales[i][:], w_bf[i][:], E4M3)
+
+        acc = {}
+        done = {}
+
+        def product(tier, c, q, which=(0, 1)):
+            i = PASSES * q + c
+            codes, scales, fmt = (gq_codes, gq_scales, E5M2) if tier == "q" else (gr_codes, gr_scales, E4M3)
+            for n in [2 * q + x for x in which]:
+                if n not in acc:
+                    acc[n] = bank(n, "acc")
+                    done[n] = 0
+                cols = slice((n % 2) * P, (n % 2 + 1) * P)
+                nc.tensor.matmul_mx(
+                    out=acc[n][:], lhsT=w_codes[i][:, cols].bitcast(E4M3), lhsT_scale=w_scales[i][:, cols],
+                    rhs=codes[c][:].bitcast(fmt), rhs_scale=scales[c][:],
+                    start=done[n] == 0, stop=done[n] == 2 * PASSES - 1,
+                )
+                done[n] = done[n] + 1
+
+        def finish(engine, n):
+            if engine == "v":
+                nc.vector.tensor_copy(out=result[n][:], in_=acc[n][:])
+            else:
+                nc.scalar.copy(out=result[n][:], in_=acc[n][:])
+            nc.sync.dma_start(out=out[n * P : (n + 1) * P, :], in_=result[n][:])
+
+        for c in range(PASSES):
+            rows = g[c * K_PASS : (c + 1) * K_PASS, :].rearrange("(p j) t -> p j t", j=PACK)
+            for h in range(2):
+                nc.sync.dma_start(out=g_half(c, h), in_=rows[:, :, h * HALF : (h + 1) * HALF])
+        for q in range(QUARTERS):
+            for c in range(PASSES):
+                rows = w[c * K_PASS : (c + 1) * K_PASS, :].rearrange("(p j) n -> p j n", j=PACK)
+                nc.sync.dma_start(out=w_raw[PASSES * q + c][:], in_=rows[:, :, q * W_COLS : (q + 1) * W_COLS])
+
+        make_identity(nc, eye[:])
+        nc.vector.memset(eye_bf[:].bitcast(U32), 0)
+        diagonal = eye_bf[:].rearrange("p (j r) -> p j r", j=PACK)[:, :, 0:K_PASS:PACK]
+        nc.scalar.copy(out=diagonal, in_=eye[:].unsqueeze(1).to_broadcast([P, PACK, P]))
+        nc.vector.quantize_mx(out=eye_codes[:].bitcast(E4M3), scales=eye_scales[:], in_=eye_bf[:, 0 : PACK * K_PASS])
+
+        cast_g("v", 0, 0, 0, HALF)
+        quant_g(0, 0, HALF)
+        cast_g("s", 0, 1, 160, HALF)
+        cast_g("v", 0, 1, 0, 160)
+        quant_g(0, HALF, T)
+        dequant(0)
+        cast_g("v", 1, 0, 0, HALF)
+        cast_g("s", 1, 1, 0, HALF)
+        for j in range(PACK):
+            subtract(0, j)
+        quant_g(1, 0, T)
+        dequant(1)
+        cast_w("s", 0, 0)
+        pack_r("v", 0, 0, T)
+        quant_w(0, 0)
+        product("q", 0, 0)
+        cast_w("s", 1, 0)
+        subtract(1, 0)
+        quant_r(0)
+        product("r", 0, 0)
+        subtract(1, 1)
+        quant_w(1, 0)
+        product("q", 1, 0)
+        cast_w("s", 0, 1)
+        subtract(1, 2)
+        subtract(1, 3)
+        quant_w(0, 1)
+        product("q", 0, 1)
+        product("r", 0, 1)
+        cast_w("s", 1, 1)
+        pack_r("s", 1, 320, T)
+        pack_r("v", 1, 0, 320)
+        quant_w(1, 1)
+        product("q", 1, 1)
+        cast_w("s", 0, 2)
+        quant_r(1)
+        product("r", 1, 0)
+        product("r", 1, 1)
+        cast_w("v", 1, 2)
+        quant_w(0, 2)
+        product("q", 0, 2)
+        product("r", 0, 2)
+        finish("s", 0)
+        cast_w("v", 0, 3)
+        quant_w(1, 2)
+        product("q", 1, 2)
+        product("r", 1, 2)
+        finish("s", 1)
+        finish("s", 2)
+        cast_w("v", 1, 3)
+        quant_w(0, 3)
+        product("q", 0, 3)
+        product("r", 0, 3)
+        finish("s", 3)
+        quant_w(1, 3)
+        product("q", 1, 3, (0,))
+        product("r", 1, 3, (0,))
+        product("q", 1, 3, (1,))
+        product("r", 1, 3, (1,))
+        finish("v", 4)
+        finish("s", 5)
+        finish("v", 6)
+        finish("s", 7)

@@ -138,77 +138,82 @@ def tile_mix_tierg_none_kernel(tc, g, w, out):
             rows = g[c * K_PASS : (c + 1) * K_PASS, :].rearrange("(p j) t -> p j t", j=PACK)
             for h in range(2):
                 nc.sync.dma_start(out=g_half(c, h), in_=rows[:, :, h * HALF : (h + 1) * HALF])
-        for q in range(QUARTERS):
-            for c in range(PASSES):
+        for c in range(PASSES):
+            for q in range(QUARTERS):
                 rows = w[c * K_PASS : (c + 1) * K_PASS, :].rearrange("(p j) n -> p j n", j=PACK)
                 nc.sync.dma_start(out=w_raw[PASSES * q + c][:], in_=rows[:, :, q * W_COLS : (q + 1) * W_COLS])
 
         make_identity(nc, eye[:])
         nc.vector.memset(eye_bf[:].bitcast(U32), 0)
         diagonal = eye_bf[:].rearrange("p (j r) -> p j r", j=PACK)[:, :, 0:K_PASS:PACK]
-        nc.scalar.copy(out=diagonal, in_=eye[:].unsqueeze(1).to_broadcast([P, PACK, P]))
+        nc.vector.tensor_copy(out=diagonal, in_=eye[:].unsqueeze(1).to_broadcast([P, PACK, P]))
         nc.vector.quantize_mx(out=eye_codes[:].bitcast(E4M3), scales=eye_scales[:], in_=eye_bf[:, 0 : PACK * K_PASS])
+
+        def close(q):
+            for x in range(2):
+                product("q", 1, q, (x,))
+                product("r", 1, q, (x,))
 
         cast_g("v", 0, 0, 0, HALF)
         quant_g(0, 0, HALF)
-        cast_g("s", 0, 1, 160, HALF)
-        cast_g("v", 0, 1, 0, 160)
+        cast_g("s", 0, 1, 128, HALF)
+        cast_g("v", 0, 1, 0, 128)
         quant_g(0, HALF, T)
         dequant(0)
         cast_g("v", 1, 0, 0, HALF)
         cast_g("s", 1, 1, 0, HALF)
-        for j in range(PACK):
-            subtract(0, j)
+        subtract(0, 0)
+        subtract(0, 1)
+        subtract(0, 2)
         quant_g(1, 0, T)
         dequant(1)
+        subtract(0, 3)
         cast_w("s", 0, 0)
-        pack_r("v", 0, 0, T)
         quant_w(0, 0)
         product("q", 0, 0)
-        cast_w("s", 1, 0)
-        subtract(1, 0)
-        quant_r(0)
-        product("r", 0, 0)
-        subtract(1, 1)
-        quant_w(1, 0)
-        product("q", 1, 0)
         cast_w("s", 0, 1)
-        subtract(1, 2)
-        subtract(1, 3)
+        pack_r("v", 0, 0, 256)
+        pack_r("s", 0, 256, T)
+        subtract(1, 0)
         quant_w(0, 1)
         product("q", 0, 1)
+        subtract(1, 1)
+        quant_r(0)
+        product("r", 0, 0)
         product("r", 0, 1)
-        cast_w("s", 1, 1)
-        pack_r("s", 1, 320, T)
-        pack_r("v", 1, 0, 320)
-        quant_w(1, 1)
-        product("q", 1, 1)
         cast_w("s", 0, 2)
-        quant_r(1)
-        product("r", 1, 0)
-        product("r", 1, 1)
-        cast_w("v", 1, 2)
+        subtract(1, 2)
         quant_w(0, 2)
         product("q", 0, 2)
         product("r", 0, 2)
-        finish("s", 0)
-        cast_w("v", 0, 3)
-        quant_w(1, 2)
-        product("q", 1, 2)
-        product("r", 1, 2)
-        finish("s", 1)
-        finish("s", 2)
-        cast_w("v", 1, 3)
+        cast_w("s", 0, 3)
+        subtract(1, 3)
+        cast_w("s", 1, 0)
         quant_w(0, 3)
         product("q", 0, 3)
         product("r", 0, 3)
-        finish("s", 3)
+        pack_r("s", 1, 384, T)
+        pack_r("v", 1, 0, 384)
+        quant_w(1, 0)
+        product("q", 1, 0)
+        quant_r(1)
+        cast_w("s", 1, 1)
+        product("r", 1, 0)
+        cast_w("v", 1, 2, 0, P)
+        quant_w(1, 1)
+        close(1)
+        finish("s", 0)
+        finish("s", 1)
+        cast_w("v", 1, 2, P, W_COLS)
+        cast_w("v", 1, 3, 0, P)
+        quant_w(1, 2)
+        close(2)
+        finish("s", 2)
+        cast_w("v", 1, 3, P, W_COLS)
         quant_w(1, 3)
-        product("q", 1, 3, (0,))
-        product("r", 1, 3, (0,))
-        product("q", 1, 3, (1,))
-        product("r", 1, 3, (1,))
-        finish("v", 4)
-        finish("s", 5)
-        finish("v", 6)
-        finish("s", 7)
+        close(3)
+        finish("s", 3)
+        finish("s", 4)
+        finish("v", 5)
+        finish("s", 6)
+        finish("v", 7)

@@ -20,11 +20,18 @@ PASSES = K // K_PASS
 HALF = T // 2
 W_COLS = 256
 QUARTERS = N // W_COLS
+LAST = QUARTERS - 1
 RUN = 4
+
+G_SPLIT = 128
+R0_SPLIT = 256
+R1_SPLIT = 384
 
 
 def tile_mix_tierg_none_kernel(tc, g, w, out):
     nc = tc.nc
+    vector_copy = nc.vector.tensor_copy
+    scalar_copy = nc.scalar.copy
     with ExitStack() as ctx:
         sb = ctx.enter_context(tc.tile_pool(name="sb", bufs=1))
         ps = ctx.enter_context(tc.psum_pool(name="ps", bufs=1))
@@ -33,11 +40,7 @@ def tile_mix_tierg_none_kernel(tc, g, w, out):
         def tiles(label, count, shape, dtype):
             return [sb.tile(shape, dtype, name=label + str(i), align_bytes=64) for i in range(count)]
 
-        g_flat = tiles("g_raw", PASSES, [P, 2 * PACK * HALF], F32)
-
-        def g_half(c, h):
-            return g_flat[c][:, h * PACK * HALF : (h + 1) * PACK * HALF].rearrange("p (j t) -> p j t", j=PACK)
-
+        g_raw = tiles("g_raw", PASSES, [P, 2 * PACK * HALF], F32)
         g_bf = tiles("g_bf", PASSES, [P, T, PACK], BF16)
         gq_codes = tiles("gq_codes", PASSES, [P, T], U32)
         gq_scales = tiles("gq_scales", PASSES, [P, T], U8)
@@ -59,89 +62,102 @@ def tile_mix_tierg_none_kernel(tc, g, w, out):
         def bank(b, label):
             return ps.tile([P, T], F32, name=label, tag="bank" + str(b))
 
-        def interleave(engine, dst, src):
-            d = dst.rearrange("p (c i) j -> p c j i", i=RUN)
-            s = src.rearrange("p j (c i) -> p c j i", i=RUN)
-            if engine == "v":
-                nc.vector.tensor_copy(out=d, in_=s)
-            else:
-                nc.scalar.copy(out=d, in_=s)
+        def g_half(c, h):
+            return g_raw[c][:, h * PACK * HALF : (h + 1) * PACK * HALF].rearrange("p (j t) -> p j t", j=PACK)
+
+        def pack(copy, dst, src):
+            copy(out=dst.rearrange("p (c i) j -> p c j i", i=RUN), in_=src.rearrange("p j (c i) -> p c j i", i=RUN))
 
         def quantize(codes, scales, values, fmt):
             nc.vector.quantize_mx(out=codes.bitcast(fmt), scales=scales, in_=values.rearrange("p c j -> p (c j)"))
 
-        def cast_g(engine, c, h, lo, hi):
-            interleave(engine, g_bf[c][:, h * HALF + lo : h * HALF + hi, :], g_half(c, h)[:, :, lo:hi])
+        def cast_g(copy, c, h, lo, hi):
+            pack(copy, g_bf[c][:, h * HALF + lo : h * HALF + hi, :], g_half(c, h)[:, :, lo:hi])
 
         def quant_g(c, lo, hi):
             quantize(gq_codes[c][:, lo:hi], gq_scales[c][:, lo:hi], g_bf[c][:, lo:hi, :], E5M2)
 
-        back = {}
+        gq_values = {}
 
         def dequant(c):
             for j in range(PACK):
-                back[c, j] = bank(PACK * c + j, "back")
+                gq_values[c, j] = bank(PACK * c + j, "gq_values")
                 cols = slice(j * P, (j + 1) * P)
                 nc.tensor.matmul_mx(
-                    out=back[c, j][:], lhsT=eye_codes[:, cols].bitcast(E4M3), lhsT_scale=eye_scales[:, cols],
-                    rhs=gq_codes[c][:].bitcast(E5M2), rhs_scale=gq_scales[c][:], start=True, stop=True,
+                    out=gq_values[c, j][:],
+                    lhsT=eye_codes[:, cols].bitcast(E4M3),
+                    lhsT_scale=eye_scales[:, cols],
+                    rhs=gq_codes[c][:].bitcast(E5M2),
+                    rhs_scale=gq_scales[c][:],
+                    start=True,
+                    stop=True,
                 )
 
         def subtract(c, j):
             nc.vector.tensor_tensor(
                 out=r_rows[c][:, j, :].rearrange("p (h t) -> p h t", h=2),
-                in0=g_flat[c][:].rearrange("p (h j t) -> p h j t", h=2, j=PACK)[:, :, j, :],
-                in1=back[c, j][:].rearrange("p (h t) -> p h t", h=2),
+                in0=g_raw[c][:].rearrange("p (h j t) -> p h j t", h=2, j=PACK)[:, :, j, :],
+                in1=gq_values[c, j][:].rearrange("p (h t) -> p h t", h=2),
                 op=mybir.AluOpType.subtract,
             )
 
-        def pack_r(engine, c, lo, hi):
-            interleave(engine, r_bf[c][:, lo:hi, :], r_rows[c][:, :, lo:hi])
+        def pack_r(copy, c, lo, hi):
+            pack(copy, r_bf[c][:, lo:hi, :], r_rows[c][:, :, lo:hi])
 
         def quant_r(c):
             quantize(gr_codes[c][:], gr_scales[c][:], r_bf[c][:], E4M3)
 
-        def cast_w(engine, c, q, lo=0, hi=W_COLS):
+        def cast_w(copy, c, q, lo=0, hi=W_COLS):
             i = PASSES * q + c
-            interleave(engine, w_bf[i][:, lo:hi, :], w_raw[i][:, :, lo:hi])
+            pack(copy, w_bf[i][:, lo:hi, :], w_raw[i][:, :, lo:hi])
 
         def quant_w(c, q):
             i = PASSES * q + c
             quantize(w_codes[i][:], w_scales[i][:], w_bf[i][:], E4M3)
 
+        first_tier = (gq_codes, gq_scales, E5M2)
+        second_tier = (gr_codes, gr_scales, E4M3)
         acc = {}
-        done = {}
+        issued = {}
 
-        def product(tier, c, q, which=(0, 1)):
+        def product(tier, c, q, sides=(0, 1)):
             i = PASSES * q + c
-            codes, scales, fmt = (gq_codes, gq_scales, E5M2) if tier == "q" else (gr_codes, gr_scales, E4M3)
-            for n in [2 * q + x for x in which]:
+            codes, scales, fmt = tier
+            for side in sides:
+                n = 2 * q + side
                 if n not in acc:
                     acc[n] = bank(n, "acc")
-                    done[n] = 0
-                cols = slice((n % 2) * P, (n % 2 + 1) * P)
+                    issued[n] = 0
+                cols = slice(side * P, (side + 1) * P)
                 nc.tensor.matmul_mx(
-                    out=acc[n][:], lhsT=w_codes[i][:, cols].bitcast(E4M3), lhsT_scale=w_scales[i][:, cols],
-                    rhs=codes[c][:].bitcast(fmt), rhs_scale=scales[c][:],
-                    start=done[n] == 0, stop=done[n] == 2 * PASSES - 1,
+                    out=acc[n][:],
+                    lhsT=w_codes[i][:, cols].bitcast(E4M3),
+                    lhsT_scale=w_scales[i][:, cols],
+                    rhs=codes[c][:].bitcast(fmt),
+                    rhs_scale=scales[c][:],
+                    start=issued[n] == 0,
+                    stop=issued[n] == 2 * PASSES - 1,
                 )
-                done[n] = done[n] + 1
+                issued[n] = issued[n] + 1
 
-        def finish(engine, n):
-            if engine == "v":
-                nc.vector.tensor_copy(out=result[n][:], in_=acc[n][:])
-            else:
-                nc.scalar.copy(out=result[n][:], in_=acc[n][:])
+        def close(q):
+            for side in range(2):
+                product(first_tier, 1, q, (side,))
+                product(second_tier, 1, q, (side,))
+
+        def finish(copy, n):
+            copy(out=result[n][:], in_=acc[n][:])
             nc.sync.dma_start(out=out[n * P : (n + 1) * P, :], in_=result[n][:])
 
         for c in range(PASSES):
             rows = g[c * K_PASS : (c + 1) * K_PASS, :].rearrange("(p j) t -> p j t", j=PACK)
             for h in range(2):
                 nc.sync.dma_start(out=g_half(c, h), in_=rows[:, :, h * HALF : (h + 1) * HALF])
-        for c in range(PASSES):
-            for q in range(QUARTERS):
-                rows = w[c * K_PASS : (c + 1) * K_PASS, :].rearrange("(p j) n -> p j n", j=PACK)
-                nc.sync.dma_start(out=w_raw[PASSES * q + c][:], in_=rows[:, :, q * W_COLS : (q + 1) * W_COLS])
+        for quarters in (range(LAST), range(LAST, QUARTERS)):
+            for c in range(PASSES):
+                for q in quarters:
+                    rows = w[c * K_PASS : (c + 1) * K_PASS, :].rearrange("(p j) n -> p j n", j=PACK)
+                    nc.sync.dma_start(out=w_raw[PASSES * q + c][:], in_=rows[:, :, q * W_COLS : (q + 1) * W_COLS])
 
         make_identity(nc, eye[:])
         nc.vector.memset(eye_bf[:].bitcast(U32), 0)
@@ -149,71 +165,68 @@ def tile_mix_tierg_none_kernel(tc, g, w, out):
         nc.vector.tensor_copy(out=diagonal, in_=eye[:].unsqueeze(1).to_broadcast([P, PACK, P]))
         nc.vector.quantize_mx(out=eye_codes[:].bitcast(E4M3), scales=eye_scales[:], in_=eye_bf[:, 0 : PACK * K_PASS])
 
-        def close(q):
-            for x in range(2):
-                product("q", 1, q, (x,))
-                product("r", 1, q, (x,))
-
-        cast_g("v", 0, 0, 0, HALF)
+        cast_g(vector_copy, 0, 0, 0, HALF)
         quant_g(0, 0, HALF)
-        cast_g("s", 0, 1, 128, HALF)
-        cast_g("v", 0, 1, 0, 128)
+        cast_g(scalar_copy, 0, 1, G_SPLIT, HALF)
+        cast_g(vector_copy, 0, 1, 0, G_SPLIT)
         quant_g(0, HALF, T)
         dequant(0)
-        cast_g("v", 1, 0, 0, HALF)
-        cast_g("s", 1, 1, 0, HALF)
-        subtract(0, 0)
-        subtract(0, 1)
-        subtract(0, 2)
+        cast_g(vector_copy, 1, 0, 0, HALF)
+        cast_g(scalar_copy, 1, 1, 0, HALF)
+        for j in range(PACK):
+            subtract(0, j)
         quant_g(1, 0, T)
         dequant(1)
-        subtract(0, 3)
-        cast_w("s", 0, 0)
+
+        cast_w(scalar_copy, 0, 0)
+        pack_r(vector_copy, 0, 0, R0_SPLIT)
+        pack_r(scalar_copy, 0, R0_SPLIT, T)
         quant_w(0, 0)
-        product("q", 0, 0)
-        cast_w("s", 0, 1)
-        pack_r("v", 0, 0, 256)
-        pack_r("s", 0, 256, T)
+        product(first_tier, 0, 0)
+        cast_w(scalar_copy, 0, 1)
         subtract(1, 0)
-        quant_w(0, 1)
-        product("q", 0, 1)
-        subtract(1, 1)
         quant_r(0)
-        product("r", 0, 0)
-        product("r", 0, 1)
-        cast_w("s", 0, 2)
+        product(second_tier, 0, 0)
+        subtract(1, 1)
+        quant_w(0, 1)
+        product(first_tier, 0, 1)
+        product(second_tier, 0, 1)
+        cast_w(scalar_copy, 0, 2)
         subtract(1, 2)
-        quant_w(0, 2)
-        product("q", 0, 2)
-        product("r", 0, 2)
-        cast_w("s", 0, 3)
         subtract(1, 3)
-        cast_w("s", 1, 0)
-        quant_w(0, 3)
-        product("q", 0, 3)
-        product("r", 0, 3)
-        pack_r("s", 1, 384, T)
-        pack_r("v", 1, 0, 384)
+        quant_w(0, 2)
+        product(first_tier, 0, 2)
+        product(second_tier, 0, 2)
+
+        cast_w(scalar_copy, 1, 0)
+        pack_r(scalar_copy, 1, R1_SPLIT, T)
+        pack_r(vector_copy, 1, 0, R1_SPLIT)
         quant_w(1, 0)
-        product("q", 1, 0)
+        product(first_tier, 1, 0)
+        cast_w(scalar_copy, 1, 1)
         quant_r(1)
-        cast_w("s", 1, 1)
-        product("r", 1, 0)
-        cast_w("v", 1, 2, 0, P)
+        product(second_tier, 1, 0)
+
+        cast_w(vector_copy, 1, 2, 0, P)
+        finish(scalar_copy, 0)
+        finish(scalar_copy, 1)
         quant_w(1, 1)
         close(1)
-        finish("s", 0)
-        finish("s", 1)
-        cast_w("v", 1, 2, P, W_COLS)
-        cast_w("v", 1, 3, 0, P)
+        cast_w(vector_copy, 1, 2, P, W_COLS)
+        cast_w(vector_copy, 0, LAST, 0, P)
         quant_w(1, 2)
         close(2)
-        finish("s", 2)
-        cast_w("v", 1, 3, P, W_COLS)
-        quant_w(1, 3)
-        close(3)
-        finish("s", 3)
-        finish("s", 4)
-        finish("v", 5)
-        finish("s", 6)
-        finish("v", 7)
+        finish(scalar_copy, 2)
+        finish(scalar_copy, 3)
+        cast_w(vector_copy, 0, LAST, P, W_COLS)
+        cast_w(vector_copy, 1, LAST, 0, P)
+        quant_w(0, LAST)
+        product(first_tier, 0, LAST)
+        product(second_tier, 0, LAST)
+        cast_w(vector_copy, 1, LAST, P, W_COLS)
+        finish(scalar_copy, 4)
+        quant_w(1, LAST)
+        close(LAST)
+        finish(scalar_copy, 5)
+        finish(vector_copy, 6)
+        finish(scalar_copy, 7)

@@ -1,7 +1,6 @@
 from contextlib import ExitStack
 
 import concourse.mybir as mybir
-from concourse.masks import make_identity
 
 K, N, T = 1024, 1024, 512
 FLOPS = 2 * 2 * K * N * T
@@ -42,8 +41,10 @@ def tile_mix_tierg_none_kernel(tc, g, w, out):
 
         g_raw = tiles("g_raw", PASSES, [P, 2 * PACK * HALF], F32)
         g_bf = tiles("g_bf", PASSES, [P, T, PACK], BF16)
-        gq_codes = tiles("gq_codes", PASSES, [P, T], U32)
-        gq_scales = tiles("gq_scales", PASSES, [P, T], U8)
+        gq_codes_wide = tiles("gq_codes", PASSES, [P, HALF + T], U32)
+        gq_codes = [t[:, HALF:] for t in gq_codes_wide]
+        gq_scales_wide = tiles("gq_scales", PASSES, [P, HALF + T], U8)
+        gq_scales = [t[:, HALF:] for t in gq_scales_wide]
         r_rows = tiles("r_rows", PASSES, [P, PACK, T], BF16)
         r_bf = tiles("r_bf", PASSES, [P, T, PACK], BF16)
         gr_codes = tiles("gr_codes", PASSES, [P, T], U32)
@@ -54,8 +55,8 @@ def tile_mix_tierg_none_kernel(tc, g, w, out):
         w_codes = tiles("w_codes", pieces, [P, W_COLS], U32)
         w_scales = tiles("w_scales", pieces, [P, W_COLS], U8)
         result = tiles("result", N // P, [P, T], F32)
-        eye = sb.tile([P, P], BF16, align_bytes=64)
-        eye_bf = sb.tile([P, PACK * (K_PASS + 1)], BF16, align_bytes=64)
+        ramp = sb.tile([P, K_PASS + PACK], BF16, name="ramp", align_bytes=64)
+        eye_bf = sb.tile([P, PACK * K_PASS], BF16, name="eye_bf", align_bytes=64)
         eye_codes = sb.tile([P, K_PASS], U32, align_bytes=64)
         eye_scales = sb.tile([P, K_PASS], U8, align_bytes=64)
 
@@ -79,16 +80,16 @@ def tile_mix_tierg_none_kernel(tc, g, w, out):
 
         gq_values = {}
 
-        def dequant(c):
+        def dequant(c, first_bank, early=False):
             for j in range(PACK):
-                gq_values[c, j] = bank(PACK * c + j, "gq_values")
+                gq_values[c, j] = bank(first_bank + j, "gq_values")
                 cols = slice(j * P, (j + 1) * P)
                 nc.tensor.matmul_mx(
                     out=gq_values[c, j][:],
                     lhsT=eye_codes[:, cols].bitcast(E4M3),
                     lhsT_scale=eye_scales[:, cols],
-                    rhs=gq_codes[c][:].bitcast(E5M2),
-                    rhs_scale=gq_scales[c][:],
+                    rhs=(gq_codes_wide[c][:, 0:T] if early else gq_codes[c]).bitcast(E5M2),
+                    rhs_scale=gq_scales_wide[c][:, 0:T] if early else gq_scales[c],
                     start=True,
                     stop=True,
                 )
@@ -100,6 +101,22 @@ def tile_mix_tierg_none_kernel(tc, g, w, out):
                 in1=gq_values[c, j][:].rearrange("p (h t) -> p h t", h=2),
                 op=mybir.AluOpType.subtract,
             )
+
+        def subtract_half(c, j, h):
+            nc.vector.tensor_tensor(
+                out=r_rows[c][:, j, h * HALF : (h + 1) * HALF],
+                in0=g_half(c, h)[:, j, :],
+                in1=gq_values[c, j][:, HALF:],
+                op=mybir.AluOpType.subtract,
+            )
+
+        def gpsimd_copy(out, in_):
+            nc.gpsimd.tensor_scalar(out=out, in0=in_, scalar1=1.0, scalar2=0.0, op0=mybir.AluOpType.mult, op1=mybir.AluOpType.add)
+
+        def warm_up(count):
+            scratch = bank(2 * PACK - 1, "scratch")
+            for i in range(count):
+                nc.tensor.matmul_mx(out=scratch[:], lhsT=eye_codes[:, 0:P].bitcast(E4M3), lhsT_scale=eye_scales[:, 0:P], rhs=eye_codes[:].bitcast(E4M3), rhs_scale=eye_scales[:], start=True, stop=True)
 
         def pack_r(copy, c, lo, hi):
             pack(copy, r_bf[c][:, lo:hi, :], r_rows[c][:, :, lo:hi])
@@ -126,7 +143,7 @@ def tile_mix_tierg_none_kernel(tc, g, w, out):
             for side in sides:
                 n = 2 * q + side
                 if n not in acc:
-                    acc[n] = bank(n, "acc")
+                    acc[n] = bank((n + PACK) % (2 * PACK), "acc")
                     issued[n] = 0
                 cols = slice(side * P, (side + 1) * P)
                 nc.tensor.matmul_mx(
@@ -149,84 +166,107 @@ def tile_mix_tierg_none_kernel(tc, g, w, out):
             copy(out=result[n][:], in_=acc[n][:])
             nc.sync.dma_start(out=out[n * P : (n + 1) * P, :], in_=result[n][:])
 
-        for c in range(PASSES):
+        def load_g(c, h):
             rows = g[c * K_PASS : (c + 1) * K_PASS, :].rearrange("(p j) t -> p j t", j=PACK)
-            for h in range(2):
-                nc.sync.dma_start(out=g_half(c, h), in_=rows[:, :, h * HALF : (h + 1) * HALF])
-        for quarters in (range(LAST), range(LAST, QUARTERS)):
-            for c in range(PASSES):
-                for q in quarters:
-                    rows = w[c * K_PASS : (c + 1) * K_PASS, :].rearrange("(p j) n -> p j n", j=PACK)
-                    nc.sync.dma_start(out=w_raw[PASSES * q + c][:], in_=rows[:, :, q * W_COLS : (q + 1) * W_COLS])
+            nc.sync.dma_start(out=g_half(c, h), in_=rows[:, :, h * HALF : (h + 1) * HALF])
 
-        make_identity(nc, eye[:])
-        nc.vector.memset(eye_bf[:].bitcast(U32), 0)
-        diagonal = eye_bf[:].rearrange("p (j r) -> p j r", j=PACK)[:, :, 0:K_PASS:PACK]
-        nc.vector.tensor_copy(out=diagonal, in_=eye[:].unsqueeze(1).to_broadcast([P, PACK, P]))
-        nc.vector.quantize_mx(out=eye_codes[:].bitcast(E4M3), scales=eye_scales[:], in_=eye_bf[:, 0 : PACK * K_PASS])
+        def load_w(c, q):
+            rows = w[c * K_PASS : (c + 1) * K_PASS, :].rearrange("(p j) n -> p j n", j=PACK)
+            nc.sync.dma_start(out=w_raw[PASSES * q + c][:], in_=rows[:, :, q * W_COLS : (q + 1) * W_COLS])
 
-        cast_g(vector_copy, 0, 0, 0, HALF)
-        quant_g(0, 0, HALF)
-        cast_g(scalar_copy, 0, 1, G_SPLIT, HALF)
-        cast_g(vector_copy, 0, 1, 0, G_SPLIT)
-        quant_g(0, HALF, T)
-        dequant(0)
-        cast_g(vector_copy, 1, 0, 0, HALF)
-        cast_g(scalar_copy, 1, 1, 0, HALF)
+        load_g(0,0)
+        load_g(0,1)
+        load_g(1,0)
+        load_g(1,1)
+        load_w(0,0)
+        load_w(0,1)
+        load_w(0,2)
+        load_w(0,3)
+        load_w(1,0)
+        load_w(1,1)
+        load_w(1,2)
+        load_w(1,3)
+
+        nc.gpsimd.iota(ramp[:], [[1, K_PASS + PACK]], base=-(PACK - 1), channel_multiplier=-PACK, allow_small_or_imprecise_dtypes=True)
+        nc.vector.memset(gq_codes_wide[0][:, 0:HALF], 0)
+        nc.vector.memset(gq_scales_wide[0][:, 0:HALF].bitcast(U32), 0)
         for j in range(PACK):
-            subtract(0, j)
-        quant_g(1, 0, T)
-        dequant(1)
+            shift = PACK - 1 - j
+            nc.vector.tensor_scalar(out=eye_bf[:, j * K_PASS : (j + 1) * K_PASS], in0=ramp[:, shift : shift + K_PASS], scalar1=0.0, scalar2=None, op0=mybir.AluOpType.is_equal)
+        for lo in (0, HALF):
+            nc.vector.quantize_mx(out=eye_codes[:, lo : lo + HALF].bitcast(E4M3), scales=eye_scales[:, lo : lo + HALF], in_=eye_bf[:, PACK * lo : PACK * (lo + HALF)])
+        warm_up(3)
+        cast_g(scalar_copy, 0, 0, 160, HALF)
+        cast_g(vector_copy, 0, 0, 0, 160)
+        quant_g(0, 0, HALF)
+        dequant(0, 0, True)
+        cast_g(scalar_copy, 0, 1, 160, HALF)
+        cast_g(vector_copy, 0, 1, 0, 160)
+        subtract_half(0, 0, 0)
+        quant_g(0, HALF, T)
+        subtract_half(0, 1, 0)
+        subtract_half(0, 2, 0)
+        subtract_half(0, 3, 0)
+        dequant(0, 4)
+        cast_g(scalar_copy, 1, 0, 0, HALF)
 
+        cast_g(scalar_copy, 1, 1, 128, HALF)
+        subtract_half(0, 0, 1)
+        cast_g(vector_copy, 1, 1, 0, 128)
+        subtract_half(0, 1, 1)
+        pack_r(scalar_copy, 0, 0, P)
+        subtract_half(0, 2, 1)
+        quant_g(1, 0, T)
+        dequant(1, 0)
+        subtract_half(0, 3, 1)
         cast_w(scalar_copy, 0, 0)
-        pack_r(vector_copy, 0, 0, R0_SPLIT)
-        pack_r(scalar_copy, 0, R0_SPLIT, T)
+        pack_r(vector_copy, 0, P, HALF)
+
+        pack_r(vector_copy, 0, HALF, 512)
         quant_w(0, 0)
         product(first_tier, 0, 0)
-        cast_w(scalar_copy, 0, 1)
-        subtract(1, 0)
         quant_r(0)
         product(second_tier, 0, 0)
-        subtract(1, 1)
+        subtract(1, 0)
+        cast_w(scalar_copy, 0, 1)
         quant_w(0, 1)
         product(first_tier, 0, 1)
         product(second_tier, 0, 1)
-        cast_w(scalar_copy, 0, 2)
+        subtract(1, 1)
         subtract(1, 2)
-        subtract(1, 3)
+        cast_w(scalar_copy, 0, 2)
         quant_w(0, 2)
+        subtract(1, 3)
         product(first_tier, 0, 2)
         product(second_tier, 0, 2)
 
+        cast_w(scalar_copy, 0, 3)
+        quant_w(0, 3)
+        product(first_tier, 0, 3)
+        product(second_tier, 0, 3)
         cast_w(scalar_copy, 1, 0)
-        pack_r(scalar_copy, 1, R1_SPLIT, T)
-        pack_r(vector_copy, 1, 0, R1_SPLIT)
+        pack_r(scalar_copy, 1, 448, T)
+        pack_r(vector_copy, 1, 0, 448)
         quant_w(1, 0)
         product(first_tier, 1, 0)
         cast_w(scalar_copy, 1, 1)
         quant_r(1)
         product(second_tier, 1, 0)
-
         cast_w(vector_copy, 1, 2, 0, P)
-        finish(scalar_copy, 0)
-        finish(scalar_copy, 1)
         quant_w(1, 1)
         close(1)
+        finish(scalar_copy, 0)
+        finish(scalar_copy, 1)
         cast_w(vector_copy, 1, 2, P, W_COLS)
-        cast_w(vector_copy, 0, LAST, 0, P)
+        cast_w(vector_copy, 1, 3, 0, P)
         quant_w(1, 2)
         close(2)
         finish(scalar_copy, 2)
         finish(scalar_copy, 3)
-        cast_w(vector_copy, 0, LAST, P, W_COLS)
-        cast_w(vector_copy, 1, LAST, 0, P)
-        quant_w(0, LAST)
-        product(first_tier, 0, LAST)
-        product(second_tier, 0, LAST)
-        cast_w(vector_copy, 1, LAST, P, W_COLS)
-        finish(scalar_copy, 4)
-        quant_w(1, LAST)
-        close(LAST)
+        cast_w(vector_copy, 1, 3, P, W_COLS)
+        quant_w(1, 3)
+        close(3)
+        finish(vector_copy, 4)
         finish(scalar_copy, 5)
         finish(vector_copy, 6)
         finish(scalar_copy, 7)

@@ -8,6 +8,7 @@ FLOPS = 2 * 2 * K * N * T
 F32 = mybir.dt.float32
 BF16 = mybir.dt.bfloat16
 U32 = mybir.dt.uint32
+I32 = mybir.dt.int32
 U8 = mybir.dt.uint8
 E4M3 = mybir.dt.float8_e4m3fn_x4
 E5M2 = mybir.dt.float8_e5m2_x4
@@ -46,6 +47,7 @@ def tile_mix_tierg_none_kernel(tc, g, w, out):
         gq_scales_wide = tiles("gq_scales", PASSES, [P, HALF + T], U8)
         gq_scales = [t[:, HALF:] for t in gq_scales_wide]
         r_rows = tiles("r_rows", PASSES, [P, PACK, T], BF16)
+        r_pairs = tiles("r_pairs", PASSES, [P, 2, HALF, 2], BF16)
         r_bf = tiles("r_bf", PASSES, [P, T, PACK], BF16)
         gr_codes = tiles("gr_codes", PASSES, [P, T], U32)
         gr_scales = tiles("gr_scales", PASSES, [P, T], U8)
@@ -54,7 +56,7 @@ def tile_mix_tierg_none_kernel(tc, g, w, out):
         w_bf = tiles("w_bf", pieces, [P, W_COLS, PACK], BF16)
         w_codes = tiles("w_codes", pieces, [P, W_COLS], U32)
         w_scales = tiles("w_scales", pieces, [P, W_COLS], U8)
-        result = tiles("result", N // P, [P, T], F32)
+        result = tiles("result", QUARTERS, [P, 2, T], F32)
         ramp = sb.tile([P, K_PASS + PACK], BF16, name="ramp", align_bytes=64)
         eye_bf = sb.tile([P, PACK * K_PASS], BF16, name="eye_bf", align_bytes=64)
         eye_codes = sb.tile([P, K_PASS], U32, align_bytes=64)
@@ -80,9 +82,9 @@ def tile_mix_tierg_none_kernel(tc, g, w, out):
 
         gq_values = {}
 
-        def dequant(c, first_bank, early=False):
+        def dequant(c, banks, early=False):
             for j in range(PACK):
-                gq_values[c, j] = bank(first_bank + j, "gq_values")
+                gq_values[c, j] = bank(banks[j], "gq_values")
                 cols = slice(j * P, (j + 1) * P)
                 nc.tensor.matmul_mx(
                     out=gq_values[c, j][:],
@@ -110,6 +112,43 @@ def tile_mix_tierg_none_kernel(tc, g, w, out):
                 op=mybir.AluOpType.subtract,
             )
 
+        def clear_pads(c):
+            nc.vector.memset(gq_codes_wide[c][:].rearrange("p (s t) -> p s t", s=3)[:, 0:3:2, :], 0)
+            nc.vector.memset(gq_scales_wide[c][:].bitcast(U32).rearrange("p (s t) -> p s t", s=3)[:, 0:3:2, :], 0)
+
+        pair_values = {}
+
+        def dequant_pairs(c, banks):
+            for u in range(2):
+                pair_values[c, u] = bank(banks[u], "pair_values")
+            for e in range(2):
+                window = slice(HALF * (1 - e), HALF * (1 - e) + T)
+                for u in range(2):
+                    cols = slice((2 * u + e) * P, (2 * u + e + 1) * P)
+                    nc.tensor.matmul_mx(
+                        out=pair_values[c, u][:],
+                        lhsT=eye_codes[:, cols].bitcast(E4M3),
+                        lhsT_scale=eye_scales[:, cols],
+                        rhs=gq_codes_wide[c][:, window].bitcast(E5M2),
+                        rhs_scale=gq_scales_wide[c][:, window],
+                        start=e == 0,
+                        stop=e == 1,
+                    )
+
+        def subtract_pair(c, u):
+            nc.vector.tensor_tensor(
+                out=r_pairs[c][:, u, :, :].rearrange("p (c i) e -> p c e i", i=RUN),
+                in0=g_half(c, 0)[:, 2 * u : 2 * u + 2, :].rearrange("p e (c i) -> p c e i", i=RUN),
+                in1=pair_values[c, u][:].rearrange("p (e c i) -> p c e i", e=2, i=RUN),
+                op=mybir.AluOpType.subtract,
+            )
+
+        def pack_pairs(copy, c, words):
+            copy(
+                out=r_bf[c][:, 0:HALF, :].rearrange("p t j -> p (t j)").bitcast(words).rearrange("p (t u) -> p t u", u=2),
+                in_=r_pairs[c][:].rearrange("p u t e -> p (u t e)").bitcast(words).rearrange("p (u t) -> p t u", u=2),
+            )
+
         def gpsimd_copy(out, in_):
             nc.gpsimd.tensor_scalar(out=out, in0=in_, scalar1=1.0, scalar2=0.0, op0=mybir.AluOpType.mult, op1=mybir.AluOpType.add)
 
@@ -121,8 +160,8 @@ def tile_mix_tierg_none_kernel(tc, g, w, out):
         def pack_r(copy, c, lo, hi):
             pack(copy, r_bf[c][:, lo:hi, :], r_rows[c][:, :, lo:hi])
 
-        def quant_r(c):
-            quantize(gr_codes[c][:], gr_scales[c][:], r_bf[c][:], E4M3)
+        def quant_r(c, lo=0, hi=T):
+            quantize(gr_codes[c][:, lo:hi], gr_scales[c][:, lo:hi], r_bf[c][:, lo:hi, :], E4M3)
 
         def cast_w(copy, c, q, lo=0, hi=W_COLS):
             i = PASSES * q + c
@@ -137,34 +176,44 @@ def tile_mix_tierg_none_kernel(tc, g, w, out):
         acc = {}
         issued = {}
 
-        def product(tier, c, q, sides=(0, 1)):
+        def product(tier, c, q, sides=(0, 1), lo=0, hi=T):
             i = PASSES * q + c
             codes, scales, fmt = tier
             for side in sides:
                 n = 2 * q + side
                 if n not in acc:
-                    acc[n] = bank((n + PACK) % (2 * PACK), "acc")
+                    acc[n] = bank((6,7,0,1,2,3,4,5)[n], "acc")
                     issued[n] = 0
                 cols = slice(side * P, (side + 1) * P)
                 nc.tensor.matmul_mx(
-                    out=acc[n][:],
+                    out=acc[n][:, lo:hi],
                     lhsT=w_codes[i][:, cols].bitcast(E4M3),
                     lhsT_scale=w_scales[i][:, cols],
-                    rhs=codes[c][:].bitcast(fmt),
-                    rhs_scale=scales[c][:],
+                    rhs=codes[c][:, lo:hi].bitcast(fmt),
+                    rhs_scale=scales[c][:, lo:hi],
                     start=issued[n] == 0,
-                    stop=issued[n] == 2 * PASSES - 1,
+                    stop=issued[n] + hi - lo == 2 * PASSES * T,
                 )
-                issued[n] = issued[n] + 1
+                issued[n] = issued[n] + hi - lo
 
-        def close(q):
-            for side in range(2):
-                product(first_tier, 1, q, (side,))
-                product(second_tier, 1, q, (side,))
+        def both_tiers(c, q, sides=(0, 1)):
+            for side in sides:
+                product(first_tier, c, q, (side,))
+                product(second_tier, c, q, (side,))
 
-        def finish(copy, n):
-            copy(out=result[n][:], in_=acc[n][:])
-            nc.sync.dma_start(out=out[n * P : (n + 1) * P, :], in_=result[n][:])
+        def drain(copy, n, lo=0, hi=T):
+            copy(out=result[n // 2][:, n % 2, lo:hi], in_=acc[n][:, lo:hi])
+
+        def store(n, lo=0, hi=T):
+            nc.sync.dma_start(out=out[n * P : (n + 1) * P, lo:hi], in_=result[n // 2][:, n % 2, lo:hi])
+
+        def store_quarter(q):
+            rows = out[q * W_COLS : (q + 1) * W_COLS, :].rearrange("(side p) t -> p side t", side=2)
+            nc.sync.dma_start(out=rows, in_=result[q][:])
+
+        def finish(copy, n, lo=0, hi=T):
+            drain(copy, n, lo, hi)
+            store(n, lo, hi)
 
         def load_g(c, h):
             rows = g[c * K_PASS : (c + 1) * K_PASS, :].rearrange("(p j) t -> p j t", j=PACK)
@@ -181,25 +230,25 @@ def tile_mix_tierg_none_kernel(tc, g, w, out):
         load_w(0,0)
         load_w(0,1)
         load_w(0,2)
-        load_w(0,3)
         load_w(1,0)
         load_w(1,1)
+        load_w(0,3)
         load_w(1,2)
         load_w(1,3)
 
-        nc.gpsimd.iota(ramp[:], [[1, K_PASS + PACK]], base=-(PACK - 1), channel_multiplier=-PACK, allow_small_or_imprecise_dtypes=True)
-        nc.vector.memset(gq_codes_wide[0][:, 0:HALF], 0)
-        nc.vector.memset(gq_scales_wide[0][:, 0:HALF].bitcast(U32), 0)
+        nc.gpsimd.iota(ramp[:].bitcast(F32), [[1, (K_PASS + PACK) // 2]], base=0, channel_multiplier=-2, allow_small_or_imprecise_dtypes=True)
+        clear_pads(0)
         for j in range(PACK):
             shift = PACK - 1 - j
-            nc.vector.tensor_scalar(out=eye_bf[:, j * K_PASS : (j + 1) * K_PASS], in0=ramp[:, shift : shift + K_PASS], scalar1=0.0, scalar2=None, op0=mybir.AluOpType.is_equal)
+            nc.vector.tensor_scalar(out=eye_bf[:, j * K_PASS : (j + 1) * K_PASS], in0=ramp[:, shift : shift + K_PASS], scalar1=1.0, scalar2=None, op0=mybir.AluOpType.is_equal)
         for lo in (0, HALF):
             nc.vector.quantize_mx(out=eye_codes[:, lo : lo + HALF].bitcast(E4M3), scales=eye_scales[:, lo : lo + HALF], in_=eye_bf[:, PACK * lo : PACK * (lo + HALF)])
         warm_up(3)
         cast_g(scalar_copy, 0, 0, 160, HALF)
         cast_g(vector_copy, 0, 0, 0, 160)
+        clear_pads(1)
         quant_g(0, 0, HALF)
-        dequant(0, 0, True)
+        dequant(0, (0, 1, 2, 3), True)
         cast_g(scalar_copy, 0, 1, 160, HALF)
         cast_g(vector_copy, 0, 1, 0, 160)
         subtract_half(0, 0, 0)
@@ -207,66 +256,69 @@ def tile_mix_tierg_none_kernel(tc, g, w, out):
         subtract_half(0, 1, 0)
         subtract_half(0, 2, 0)
         subtract_half(0, 3, 0)
-        dequant(0, 4)
+        dequant(0, (4, 5, 6, 7))
         cast_g(scalar_copy, 1, 0, 0, HALF)
-
-        cast_g(scalar_copy, 1, 1, 128, HALF)
+        cast_g(scalar_copy, 1, 1, 0, HALF)
         subtract_half(0, 0, 1)
-        cast_g(vector_copy, 1, 1, 0, 128)
         subtract_half(0, 1, 1)
-        pack_r(scalar_copy, 0, 0, P)
+        quant_g(1, 0, HALF)
+        dequant_pairs(1, (0, 1))
         subtract_half(0, 2, 1)
-        quant_g(1, 0, T)
-        dequant(1, 0)
         subtract_half(0, 3, 1)
+        pack_r(vector_copy, 0, 0, HALF)
+        quant_g(1, HALF, T)
+        dequant(1, (2, 3, 4, 5))
+        pack_r(vector_copy, 0, HALF, T)
         cast_w(scalar_copy, 0, 0)
-        pack_r(vector_copy, 0, P, HALF)
-
-        pack_r(vector_copy, 0, HALF, 512)
         quant_w(0, 0)
         product(first_tier, 0, 0)
         quant_r(0)
         product(second_tier, 0, 0)
-        subtract(1, 0)
+        subtract_pair(1, 0)
         cast_w(scalar_copy, 0, 1)
         quant_w(0, 1)
-        product(first_tier, 0, 1)
-        product(second_tier, 0, 1)
-        subtract(1, 1)
-        subtract(1, 2)
+        subtract_pair(1, 1)
+        both_tiers(0, 1)
         cast_w(scalar_copy, 0, 2)
+        subtract_half(1, 0, 1)
         quant_w(0, 2)
-        subtract(1, 3)
-        product(first_tier, 0, 2)
-        product(second_tier, 0, 2)
-
-        cast_w(scalar_copy, 0, 3)
-        quant_w(0, 3)
-        product(first_tier, 0, 3)
-        product(second_tier, 0, 3)
+        subtract_half(1, 1, 1)
+        both_tiers(0, 2)
+        subtract_half(1, 2, 1)
+        subtract_half(1, 3, 1)
         cast_w(scalar_copy, 1, 0)
-        pack_r(scalar_copy, 1, 448, T)
-        pack_r(vector_copy, 1, 0, 448)
+        pack_pairs(scalar_copy, 1, U32)
         quant_w(1, 0)
         product(first_tier, 1, 0)
+        pack_r(vector_copy, 1, HALF, T)
+        quant_r(1, 0, HALF)
+        product(second_tier, 1, 0, (0,), 0, HALF)
+        quant_r(1, HALF, T)
+        product(second_tier, 1, 0, (0,), HALF, T)
+        product(second_tier, 1, 0, (1,))
         cast_w(scalar_copy, 1, 1)
-        quant_r(1)
-        product(second_tier, 1, 0)
-        cast_w(vector_copy, 1, 2, 0, P)
         quant_w(1, 1)
-        close(1)
-        finish(scalar_copy, 0)
+        both_tiers(1, 1)
+        cast_w(scalar_copy, 0, 3, 128, W_COLS)
+        finish(scalar_copy, 0, 0, HALF)
+        finish(scalar_copy, 0, HALF, T)
         finish(scalar_copy, 1)
-        cast_w(vector_copy, 1, 2, P, W_COLS)
-        cast_w(vector_copy, 1, 3, 0, P)
+        cast_w(vector_copy, 1, 2)
+        cast_w(vector_copy, 0, 3, 0, 128)
         quant_w(1, 2)
-        close(2)
+        both_tiers(1, 2)
         finish(scalar_copy, 2)
         finish(scalar_copy, 3)
+        cast_w(vector_copy, 1, 3, 0, P)
+        quant_w(0, 3)
+        both_tiers(0, 3, (0,))
         cast_w(vector_copy, 1, 3, P, W_COLS)
         quant_w(1, 3)
-        close(3)
-        finish(vector_copy, 4)
+        both_tiers(1, 3, (0,))
+        both_tiers(0, 3, (1,))
+        both_tiers(1, 3, (1,))
+        finish(scalar_copy, 4)
         finish(scalar_copy, 5)
         finish(vector_copy, 6)
-        finish(scalar_copy, 7)
+        finish(scalar_copy, 7, 0, HALF)
+        finish(scalar_copy, 7, HALF, T)

@@ -137,9 +137,9 @@ def tile_mix_tierg_none_kernel(tc, g, w, out):
 
         def subtract_pair(c, u):
             nc.vector.tensor_tensor(
-                out=r_pairs[c][:, u, :, :].rearrange("p (c i) e -> p c e i", i=RUN),
-                in0=g_half(c, 0)[:, 2 * u : 2 * u + 2, :].rearrange("p e (c i) -> p c e i", i=RUN),
-                in1=pair_values[c, u][:].rearrange("p (e c i) -> p c e i", e=2, i=RUN),
+                out=r_pairs[c][:, u, :, :],
+                in0=g_half(c, 0)[:, 2 * u : 2 * u + 2, :].rearrange("p e t -> p t e"),
+                in1=pair_values[c, u][:].rearrange("p (e t) -> p t e", e=2),
                 op=mybir.AluOpType.subtract,
             )
 
@@ -167,9 +167,9 @@ def tile_mix_tierg_none_kernel(tc, g, w, out):
             i = PASSES * q + c
             pack(copy, w_bf[i][:, lo:hi, :], w_raw[i][:, :, lo:hi])
 
-        def quant_w(c, q):
+        def quant_w(c, q, lo=0, hi=W_COLS):
             i = PASSES * q + c
-            quantize(w_codes[i][:], w_scales[i][:], w_bf[i][:], E4M3)
+            quantize(w_codes[i][:, lo:hi], w_scales[i][:, lo:hi], w_bf[i][:, lo:hi, :], E4M3)
 
         first_tier = (gq_codes, gq_scales, E5M2)
         second_tier = (gr_codes, gr_scales, E4M3)
@@ -232,10 +232,9 @@ def tile_mix_tierg_none_kernel(tc, g, w, out):
         load_w(0,2)
         load_w(1,0)
         load_w(1,1)
-        load_w(0,3)
         load_w(1,2)
+        load_w(0,3)
         load_w(1,3)
-
         nc.gpsimd.iota(ramp[:].bitcast(F32), [[1, (K_PASS + PACK) // 2]], base=0, channel_multiplier=-2, allow_small_or_imprecise_dtypes=True)
         clear_pads(0)
         for j in range(PACK):
@@ -299,23 +298,25 @@ def tile_mix_tierg_none_kernel(tc, g, w, out):
         cast_w(scalar_copy, 1, 1)
         quant_w(1, 1)
         both_tiers(1, 1)
-        cast_w(scalar_copy, 0, 3, 128, W_COLS)
+        cast_w(scalar_copy, 1, 2, P, W_COLS)
+        cast_w(vector_copy, 1, 2, 0, P)
         finish(scalar_copy, 0, 0, HALF)
         finish(scalar_copy, 0, HALF, T)
         finish(scalar_copy, 1)
-        cast_w(vector_copy, 1, 2)
-        cast_w(vector_copy, 0, 3, 0, 128)
+        cast_w(vector_copy, 0, 3, 0, P)
         quant_w(1, 2)
         both_tiers(1, 2)
+        cast_w(vector_copy, 0, 3, P, W_COLS)
         finish(scalar_copy, 2)
         finish(scalar_copy, 3)
         cast_w(vector_copy, 1, 3, 0, P)
         quant_w(0, 3)
         both_tiers(0, 3, (0,))
+        quant_w(1, 3, 0, P)
         cast_w(vector_copy, 1, 3, P, W_COLS)
-        quant_w(1, 3)
         both_tiers(1, 3, (0,))
         both_tiers(0, 3, (1,))
+        quant_w(1, 3, P, W_COLS)
         both_tiers(1, 3, (1,))
         finish(scalar_copy, 4)
         finish(scalar_copy, 5)

@@ -8,7 +8,6 @@ FLOPS = 2 * 2 * K * N * T
 F32 = mybir.dt.float32
 BF16 = mybir.dt.bfloat16
 U32 = mybir.dt.uint32
-I32 = mybir.dt.int32
 U8 = mybir.dt.uint8
 E4M3 = mybir.dt.float8_e4m3fn_x4
 E5M2 = mybir.dt.float8_e5m2_x4
@@ -21,11 +20,10 @@ HALF = T // 2
 W_COLS = 256
 QUARTERS = N // W_COLS
 LAST = QUARTERS - 1
+BANKS = 8
 RUN = 4
-
-G_SPLIT = 128
-R0_SPLIT = 256
-R1_SPLIT = 384
+G_SPLIT = 160
+WARM_UPS = 3
 
 
 def tile_mix_tierg_none_kernel(tc, g, w, out):
@@ -42,12 +40,12 @@ def tile_mix_tierg_none_kernel(tc, g, w, out):
 
         g_raw = tiles("g_raw", PASSES, [P, 2 * PACK * HALF], F32)
         g_bf = tiles("g_bf", PASSES, [P, T, PACK], BF16)
-        gq_codes_wide = tiles("gq_codes", PASSES, [P, HALF + T], U32)
-        gq_codes = [t[:, HALF:] for t in gq_codes_wide]
-        gq_scales_wide = tiles("gq_scales", PASSES, [P, HALF + T], U8)
-        gq_scales = [t[:, HALF:] for t in gq_scales_wide]
+        padded_codes = tiles("gq_codes", PASSES, [P, HALF + T], U32)
+        padded_scales = tiles("gq_scales", PASSES, [P, HALF + T], U8)
+        gq_codes = [tile[:, HALF:] for tile in padded_codes]
+        gq_scales = [tile[:, HALF:] for tile in padded_scales]
         r_rows = tiles("r_rows", PASSES, [P, PACK, T], BF16)
-        r_pairs = tiles("r_pairs", PASSES, [P, 2, HALF, 2], BF16)
+        r_pairs = sb.tile([P, 2, HALF, 2], BF16, name="r_pairs", align_bytes=64)
         r_bf = tiles("r_bf", PASSES, [P, T, PACK], BF16)
         gr_codes = tiles("gr_codes", PASSES, [P, T], U32)
         gr_scales = tiles("gr_scales", PASSES, [P, T], U8)
@@ -56,11 +54,11 @@ def tile_mix_tierg_none_kernel(tc, g, w, out):
         w_bf = tiles("w_bf", pieces, [P, W_COLS, PACK], BF16)
         w_codes = tiles("w_codes", pieces, [P, W_COLS], U32)
         w_scales = tiles("w_scales", pieces, [P, W_COLS], U8)
-        result = tiles("result", QUARTERS, [P, 2, T], F32)
+        result = tiles("result", N // P, [P, T], F32)
         ramp = sb.tile([P, K_PASS + PACK], BF16, name="ramp", align_bytes=64)
         eye_bf = sb.tile([P, PACK * K_PASS], BF16, name="eye_bf", align_bytes=64)
-        eye_codes = sb.tile([P, K_PASS], U32, align_bytes=64)
-        eye_scales = sb.tile([P, K_PASS], U8, align_bytes=64)
+        eye_codes = sb.tile([P, K_PASS], U32, name="eye_codes", align_bytes=64)
+        eye_scales = sb.tile([P, K_PASS], U8, name="eye_scales", align_bytes=64)
 
         def bank(b, label):
             return ps.tile([P, T], F32, name=label, tag="bank" + str(b))
@@ -68,97 +66,80 @@ def tile_mix_tierg_none_kernel(tc, g, w, out):
         def g_half(c, h):
             return g_raw[c][:, h * PACK * HALF : (h + 1) * PACK * HALF].rearrange("p (j t) -> p j t", j=PACK)
 
+        def load_g(c, h):
+            rows = g[c * K_PASS : (c + 1) * K_PASS, :].rearrange("(p j) t -> p j t", j=PACK)
+            nc.sync.dma_start(out=g_half(c, h), in_=rows[:, :, h * HALF : (h + 1) * HALF])
+
+        def load_w(c, q):
+            rows = w[c * K_PASS : (c + 1) * K_PASS, :].rearrange("(p j) n -> p j n", j=PACK)
+            nc.sync.dma_start(out=w_raw[PASSES * q + c][:], in_=rows[:, :, q * W_COLS : (q + 1) * W_COLS])
+
         def pack(copy, dst, src):
             copy(out=dst.rearrange("p (c i) j -> p c j i", i=RUN), in_=src.rearrange("p j (c i) -> p c j i", i=RUN))
 
         def quantize(codes, scales, values, fmt):
             nc.vector.quantize_mx(out=codes.bitcast(fmt), scales=scales, in_=values.rearrange("p c j -> p (c j)"))
 
-        def cast_g(copy, c, h, lo, hi):
+        def cast_g(copy, c, h, lo=0, hi=HALF):
             pack(copy, g_bf[c][:, h * HALF + lo : h * HALF + hi, :], g_half(c, h)[:, :, lo:hi])
 
-        def quant_g(c, lo, hi):
-            quantize(gq_codes[c][:, lo:hi], gq_scales[c][:, lo:hi], g_bf[c][:, lo:hi, :], E5M2)
+        def quant_g(c, h):
+            cols = slice(h * HALF, (h + 1) * HALF)
+            quantize(gq_codes[c][:, cols], gq_scales[c][:, cols], g_bf[c][:, cols, :], E5M2)
 
-        gq_values = {}
-
-        def dequant(c, banks, early=False):
-            for j in range(PACK):
-                gq_values[c, j] = bank(banks[j], "gq_values")
-                cols = slice(j * P, (j + 1) * P)
-                nc.tensor.matmul_mx(
-                    out=gq_values[c, j][:],
-                    lhsT=eye_codes[:, cols].bitcast(E4M3),
-                    lhsT_scale=eye_scales[:, cols],
-                    rhs=(gq_codes_wide[c][:, 0:T] if early else gq_codes[c]).bitcast(E5M2),
-                    rhs_scale=gq_scales_wide[c][:, 0:T] if early else gq_scales[c],
-                    start=True,
-                    stop=True,
-                )
-
-        def subtract(c, j):
-            nc.vector.tensor_tensor(
-                out=r_rows[c][:, j, :].rearrange("p (h t) -> p h t", h=2),
-                in0=g_raw[c][:].rearrange("p (h j t) -> p h j t", h=2, j=PACK)[:, :, j, :],
-                in1=gq_values[c, j][:].rearrange("p (h t) -> p h t", h=2),
-                op=mybir.AluOpType.subtract,
+        def pick_row(target, c, j, first, start, stop):
+            cols = slice(j * P, (j + 1) * P)
+            nc.tensor.matmul_mx(
+                out=target[:],
+                lhsT=eye_codes[:, cols].bitcast(E4M3),
+                lhsT_scale=eye_scales[:, cols],
+                rhs=padded_codes[c][:, first : first + T].bitcast(E5M2),
+                rhs_scale=padded_scales[c][:, first : first + T],
+                start=start,
+                stop=stop,
             )
 
-        def subtract_half(c, j, h):
+        row_values = {}
+
+        def dequant(c, h, first_bank):
+            for j in range(PACK):
+                row_values[c, j, h] = bank(first_bank + j, "row_values")
+                pick_row(row_values[c, j, h], c, j, h * HALF, True, True)
+
+        def subtract(c, j, h):
             nc.vector.tensor_tensor(
                 out=r_rows[c][:, j, h * HALF : (h + 1) * HALF],
                 in0=g_half(c, h)[:, j, :],
-                in1=gq_values[c, j][:, HALF:],
+                in1=row_values[c, j, h][:, HALF:],
                 op=mybir.AluOpType.subtract,
             )
 
-        def clear_pads(c):
-            nc.vector.memset(gq_codes_wide[c][:].rearrange("p (s t) -> p s t", s=3)[:, 0:3:2, :], 0)
-            nc.vector.memset(gq_scales_wide[c][:].bitcast(U32).rearrange("p (s t) -> p s t", s=3)[:, 0:3:2, :], 0)
+        def pack_r(c, h):
+            cols = slice(h * HALF, (h + 1) * HALF)
+            pack(vector_copy, r_bf[c][:, cols, :], r_rows[c][:, :, cols])
 
         pair_values = {}
 
-        def dequant_pairs(c, banks):
+        def dequant_pairs(first_bank):
             for u in range(2):
-                pair_values[c, u] = bank(banks[u], "pair_values")
+                pair_values[u] = bank(first_bank + u, "pair_values")
             for e in range(2):
-                window = slice(HALF * (1 - e), HALF * (1 - e) + T)
                 for u in range(2):
-                    cols = slice((2 * u + e) * P, (2 * u + e + 1) * P)
-                    nc.tensor.matmul_mx(
-                        out=pair_values[c, u][:],
-                        lhsT=eye_codes[:, cols].bitcast(E4M3),
-                        lhsT_scale=eye_scales[:, cols],
-                        rhs=gq_codes_wide[c][:, window].bitcast(E5M2),
-                        rhs_scale=gq_scales_wide[c][:, window],
-                        start=e == 0,
-                        stop=e == 1,
-                    )
+                    pick_row(pair_values[u], 1, 2 * u + e, (1 - e) * HALF, e == 0, e == 1)
 
-        def subtract_pair(c, u):
+        def subtract_pair(u):
             nc.vector.tensor_tensor(
-                out=r_pairs[c][:, u, :, :],
-                in0=g_half(c, 0)[:, 2 * u : 2 * u + 2, :].rearrange("p e t -> p t e"),
-                in1=pair_values[c, u][:].rearrange("p (e t) -> p t e", e=2),
+                out=r_pairs[:, u, :, :],
+                in0=g_half(1, 0)[:, 2 * u : 2 * u + 2, :].rearrange("p e t -> p t e"),
+                in1=pair_values[u][:].rearrange("p (e t) -> p t e", e=2),
                 op=mybir.AluOpType.subtract,
             )
 
-        def pack_pairs(copy, c, words):
-            copy(
-                out=r_bf[c][:, 0:HALF, :].rearrange("p t j -> p (t j)").bitcast(words).rearrange("p (t u) -> p t u", u=2),
-                in_=r_pairs[c][:].rearrange("p u t e -> p (u t e)").bitcast(words).rearrange("p (u t) -> p t u", u=2),
+        def pack_pairs():
+            scalar_copy(
+                out=r_bf[1][:, 0:HALF, :].rearrange("p t j -> p (t j)").bitcast(U32).rearrange("p (t u) -> p t u", u=2),
+                in_=r_pairs[:].rearrange("p u t e -> p (u t e)").bitcast(U32).rearrange("p (u t) -> p t u", u=2),
             )
-
-        def gpsimd_copy(out, in_):
-            nc.gpsimd.tensor_scalar(out=out, in0=in_, scalar1=1.0, scalar2=0.0, op0=mybir.AluOpType.mult, op1=mybir.AluOpType.add)
-
-        def warm_up(count):
-            scratch = bank(2 * PACK - 1, "scratch")
-            for i in range(count):
-                nc.tensor.matmul_mx(out=scratch[:], lhsT=eye_codes[:, 0:P].bitcast(E4M3), lhsT_scale=eye_scales[:, 0:P], rhs=eye_codes[:].bitcast(E4M3), rhs_scale=eye_scales[:], start=True, stop=True)
-
-        def pack_r(copy, c, lo, hi):
-            pack(copy, r_bf[c][:, lo:hi, :], r_rows[c][:, :, lo:hi])
 
         def quant_r(c, lo=0, hi=T):
             quantize(gr_codes[c][:, lo:hi], gr_scales[c][:, lo:hi], r_bf[c][:, lo:hi, :], E4M3)
@@ -174,7 +155,7 @@ def tile_mix_tierg_none_kernel(tc, g, w, out):
         first_tier = (gq_codes, gq_scales, E5M2)
         second_tier = (gr_codes, gr_scales, E4M3)
         acc = {}
-        issued = {}
+        columns_done = {}
 
         def product(tier, c, q, sides=(0, 1), lo=0, hi=T):
             i = PASSES * q + c
@@ -182,8 +163,8 @@ def tile_mix_tierg_none_kernel(tc, g, w, out):
             for side in sides:
                 n = 2 * q + side
                 if n not in acc:
-                    acc[n] = bank((6,7,0,1,2,3,4,5)[n], "acc")
-                    issued[n] = 0
+                    acc[n] = bank((n - 2) % BANKS, "acc")
+                    columns_done[n] = 0
                 cols = slice(side * P, (side + 1) * P)
                 nc.tensor.matmul_mx(
                     out=acc[n][:, lo:hi],
@@ -191,133 +172,145 @@ def tile_mix_tierg_none_kernel(tc, g, w, out):
                     lhsT_scale=w_scales[i][:, cols],
                     rhs=codes[c][:, lo:hi].bitcast(fmt),
                     rhs_scale=scales[c][:, lo:hi],
-                    start=issued[n] == 0,
-                    stop=issued[n] + hi - lo == 2 * PASSES * T,
+                    start=columns_done[n] == 0,
+                    stop=columns_done[n] + hi - lo == 2 * PASSES * T,
                 )
-                issued[n] = issued[n] + hi - lo
+                columns_done[n] = columns_done[n] + hi - lo
 
         def both_tiers(c, q, sides=(0, 1)):
             for side in sides:
                 product(first_tier, c, q, (side,))
                 product(second_tier, c, q, (side,))
 
-        def drain(copy, n, lo=0, hi=T):
-            copy(out=result[n // 2][:, n % 2, lo:hi], in_=acc[n][:, lo:hi])
-
-        def store(n, lo=0, hi=T):
-            nc.sync.dma_start(out=out[n * P : (n + 1) * P, lo:hi], in_=result[n // 2][:, n % 2, lo:hi])
-
-        def store_quarter(q):
-            rows = out[q * W_COLS : (q + 1) * W_COLS, :].rearrange("(side p) t -> p side t", side=2)
-            nc.sync.dma_start(out=rows, in_=result[q][:])
-
         def finish(copy, n, lo=0, hi=T):
-            drain(copy, n, lo, hi)
-            store(n, lo, hi)
+            copy(out=result[n][:, lo:hi], in_=acc[n][:, lo:hi])
+            nc.sync.dma_start(out=out[n * P : (n + 1) * P, lo:hi], in_=result[n][:, lo:hi])
 
-        def load_g(c, h):
-            rows = g[c * K_PASS : (c + 1) * K_PASS, :].rearrange("(p j) t -> p j t", j=PACK)
-            nc.sync.dma_start(out=g_half(c, h), in_=rows[:, :, h * HALF : (h + 1) * HALF])
+        for c in range(PASSES):
+            for h in range(2):
+                load_g(c, h)
+        for quarters in (range(LAST), range(LAST, QUARTERS)):
+            for c in range(PASSES):
+                for q in quarters:
+                    load_w(c, q)
 
-        def load_w(c, q):
-            rows = w[c * K_PASS : (c + 1) * K_PASS, :].rearrange("(p j) n -> p j n", j=PACK)
-            nc.sync.dma_start(out=w_raw[PASSES * q + c][:], in_=rows[:, :, q * W_COLS : (q + 1) * W_COLS])
-
-        load_g(0,0)
-        load_g(0,1)
-        load_g(1,0)
-        load_g(1,1)
-        load_w(0,0)
-        load_w(0,1)
-        load_w(0,2)
-        load_w(1,0)
-        load_w(1,1)
-        load_w(1,2)
-        load_w(0,3)
-        load_w(1,3)
-        nc.gpsimd.iota(ramp[:].bitcast(F32), [[1, (K_PASS + PACK) // 2]], base=0, channel_multiplier=-2, allow_small_or_imprecise_dtypes=True)
-        clear_pads(0)
+        words = (K_PASS + PACK) // 2
+        nc.gpsimd.iota(ramp[:].bitcast(F32), [[1, words]], base=0, channel_multiplier=-2, allow_small_or_imprecise_dtypes=True)
+        nc.vector.memset(padded_codes[0][:, 0:HALF], 0)
+        nc.vector.memset(padded_scales[0][:, 0:HALF].bitcast(U32), 0)
         for j in range(PACK):
             shift = PACK - 1 - j
-            nc.vector.tensor_scalar(out=eye_bf[:, j * K_PASS : (j + 1) * K_PASS], in0=ramp[:, shift : shift + K_PASS], scalar1=1.0, scalar2=None, op0=mybir.AluOpType.is_equal)
-        for lo in (0, HALF):
-            nc.vector.quantize_mx(out=eye_codes[:, lo : lo + HALF].bitcast(E4M3), scales=eye_scales[:, lo : lo + HALF], in_=eye_bf[:, PACK * lo : PACK * (lo + HALF)])
-        warm_up(3)
-        cast_g(scalar_copy, 0, 0, 160, HALF)
-        cast_g(vector_copy, 0, 0, 0, 160)
-        clear_pads(1)
-        quant_g(0, 0, HALF)
-        dequant(0, (0, 1, 2, 3), True)
-        cast_g(scalar_copy, 0, 1, 160, HALF)
-        cast_g(vector_copy, 0, 1, 0, 160)
-        subtract_half(0, 0, 0)
-        quant_g(0, HALF, T)
-        subtract_half(0, 1, 0)
-        subtract_half(0, 2, 0)
-        subtract_half(0, 3, 0)
-        dequant(0, (4, 5, 6, 7))
-        cast_g(scalar_copy, 1, 0, 0, HALF)
-        cast_g(scalar_copy, 1, 1, 0, HALF)
-        subtract_half(0, 0, 1)
-        subtract_half(0, 1, 1)
-        quant_g(1, 0, HALF)
-        dequant_pairs(1, (0, 1))
-        subtract_half(0, 2, 1)
-        subtract_half(0, 3, 1)
-        pack_r(vector_copy, 0, 0, HALF)
-        quant_g(1, HALF, T)
-        dequant(1, (2, 3, 4, 5))
-        pack_r(vector_copy, 0, HALF, T)
+            nc.vector.tensor_scalar(
+                out=eye_bf[:, j * K_PASS : (j + 1) * K_PASS],
+                in0=ramp[:, shift : shift + K_PASS],
+                scalar1=1.0,
+                scalar2=None,
+                op0=mybir.AluOpType.is_equal,
+            )
+        for lo in (0, K_PASS // 2):
+            cols = slice(lo, lo + K_PASS // 2)
+            nc.vector.quantize_mx(
+                out=eye_codes[:, cols].bitcast(E4M3),
+                scales=eye_scales[:, cols],
+                in_=eye_bf[:, PACK * lo : PACK * (lo + K_PASS // 2)],
+            )
+
+        unread = bank(BANKS - 1, "unread")
+        for repeat in range(WARM_UPS):
+            nc.tensor.matmul_mx(
+                out=unread[:],
+                lhsT=eye_codes[:, 0:P].bitcast(E4M3),
+                lhsT_scale=eye_scales[:, 0:P],
+                rhs=eye_codes[:].bitcast(E4M3),
+                rhs_scale=eye_scales[:],
+                start=True,
+                stop=True,
+            )
+
+        cast_g(scalar_copy, 0, 0, G_SPLIT, HALF)
+        cast_g(vector_copy, 0, 0, 0, G_SPLIT)
+        nc.vector.memset(padded_codes[1][:].rearrange("p (s t) -> p s t", s=3)[:, 0:3:2, :], 0)
+        nc.vector.memset(padded_scales[1][:].bitcast(U32).rearrange("p (s t) -> p s t", s=3)[:, 0:3:2, :], 0)
+        quant_g(0, 0)
+        dequant(0, 0, first_bank=0)
+        cast_g(scalar_copy, 0, 1, G_SPLIT, HALF)
+        cast_g(vector_copy, 0, 1, 0, G_SPLIT)
+        subtract(0, 0, 0)
+        quant_g(0, 1)
+        for j in range(1, PACK):
+            subtract(0, j, 0)
+        dequant(0, 1, first_bank=PACK)
+
+        cast_g(scalar_copy, 1, 0)
+        cast_g(scalar_copy, 1, 1)
+        subtract(0, 0, 1)
+        subtract(0, 1, 1)
+        quant_g(1, 0)
+        dequant_pairs(first_bank=0)
+        subtract(0, 2, 1)
+        subtract(0, 3, 1)
+        pack_r(0, 0)
+        quant_g(1, 1)
+        dequant(1, 1, first_bank=2)
+        pack_r(0, 1)
+
         cast_w(scalar_copy, 0, 0)
+        subtract_pair(0)
         quant_w(0, 0)
         product(first_tier, 0, 0)
         quant_r(0)
         product(second_tier, 0, 0)
-        subtract_pair(1, 0)
         cast_w(scalar_copy, 0, 1)
         quant_w(0, 1)
-        subtract_pair(1, 1)
+        subtract_pair(1)
         both_tiers(0, 1)
         cast_w(scalar_copy, 0, 2)
-        subtract_half(1, 0, 1)
+        subtract(1, 0, 1)
         quant_w(0, 2)
-        subtract_half(1, 1, 1)
+        subtract(1, 1, 1)
         both_tiers(0, 2)
-        subtract_half(1, 2, 1)
-        subtract_half(1, 3, 1)
+        subtract(1, 2, 1)
+        subtract(1, 3, 1)
+
         cast_w(scalar_copy, 1, 0)
-        pack_pairs(scalar_copy, 1, U32)
+        pack_pairs()
         quant_w(1, 0)
         product(first_tier, 1, 0)
-        pack_r(vector_copy, 1, HALF, T)
+        pack_r(1, 1)
         quant_r(1, 0, HALF)
         product(second_tier, 1, 0, (0,), 0, HALF)
+        cast_w(scalar_copy, 1, 1, 0, P)
+        quant_w(1, 1, 0, P)
+        product(first_tier, 1, 1, (0,))
         quant_r(1, HALF, T)
         product(second_tier, 1, 0, (0,), HALF, T)
         product(second_tier, 1, 0, (1,))
-        cast_w(scalar_copy, 1, 1)
-        quant_w(1, 1)
-        both_tiers(1, 1)
+        product(second_tier, 1, 1, (0,))
+        cast_w(scalar_copy, 1, 1, P, W_COLS)
+        quant_w(1, 1, P, W_COLS)
+        both_tiers(1, 1, (1,))
+
         cast_w(scalar_copy, 1, 2, P, W_COLS)
         cast_w(vector_copy, 1, 2, 0, P)
         finish(scalar_copy, 0, 0, HALF)
         finish(scalar_copy, 0, HALF, T)
         finish(scalar_copy, 1)
-        cast_w(vector_copy, 0, 3, 0, P)
+        cast_w(vector_copy, 0, LAST, 0, P)
         quant_w(1, 2)
         both_tiers(1, 2)
-        cast_w(vector_copy, 0, 3, P, W_COLS)
+        cast_w(vector_copy, 0, LAST, P, W_COLS)
         finish(scalar_copy, 2)
         finish(scalar_copy, 3)
-        cast_w(vector_copy, 1, 3, 0, P)
-        quant_w(0, 3)
-        both_tiers(0, 3, (0,))
-        quant_w(1, 3, 0, P)
-        cast_w(vector_copy, 1, 3, P, W_COLS)
-        both_tiers(1, 3, (0,))
-        both_tiers(0, 3, (1,))
-        quant_w(1, 3, P, W_COLS)
-        both_tiers(1, 3, (1,))
+
+        cast_w(vector_copy, 1, LAST, 0, P)
+        quant_w(0, LAST)
+        both_tiers(0, LAST, (0,))
+        quant_w(1, LAST, 0, P)
+        cast_w(vector_copy, 1, LAST, P, W_COLS)
+        both_tiers(1, LAST, (0,))
+        both_tiers(0, LAST, (1,))
+        quant_w(1, LAST, P, W_COLS)
+        both_tiers(1, LAST, (1,))
         finish(scalar_copy, 4)
         finish(scalar_copy, 5)
         finish(vector_copy, 6)

@@ -8,6 +8,7 @@ FLOPS = 2 * 2 * K * N * T
 F32 = mybir.dt.float32
 BF16 = mybir.dt.bfloat16
 U32 = mybir.dt.uint32
+I32 = mybir.dt.int32
 U8 = mybir.dt.uint8
 E4M3 = mybir.dt.float8_e4m3fn_x4
 E5M2 = mybir.dt.float8_e5m2_x4
@@ -23,7 +24,7 @@ LAST = QUARTERS - 1
 BANKS = 8
 RUN = 4
 G_SPLIT = 160
-WARM_UPS = 3
+ACC_BANKS = (6, 7, 0, 1, 2, 3, 4, 5)
 
 
 def tile_mix_tierg_none_kernel(tc, g, w, out):
@@ -38,41 +39,49 @@ def tile_mix_tierg_none_kernel(tc, g, w, out):
         def tiles(label, count, shape, dtype):
             return [sb.tile(shape, dtype, name=label + str(i), align_bytes=64) for i in range(count)]
 
-        g_raw = tiles("g_raw", PASSES, [P, 2 * PACK * HALF], F32)
+        g_loaded = []
+        w_loaded = {}
         g_bf = tiles("g_bf", PASSES, [P, T, PACK], BF16)
-        padded_codes = tiles("gq_codes", PASSES, [P, HALF + T], U32)
-        padded_scales = tiles("gq_scales", PASSES, [P, HALF + T], U8)
-        gq_codes = [tile[:, HALF:] for tile in padded_codes]
-        gq_scales = [tile[:, HALF:] for tile in padded_scales]
+        all_codes = sb.tile([P, 2 * T + HALF], U32, name="gq_codes", align_bytes=64)
+        all_scales = sb.tile([P, 2 * T + HALF], U8, name="gq_scales", align_bytes=64)
+        origin = (T + HALF, 0)
+        gq_codes = [all_codes[:, origin[c] : origin[c] + T] for c in range(PASSES)]
+        gq_scales = [all_scales[:, origin[c] : origin[c] + T] for c in range(PASSES)]
         r_rows = tiles("r_rows", PASSES, [P, PACK, T], BF16)
-        r_pairs = sb.tile([P, 2, HALF, 2], BF16, name="r_pairs", align_bytes=64)
+        r_pairs = tiles("r_pairs", PASSES, [P, 2, HALF, 2], BF16)
         r_bf = tiles("r_bf", PASSES, [P, T, PACK], BF16)
         gr_codes = tiles("gr_codes", PASSES, [P, T], U32)
         gr_scales = tiles("gr_scales", PASSES, [P, T], U8)
-        pieces = PASSES * QUARTERS
-        w_raw = tiles("w_raw", pieces, [P, PACK, W_COLS], F32)
-        w_bf = tiles("w_bf", pieces, [P, W_COLS, PACK], BF16)
-        w_codes = tiles("w_codes", pieces, [P, W_COLS], U32)
-        w_scales = tiles("w_scales", pieces, [P, W_COLS], U8)
+        w_bf = tiles("w_bf", PASSES, [P, N, PACK], BF16)
+        w_codes = tiles("w_codes", PASSES, [P, N], U32)
+        w_scales = tiles("w_scales", PASSES, [P, N], U8)
         result = tiles("result", N // P, [P, T], F32)
         ramp = sb.tile([P, K_PASS + PACK], BF16, name="ramp", align_bytes=64)
         eye_bf = sb.tile([P, PACK * K_PASS], BF16, name="eye_bf", align_bytes=64)
         eye_codes = sb.tile([P, K_PASS], U32, name="eye_codes", align_bytes=64)
         eye_scales = sb.tile([P, K_PASS], U8, name="eye_scales", align_bytes=64)
 
+        r_place = {(c, h): r_bf[c][:, h * HALF : (h + 1) * HALF, :] for c in range(PASSES) for h in range(2)}
+
         def bank(b, label):
             return ps.tile([P, T], F32, name=label, tag="bank" + str(b))
 
-        def g_half(c, h):
-            return g_raw[c][:, h * PACK * HALF : (h + 1) * PACK * HALF].rearrange("p (j t) -> p j t", j=PACK)
+        def g_rows(c, lo, hi):
+            raw, first = [(raw, first) for (cc, first, last, raw) in g_loaded if cc == c and first <= lo and hi <= last][0]
+            return raw[:, :, lo - first : hi - first]
 
-        def load_g(c, h):
+        def load_g(c, lo, hi):
             rows = g[c * K_PASS : (c + 1) * K_PASS, :].rearrange("(p j) t -> p j t", j=PACK)
-            nc.sync.dma_start(out=g_half(c, h), in_=rows[:, :, h * HALF : (h + 1) * HALF])
+            raw = sb.tile([P, PACK, hi - lo], F32, name="g_raw" + str(c * T + lo), align_bytes=64)
+            nc.sync.dma_start(out=raw[:], in_=rows[:, :, lo:hi])
+            g_loaded.append((c, lo, hi, raw))
 
-        def load_w(c, q):
+        def load_w(c, first, count):
             rows = w[c * K_PASS : (c + 1) * K_PASS, :].rearrange("(p j) n -> p j n", j=PACK)
-            nc.sync.dma_start(out=w_raw[PASSES * q + c][:], in_=rows[:, :, q * W_COLS : (q + 1) * W_COLS])
+            raw = sb.tile([P, PACK, count * P], F32, name="w_raw" + str(BANKS * c + first), align_bytes=64)
+            nc.sync.dma_start(out=raw[:], in_=rows[:, :, first * P : (first + count) * P])
+            for n in range(first, first + count):
+                w_loaded[c, n] = (raw, first)
 
         def pack(copy, dst, src):
             copy(out=dst.rearrange("p (c i) j -> p c j i", i=RUN), in_=src.rearrange("p j (c i) -> p c j i", i=RUN))
@@ -80,125 +89,109 @@ def tile_mix_tierg_none_kernel(tc, g, w, out):
         def quantize(codes, scales, values, fmt):
             nc.vector.quantize_mx(out=codes.bitcast(fmt), scales=scales, in_=values.rearrange("p c j -> p (c j)"))
 
-        def cast_g(copy, c, h, lo=0, hi=HALF):
-            pack(copy, g_bf[c][:, h * HALF + lo : h * HALF + hi, :], g_half(c, h)[:, :, lo:hi])
+        def cast_g(copy, c, lo, hi):
+            pack(copy, g_bf[c][:, lo:hi, :], g_rows(c, lo, hi))
 
-        def quant_g(c, h):
-            cols = slice(h * HALF, (h + 1) * HALF)
-            quantize(gq_codes[c][:, cols], gq_scales[c][:, cols], g_bf[c][:, cols, :], E5M2)
+        def quant_g(c, lo, hi):
+            quantize(gq_codes[c][:, lo:hi], gq_scales[c][:, lo:hi], g_bf[c][:, lo:hi, :], E5M2)
 
-        def pick_row(target, c, j, first, start, stop):
+        def pick_row(target, j, first, start, stop):
             cols = slice(j * P, (j + 1) * P)
             nc.tensor.matmul_mx(
                 out=target[:],
                 lhsT=eye_codes[:, cols].bitcast(E4M3),
                 lhsT_scale=eye_scales[:, cols],
-                rhs=padded_codes[c][:, first : first + T].bitcast(E5M2),
-                rhs_scale=padded_scales[c][:, first : first + T],
+                rhs=all_codes[:, first : first + T].bitcast(E5M2),
+                rhs_scale=all_scales[:, first : first + T],
                 start=start,
                 stop=stop,
             )
 
         row_values = {}
 
-        def dequant(c, h, first_bank):
+        def dequant(c, h, shift, banks):
             for j in range(PACK):
-                row_values[c, j, h] = bank(first_bank + j, "row_values")
-                pick_row(row_values[c, j, h], c, j, h * HALF, True, True)
+                target = bank(banks[j], "row_values")
+                pick_row(target, j, origin[c] + shift, True, True)
+                row_values[c, j, h] = target[:, h * HALF - shift : (h + 1) * HALF - shift]
 
         def subtract(c, j, h):
             nc.vector.tensor_tensor(
                 out=r_rows[c][:, j, h * HALF : (h + 1) * HALF],
-                in0=g_half(c, h)[:, j, :],
-                in1=row_values[c, j, h][:, HALF:],
+                in0=g_rows(c, h * HALF, (h + 1) * HALF)[:, j, :],
+                in1=row_values[c, j, h],
                 op=mybir.AluOpType.subtract,
             )
 
-        def pack_r(c, h):
-            cols = slice(h * HALF, (h + 1) * HALF)
-            pack(vector_copy, r_bf[c][:, cols, :], r_rows[c][:, :, cols])
+        def gpsimd_copy(out, in_):
+            nc.gpsimd.tensor_scalar(out=out, in0=in_, scalar1=1.0, scalar2=0.0, op0=mybir.AluOpType.mult, op1=mybir.AluOpType.add)
+
+        def r_packed(c, lo, hi):
+            if hi - lo == T:
+                return r_bf[c][:]
+            h = lo // HALF
+            return r_place[c, h][:, lo - h * HALF : hi - h * HALF, :]
+
+        def pack_r(copy, c, lo, hi):
+            pack(copy, r_packed(c, lo, hi), r_rows[c][:, :, lo:hi])
 
         pair_values = {}
 
-        def dequant_pairs(first_bank):
+        def dequant_pairs(c, first_bank):
             for u in range(2):
-                pair_values[u] = bank(first_bank + u, "pair_values")
-            for e in range(2):
+                pair_values[c, u] = bank(first_bank + u, "pair_values")
+            for e in (1, 0):
                 for u in range(2):
-                    pick_row(pair_values[u], 1, 2 * u + e, (1 - e) * HALF, e == 0, e == 1)
+                    pick_row(pair_values[c, u], 2 * u + e, origin[c] + (1 - e) * HALF, e == 1, e == 0)
 
-        def subtract_pair(u):
+        def subtract_pair(c, u):
             nc.vector.tensor_tensor(
-                out=r_pairs[:, u, :, :],
-                in0=g_half(1, 0)[:, 2 * u : 2 * u + 2, :].rearrange("p e t -> p t e"),
-                in1=pair_values[u][:].rearrange("p (e t) -> p t e", e=2),
+                out=r_pairs[c][:, u, :, :],
+                in0=g_rows(c, HALF, T)[:, 2 * u : 2 * u + 2, :].rearrange("p e t -> p t e"),
+                in1=pair_values[c, u][:].rearrange("p (e t) -> p t e", e=2),
                 op=mybir.AluOpType.subtract,
             )
 
-        def pack_pairs():
-            scalar_copy(
-                out=r_bf[1][:, 0:HALF, :].rearrange("p t j -> p (t j)").bitcast(U32).rearrange("p (t u) -> p t u", u=2),
-                in_=r_pairs[:].rearrange("p u t e -> p (u t e)").bitcast(U32).rearrange("p (u t) -> p t u", u=2),
+        def pack_pairs(c, copy, word):
+            copy(
+                out=r_place[c, 1].rearrange("p t j -> p (t j)").bitcast(word).rearrange("p (t u) -> p t u", u=2),
+                in_=r_pairs[c][:].rearrange("p u t e -> p (u t e)").bitcast(word).rearrange("p (u t) -> p t u", u=2),
             )
 
         def quant_r(c, lo=0, hi=T):
-            quantize(gr_codes[c][:, lo:hi], gr_scales[c][:, lo:hi], r_bf[c][:, lo:hi, :], E4M3)
+            quantize(gr_codes[c][:, lo:hi], gr_scales[c][:, lo:hi], r_packed(c, lo, hi), E4M3)
 
-        def cast_w(copy, c, q, lo=0, hi=W_COLS):
-            i = PASSES * q + c
-            pack(copy, w_bf[i][:, lo:hi, :], w_raw[i][:, :, lo:hi])
+        def cast_w(copy, c, n, count=1):
+            raw, first = w_loaded[c, n]
+            pack(copy, w_bf[c][:, n * P : (n + count) * P, :], raw[:, :, (n - first) * P : (n - first + count) * P])
 
-        def quant_w(c, q, lo=0, hi=W_COLS):
-            i = PASSES * q + c
-            quantize(w_codes[i][:, lo:hi], w_scales[i][:, lo:hi], w_bf[i][:, lo:hi, :], E4M3)
+        def quant_w(c, n, count=1):
+            cols = slice(n * P, (n + count) * P)
+            quantize(w_codes[c][:, cols], w_scales[c][:, cols], w_bf[c][:, cols, :], E4M3)
 
         first_tier = (gq_codes, gq_scales, E5M2)
         second_tier = (gr_codes, gr_scales, E4M3)
         acc = {}
         columns_done = {}
 
-        def product(tier, c, q, sides=(0, 1), lo=0, hi=T):
-            i = PASSES * q + c
+        def product(tier, c, n, lo=0, hi=T):
             codes, scales, fmt = tier
-            for side in sides:
-                n = 2 * q + side
-                if n not in acc:
-                    acc[n] = bank((n - 2) % BANKS, "acc")
-                    columns_done[n] = 0
-                cols = slice(side * P, (side + 1) * P)
-                nc.tensor.matmul_mx(
-                    out=acc[n][:, lo:hi],
-                    lhsT=w_codes[i][:, cols].bitcast(E4M3),
-                    lhsT_scale=w_scales[i][:, cols],
-                    rhs=codes[c][:, lo:hi].bitcast(fmt),
-                    rhs_scale=scales[c][:, lo:hi],
-                    start=columns_done[n] == 0,
-                    stop=columns_done[n] + hi - lo == 2 * PASSES * T,
-                )
-                columns_done[n] = columns_done[n] + hi - lo
+            if n not in acc:
+                acc[n] = bank(ACC_BANKS[n], "acc")
+                columns_done[n] = 0
+            cols = slice(n * P, (n + 1) * P)
+            nc.tensor.matmul_mx(
+                out=acc[n][:, lo:hi],
+                lhsT=w_codes[c][:, cols].bitcast(E4M3),
+                lhsT_scale=w_scales[c][:, cols],
+                rhs=codes[c][:, lo:hi].bitcast(fmt),
+                rhs_scale=scales[c][:, lo:hi],
+                start=columns_done[n] == 0,
+                stop=columns_done[n] + hi - lo == 2 * PASSES * T,
+            )
+            columns_done[n] = columns_done[n] + hi - lo
 
-        def both_tiers(c, q, sides=(0, 1)):
-            for side in sides:
-                product(first_tier, c, q, (side,))
-                product(second_tier, c, q, (side,))
-
-        def finish(copy, n, lo=0, hi=T):
-            copy(out=result[n][:, lo:hi], in_=acc[n][:, lo:hi])
-            nc.sync.dma_start(out=out[n * P : (n + 1) * P, lo:hi], in_=result[n][:, lo:hi])
-
-        for c in range(PASSES):
-            for h in range(2):
-                load_g(c, h)
-        for quarters in (range(LAST), range(LAST, QUARTERS)):
-            for c in range(PASSES):
-                for q in quarters:
-                    load_w(c, q)
-
-        words = (K_PASS + PACK) // 2
-        nc.gpsimd.iota(ramp[:].bitcast(F32), [[1, words]], base=0, channel_multiplier=-2, allow_small_or_imprecise_dtypes=True)
-        nc.vector.memset(padded_codes[0][:, 0:HALF], 0)
-        nc.vector.memset(padded_scales[0][:, 0:HALF].bitcast(U32), 0)
-        for j in range(PACK):
+        def compare(j):
             shift = PACK - 1 - j
             nc.vector.tensor_scalar(
                 out=eye_bf[:, j * K_PASS : (j + 1) * K_PASS],
@@ -207,110 +200,143 @@ def tile_mix_tierg_none_kernel(tc, g, w, out):
                 scalar2=None,
                 op0=mybir.AluOpType.is_equal,
             )
-        for lo in (0, K_PASS // 2):
-            cols = slice(lo, lo + K_PASS // 2)
+
+        def quant_eye(lo, hi):
             nc.vector.quantize_mx(
-                out=eye_codes[:, cols].bitcast(E4M3),
-                scales=eye_scales[:, cols],
-                in_=eye_bf[:, PACK * lo : PACK * (lo + K_PASS // 2)],
+                out=eye_codes[:, lo * P : hi * P].bitcast(E4M3),
+                scales=eye_scales[:, lo * P : hi * P],
+                in_=eye_bf[:, lo * K_PASS : hi * K_PASS],
             )
 
         unread = bank(BANKS - 1, "unread")
-        for repeat in range(WARM_UPS):
+
+        def warm_up(codes, scales):
             nc.tensor.matmul_mx(
                 out=unread[:],
-                lhsT=eye_codes[:, 0:P].bitcast(E4M3),
-                lhsT_scale=eye_scales[:, 0:P],
-                rhs=eye_codes[:].bitcast(E4M3),
-                rhs_scale=eye_scales[:],
+                lhsT=codes.bitcast(E4M3),
+                lhsT_scale=scales,
+                rhs=all_codes[:, HALF : HALF + T].bitcast(E5M2),
+                rhs_scale=all_codes[:, HALF : HALF + T // 4].bitcast(U8),
                 start=True,
                 stop=True,
             )
 
-        cast_g(scalar_copy, 0, 0, G_SPLIT, HALF)
-        cast_g(vector_copy, 0, 0, 0, G_SPLIT)
-        nc.vector.memset(padded_codes[1][:].rearrange("p (s t) -> p s t", s=3)[:, 0:3:2, :], 0)
-        nc.vector.memset(padded_scales[1][:].bitcast(U32).rearrange("p (s t) -> p s t", s=3)[:, 0:3:2, :], 0)
-        quant_g(0, 0)
-        dequant(0, 0, first_bank=0)
-        cast_g(scalar_copy, 0, 1, G_SPLIT, HALF)
-        cast_g(vector_copy, 0, 1, 0, G_SPLIT)
+        def both_tiers(c, n):
+            product(first_tier, c, n)
+            product(second_tier, c, n)
+
+        def finish(copy, n, lo=0, hi=T):
+            copy(out=result[n][:, lo:hi], in_=acc[n][:, lo:hi])
+            nc.sync.dma_start(out=out[n * P : (n + 1) * P, lo:hi], in_=result[n][:, lo:hi])
+
+        load_g(0, 0, 256)
+        load_g(0, 256, 512)
+        load_g(1, 256, 512)
+        load_g(1, 0, 256)
+        load_w(0, 0, 2)
+        load_w(0, 2, 2)
+        load_w(0, 4, 2)
+        load_w(1, 0, 2)
+        load_w(1, 2, 2)
+        load_w(1, 4, 2)
+        load_w(0, 6, 2)
+        load_w(1, 6, 2)
+        nc.gpsimd.iota(ramp[:].bitcast(F32), [[1, (K_PASS + PACK) // 2]], base=0, channel_multiplier=-2, allow_small_or_imprecise_dtypes=True)
+        nc.vector.memset(all_codes[:, 0 : T + HALF], 0)
+        for repeat in range(2):
+            warm_up(all_codes[:, T : T + P], all_codes[:, T : T + P // 4].bitcast(U8))
+        compare(0)
+        compare(1)
+        quant_eye(0, 2)
+        for repeat in range(2):
+            warm_up(eye_codes[:, 0:P], eye_scales[:, 0:P])
+        nc.vector.memset(all_scales[:, 0 : T + HALF].bitcast(U32), 0)
+        cast_g(scalar_copy, 0, G_SPLIT, HALF)
+        cast_g(vector_copy, 0, 0, G_SPLIT)
+        compare(2)
+        compare(3)
+        quant_g(0, 0, HALF)
+        quant_eye(2, 4)
+        dequant(0, 0, -HALF, (0, 1, 2, 3))
+        cast_g(scalar_copy, 0, HALF + G_SPLIT, T)
+        cast_g(vector_copy, 0, HALF, HALF + G_SPLIT)
         subtract(0, 0, 0)
-        quant_g(0, 1)
+        quant_g(0, HALF, T)
         for j in range(1, PACK):
             subtract(0, j, 0)
-        dequant(0, 1, first_bank=PACK)
-
-        cast_g(scalar_copy, 1, 0)
-        cast_g(scalar_copy, 1, 1)
+        dequant(0, 1, 0, (4, 5, 6, 7))
+        cast_g(scalar_copy, 1, HALF, T)
+        cast_g(scalar_copy, 1, 0, HALF)
         subtract(0, 0, 1)
         subtract(0, 1, 1)
-        quant_g(1, 0)
-        dequant_pairs(first_bank=0)
+        quant_g(1, HALF, T)
+        dequant_pairs(1, first_bank=0)
         subtract(0, 2, 1)
         subtract(0, 3, 1)
-        pack_r(0, 0)
-        quant_g(1, 1)
-        dequant(1, 1, first_bank=2)
-        pack_r(0, 1)
-
-        cast_w(scalar_copy, 0, 0)
-        subtract_pair(0)
-        quant_w(0, 0)
+        pack_r(vector_copy, 0, 0, HALF)
+        quant_g(1, 0, HALF)
+        dequant(1, 0, 0, (2, 3, 4, 5))
+        pack_r(vector_copy, 0, HALF, T)
+        cast_w(scalar_copy, 0, 0, 2)
+        subtract_pair(1, 0)
+        quant_w(0, 0, 2)
         product(first_tier, 0, 0)
+        product(first_tier, 0, 1)
         quant_r(0)
         product(second_tier, 0, 0)
-        cast_w(scalar_copy, 0, 1)
-        quant_w(0, 1)
-        subtract_pair(1)
-        both_tiers(0, 1)
-        cast_w(scalar_copy, 0, 2)
-        subtract(1, 0, 1)
-        quant_w(0, 2)
-        subtract(1, 1, 1)
+        product(second_tier, 0, 1)
+        cast_w(scalar_copy, 0, 2, 2)
+        quant_w(0, 2, 2)
+        subtract_pair(1, 1)
         both_tiers(0, 2)
-        subtract(1, 2, 1)
-        subtract(1, 3, 1)
-
-        cast_w(scalar_copy, 1, 0)
-        pack_pairs()
-        quant_w(1, 0)
+        both_tiers(0, 3)
+        cast_w(scalar_copy, 0, 4, 2)
+        subtract(1, 0, 0)
+        quant_w(0, 4, 2)
+        subtract(1, 1, 0)
+        both_tiers(0, 4)
+        both_tiers(0, 5)
+        subtract(1, 2, 0)
+        subtract(1, 3, 0)
+        cast_w(scalar_copy, 1, 0, 2)
+        pack_pairs(1, scalar_copy, U32)
+        quant_w(1, 0, 2)
         product(first_tier, 1, 0)
-        pack_r(1, 1)
-        quant_r(1, 0, HALF)
-        product(second_tier, 1, 0, (0,), 0, HALF)
-        cast_w(scalar_copy, 1, 1, 0, P)
-        quant_w(1, 1, 0, P)
-        product(first_tier, 1, 1, (0,))
+        product(first_tier, 1, 1)
+        pack_r(vector_copy, 1, 0, HALF)
         quant_r(1, HALF, T)
-        product(second_tier, 1, 0, (0,), HALF, T)
-        product(second_tier, 1, 0, (1,))
-        product(second_tier, 1, 1, (0,))
-        cast_w(scalar_copy, 1, 1, P, W_COLS)
-        quant_w(1, 1, P, W_COLS)
-        both_tiers(1, 1, (1,))
-
-        cast_w(scalar_copy, 1, 2, P, W_COLS)
-        cast_w(vector_copy, 1, 2, 0, P)
+        product(second_tier, 1, 0, HALF, T)
+        cast_w(scalar_copy, 1, 2)
+        quant_w(1, 2)
+        product(first_tier, 1, 2)
+        quant_r(1, 0, HALF)
+        product(second_tier, 1, 0, 0, HALF)
+        product(second_tier, 1, 1)
+        product(second_tier, 1, 2)
+        cast_w(scalar_copy, 1, 3)
+        quant_w(1, 3)
+        both_tiers(1, 3)
+        cast_w(scalar_copy, 1, 5)
+        cast_w(vector_copy, 1, 4)
         finish(scalar_copy, 0, 0, HALF)
         finish(scalar_copy, 0, HALF, T)
         finish(scalar_copy, 1)
-        cast_w(vector_copy, 0, LAST, 0, P)
-        quant_w(1, 2)
-        both_tiers(1, 2)
-        cast_w(vector_copy, 0, LAST, P, W_COLS)
+        cast_w(vector_copy, 0, 6)
+        quant_w(1, 4, 2)
+        both_tiers(1, 4)
+        both_tiers(1, 5)
+        cast_w(vector_copy, 0, 7)
         finish(scalar_copy, 2)
         finish(scalar_copy, 3)
-
-        cast_w(vector_copy, 1, LAST, 0, P)
-        quant_w(0, LAST)
-        both_tiers(0, LAST, (0,))
-        quant_w(1, LAST, 0, P)
-        cast_w(vector_copy, 1, LAST, P, W_COLS)
-        both_tiers(1, LAST, (0,))
-        both_tiers(0, LAST, (1,))
-        quant_w(1, LAST, P, W_COLS)
-        both_tiers(1, LAST, (1,))
+        cast_w(vector_copy, 1, 6)
+        quant_w(0, 6, 2)
+        both_tiers(0, 6)
+        quant_w(1, 6)
+        cast_w(vector_copy, 1, 7)
+        both_tiers(1, 6)
+        both_tiers(0, 7)
+        quant_w(1, 7)
+        both_tiers(1, 7)
         finish(scalar_copy, 4)
         finish(scalar_copy, 5)
         finish(vector_copy, 6)

@@ -24,7 +24,7 @@ LAST = QUARTERS - 1
 BANKS = 8
 RUN = 4
 G_SPLIT = 160
-ACC_BANKS = (6, 7, 0, 1, 2, 3, 4, 5)
+ACC_BANKS = (0, 1, 2, 3, 4, 5, 6, 7)
 
 
 def tile_mix_tierg_none_kernel(tc, g, w, out):
@@ -62,6 +62,8 @@ def tile_mix_tierg_none_kernel(tc, g, w, out):
         eye_scales = sb.tile([P, K_PASS], U8, name="eye_scales", align_bytes=64)
 
         r_place = {(c, h): r_bf[c][:, h * HALF : (h + 1) * HALF, :] for c in range(PASSES) for h in range(2)}
+        r_place[0, 1] = g_bf[1][:, 0:HALF, :]
+        r_place[1, 1] = g_bf[1][:, 0:HALF, :]
 
         def bank(b, label):
             return ps.tile([P, T], F32, name=label, tag="bank" + str(b))
@@ -123,8 +125,15 @@ def tile_mix_tierg_none_kernel(tc, g, w, out):
                 op=mybir.AluOpType.subtract,
             )
 
-        def gpsimd_copy(out, in_):
-            nc.gpsimd.tensor_scalar(out=out, in0=in_, scalar1=1.0, scalar2=0.0, op0=mybir.AluOpType.mult, op1=mybir.AluOpType.add)
+        def gpsimd_pack_r(c, lo, hi):
+            nc.gpsimd.tensor_scalar(
+                out=r_packed(c, lo, hi),
+                in0=r_rows[c][:, :, lo:hi].rearrange("p j t -> p t j"),
+                scalar1=1.0,
+                scalar2=0.0,
+                op0=mybir.AluOpType.mult,
+                op1=mybir.AluOpType.add,
+            )
 
         def r_packed(c, lo, hi):
             if hi - lo == T:
@@ -242,7 +251,7 @@ def tile_mix_tierg_none_kernel(tc, g, w, out):
         load_w(0, 6, 2)
         load_w(1, 6, 2)
         nc.gpsimd.iota(ramp[:].bitcast(F32), [[1, (K_PASS + PACK) // 2]], base=0, channel_multiplier=-2, allow_small_or_imprecise_dtypes=True)
-        nc.vector.memset(all_codes[:, 0 : T + HALF], 0)
+        nc.vector.memset(all_codes[:, HALF : T + HALF], 0)
         for repeat in range(2):
             warm_up(all_codes[:, T : T + P], all_codes[:, T : T + P // 4].bitcast(U8))
         compare(0)
@@ -250,7 +259,7 @@ def tile_mix_tierg_none_kernel(tc, g, w, out):
         quant_eye(0, 2)
         for repeat in range(2):
             warm_up(eye_codes[:, 0:P], eye_scales[:, 0:P])
-        nc.vector.memset(all_scales[:, 0 : T + HALF].bitcast(U32), 0)
+        nc.vector.memset(all_scales[:, T : T + HALF].bitcast(U32), 0)
         cast_g(scalar_copy, 0, G_SPLIT, HALF)
         cast_g(vector_copy, 0, 0, G_SPLIT)
         compare(2)
@@ -267,52 +276,55 @@ def tile_mix_tierg_none_kernel(tc, g, w, out):
         dequant(0, 1, 0, (4, 5, 6, 7))
         cast_g(scalar_copy, 1, HALF, T)
         cast_g(scalar_copy, 1, 0, HALF)
-        subtract(0, 0, 1)
-        subtract(0, 1, 1)
+        gpsimd_pack_r(0, 0, 112)
+        for j in range(PACK):
+            subtract(0, j, 1)
         quant_g(1, HALF, T)
-        dequant_pairs(1, first_bank=0)
-        subtract(0, 2, 1)
-        subtract(0, 3, 1)
-        pack_r(vector_copy, 0, 0, HALF)
+        dequant(1, 1, HALF, (0, 1, 2, 3))
+        pack_r(vector_copy, 0, 112, HALF)
         quant_g(1, 0, HALF)
-        dequant(1, 0, 0, (2, 3, 4, 5))
-        pack_r(vector_copy, 0, HALF, T)
+        dequant(1, 0, 0, (4, 5, 6, 7))
+        quant_r(0, 0, HALF)
+        gpsimd_pack_r(0, HALF, HALF + 144)
+        for j in range(PACK):
+            subtract(1, j, 1)
         cast_w(scalar_copy, 0, 0, 2)
-        subtract_pair(1, 0)
         quant_w(0, 0, 2)
         product(first_tier, 0, 0)
         product(first_tier, 0, 1)
-        quant_r(0)
-        product(second_tier, 0, 0)
-        product(second_tier, 0, 1)
+        product(second_tier, 0, 0, 0, HALF)
+        product(second_tier, 0, 1, 0, HALF)
+        pack_r(vector_copy, 0, HALF + 144, T)
+        subtract(1, 0, 0)
+        quant_r(0, HALF, T)
+        product(second_tier, 0, 0, HALF, T)
+        product(second_tier, 0, 1, HALF, T)
         cast_w(scalar_copy, 0, 2, 2)
         quant_w(0, 2, 2)
-        subtract_pair(1, 1)
         both_tiers(0, 2)
         both_tiers(0, 3)
+        gpsimd_pack_r(1, HALF, HALF + 96)
+        for j in range(1, PACK):
+            subtract(1, j, 0)
         cast_w(scalar_copy, 0, 4, 2)
-        subtract(1, 0, 0)
         quant_w(0, 4, 2)
-        subtract(1, 1, 0)
         both_tiers(0, 4)
         both_tiers(0, 5)
-        subtract(1, 2, 0)
-        subtract(1, 3, 0)
         cast_w(scalar_copy, 1, 0, 2)
-        pack_pairs(1, scalar_copy, U32)
+        pack_r(scalar_copy, 1, T - 96, T)
+        pack_r(vector_copy, 1, HALF + 96, T - 96)
+        pack_r(vector_copy, 1, 0, HALF - 0)
         quant_w(1, 0, 2)
         product(first_tier, 1, 0)
         product(first_tier, 1, 1)
-        pack_r(vector_copy, 1, 0, HALF)
         quant_r(1, HALF, T)
         product(second_tier, 1, 0, HALF, T)
-        cast_w(scalar_copy, 1, 2)
-        quant_w(1, 2)
-        product(first_tier, 1, 2)
         quant_r(1, 0, HALF)
         product(second_tier, 1, 0, 0, HALF)
         product(second_tier, 1, 1)
-        product(second_tier, 1, 2)
+        cast_w(scalar_copy, 1, 2)
+        quant_w(1, 2)
+        both_tiers(1, 2)
         cast_w(scalar_copy, 1, 3)
         quant_w(1, 3)
         both_tiers(1, 3)

@@ -8,7 +8,6 @@ FLOPS = 2 * 2 * K * N * T
 F32 = mybir.dt.float32
 BF16 = mybir.dt.bfloat16
 U32 = mybir.dt.uint32
-I32 = mybir.dt.int32
 U8 = mybir.dt.uint8
 E4M3 = mybir.dt.float8_e4m3fn_x4
 E5M2 = mybir.dt.float8_e5m2_x4
@@ -18,13 +17,12 @@ PACK = 4
 K_PASS = P * PACK
 PASSES = K // K_PASS
 HALF = T // 2
-W_COLS = 256
-QUARTERS = N // W_COLS
-LAST = QUARTERS - 1
-BANKS = 8
+TILES = N // P
+PAIR = 2
 RUN = 4
+WARM_UPS = 2
 G_SPLIT = 160
-ACC_BANKS = (0, 1, 2, 3, 4, 5, 6, 7)
+GPSIMD_COLUMNS = {(0, 0): 144, (0, 1): 176, (1, 1): 128}
 
 
 def tile_mix_tierg_none_kernel(tc, g, w, out):
@@ -36,171 +34,58 @@ def tile_mix_tierg_none_kernel(tc, g, w, out):
         ps = ctx.enter_context(tc.psum_pool(name="ps", bufs=1))
         ctx.enter_context(tc.manual_schedule())
 
-        def tiles(label, count, shape, dtype):
-            return [sb.tile(shape, dtype, name=label + str(i), align_bytes=64) for i in range(count)]
+        def tile(label, shape, dtype):
+            return sb.tile(shape, dtype, name=label, align_bytes=64)
 
-        g_loaded = []
-        w_loaded = {}
+        def tiles(label, count, shape, dtype):
+            return [tile(label + str(i), shape, dtype) for i in range(count)]
+
+        halves = ((0, 0), (0, 1), (1, 1), (1, 0))
+        g_raw = {(c, h): tile("g_raw" + str(2 * c + h), [P, PACK, HALF], F32) for c, h in halves}
         g_bf = tiles("g_bf", PASSES, [P, T, PACK], BF16)
-        all_codes = sb.tile([P, 2 * T + HALF], U32, name="gq_codes", align_bytes=64)
-        all_scales = sb.tile([P, 2 * T + HALF], U8, name="gq_scales", align_bytes=64)
+        padded_codes = tile("gq_codes", [P, 2 * T + HALF], U32)
+        padded_scales = tile("gq_scales", [P, 2 * T + HALF], U8)
+        pad = slice(T, T + HALF)
         origin = (T + HALF, 0)
-        gq_codes = [all_codes[:, origin[c] : origin[c] + T] for c in range(PASSES)]
-        gq_scales = [all_scales[:, origin[c] : origin[c] + T] for c in range(PASSES)]
+        gq_codes = [padded_codes[:, origin[c] : origin[c] + T] for c in range(PASSES)]
+        gq_scales = [padded_scales[:, origin[c] : origin[c] + T] for c in range(PASSES)]
         r_rows = tiles("r_rows", PASSES, [P, PACK, T], BF16)
-        r_pairs = tiles("r_pairs", PASSES, [P, 2, HALF, 2], BF16)
-        r_bf = tiles("r_bf", PASSES, [P, T, PACK], BF16)
+        r_own = tiles("r_bf", PASSES, [P, HALF, PACK], BF16)
+        r_bf = {(0, 0): r_own[0][:], (0, 1): g_bf[1][:, 0:HALF, :], (1, 1): g_bf[1][:, 0:HALF, :], (1, 0): r_own[1][:]}
         gr_codes = tiles("gr_codes", PASSES, [P, T], U32)
         gr_scales = tiles("gr_scales", PASSES, [P, T], U8)
+        w_raw = [tiles("w_raw" + str(c), TILES // PAIR, [P, PACK, PAIR * P], F32) for c in range(PASSES)]
         w_bf = tiles("w_bf", PASSES, [P, N, PACK], BF16)
         w_codes = tiles("w_codes", PASSES, [P, N], U32)
         w_scales = tiles("w_scales", PASSES, [P, N], U8)
-        result = tiles("result", N // P, [P, T], F32)
-        ramp = sb.tile([P, K_PASS + PACK], BF16, name="ramp", align_bytes=64)
-        eye_bf = sb.tile([P, PACK * K_PASS], BF16, name="eye_bf", align_bytes=64)
-        eye_codes = sb.tile([P, K_PASS], U32, name="eye_codes", align_bytes=64)
-        eye_scales = sb.tile([P, K_PASS], U8, name="eye_scales", align_bytes=64)
-
-        r_place = {(c, h): r_bf[c][:, h * HALF : (h + 1) * HALF, :] for c in range(PASSES) for h in range(2)}
-        r_place[0, 1] = g_bf[1][:, 0:HALF, :]
-        r_place[1, 1] = g_bf[1][:, 0:HALF, :]
+        result = tiles("result", TILES, [P, T], F32)
+        ramp = tile("ramp", [P, K_PASS + PACK], BF16)
+        eye_bf = tile("eye_bf", [P, PACK * K_PASS], BF16)
+        eye_codes = tile("eye_codes", [P, K_PASS], U32)
+        eye_scales = tile("eye_scales", [P, K_PASS], U8)
 
         def bank(b, label):
             return ps.tile([P, T], F32, name=label, tag="bank" + str(b))
 
-        def g_rows(c, lo, hi):
-            raw, first = [(raw, first) for (cc, first, last, raw) in g_loaded if cc == c and first <= lo and hi <= last][0]
-            return raw[:, :, lo - first : hi - first]
+        def half_columns(h, lo=0, hi=HALF):
+            return slice(h * HALF + lo, h * HALF + hi)
 
-        def load_g(c, lo, hi):
-            rows = g[c * K_PASS : (c + 1) * K_PASS, :].rearrange("(p j) t -> p j t", j=PACK)
-            raw = sb.tile([P, PACK, hi - lo], F32, name="g_raw" + str(c * T + lo), align_bytes=64)
-            nc.sync.dma_start(out=raw[:], in_=rows[:, :, lo:hi])
-            g_loaded.append((c, lo, hi, raw))
+        def tile_columns(n, count=1):
+            return slice(n * P, (n + count) * P)
 
-        def load_w(c, first, count):
-            rows = w[c * K_PASS : (c + 1) * K_PASS, :].rearrange("(p j) n -> p j n", j=PACK)
-            raw = sb.tile([P, PACK, count * P], F32, name="w_raw" + str(BANKS * c + first), align_bytes=64)
-            nc.sync.dma_start(out=raw[:], in_=rows[:, :, first * P : (first + count) * P])
-            for n in range(first, first + count):
-                w_loaded[c, n] = (raw, first)
+        def pass_rows(x, c):
+            return x[c * K_PASS : (c + 1) * K_PASS, :].rearrange("(p j) x -> p j x", j=PACK)
 
         def pack(copy, dst, src):
             copy(out=dst.rearrange("p (c i) j -> p c j i", i=RUN), in_=src.rearrange("p j (c i) -> p c j i", i=RUN))
 
         def quantize(codes, scales, values, fmt):
-            nc.vector.quantize_mx(out=codes.bitcast(fmt), scales=scales, in_=values.rearrange("p c j -> p (c j)"))
+            nc.vector.quantize_mx(out=codes.bitcast(fmt), scales=scales, in_=values)
 
-        def cast_g(copy, c, lo, hi):
-            pack(copy, g_bf[c][:, lo:hi, :], g_rows(c, lo, hi))
+        def quantize_packed(codes, scales, values, fmt):
+            quantize(codes, scales, values.rearrange("p c j -> p (c j)"), fmt)
 
-        def quant_g(c, lo, hi):
-            quantize(gq_codes[c][:, lo:hi], gq_scales[c][:, lo:hi], g_bf[c][:, lo:hi, :], E5M2)
-
-        def pick_row(target, j, first, start, stop):
-            cols = slice(j * P, (j + 1) * P)
-            nc.tensor.matmul_mx(
-                out=target[:],
-                lhsT=eye_codes[:, cols].bitcast(E4M3),
-                lhsT_scale=eye_scales[:, cols],
-                rhs=all_codes[:, first : first + T].bitcast(E5M2),
-                rhs_scale=all_scales[:, first : first + T],
-                start=start,
-                stop=stop,
-            )
-
-        row_values = {}
-
-        def dequant(c, h, shift, banks):
-            for j in range(PACK):
-                target = bank(banks[j], "row_values")
-                pick_row(target, j, origin[c] + shift, True, True)
-                row_values[c, j, h] = target[:, h * HALF - shift : (h + 1) * HALF - shift]
-
-        def subtract(c, j, h):
-            nc.vector.tensor_tensor(
-                out=r_rows[c][:, j, h * HALF : (h + 1) * HALF],
-                in0=g_rows(c, h * HALF, (h + 1) * HALF)[:, j, :],
-                in1=row_values[c, j, h],
-                op=mybir.AluOpType.subtract,
-            )
-
-        def gpsimd_pack_r(c, lo, hi):
-            nc.gpsimd.tensor_scalar(
-                out=r_packed(c, lo, hi),
-                in0=r_rows[c][:, :, lo:hi].rearrange("p j t -> p t j"),
-                scalar1=1.0,
-                scalar2=0.0,
-                op0=mybir.AluOpType.mult,
-                op1=mybir.AluOpType.add,
-            )
-
-        def r_packed(c, lo, hi):
-            if hi - lo == T:
-                return r_bf[c][:]
-            h = lo // HALF
-            return r_place[c, h][:, lo - h * HALF : hi - h * HALF, :]
-
-        def pack_r(copy, c, lo, hi):
-            pack(copy, r_packed(c, lo, hi), r_rows[c][:, :, lo:hi])
-
-        pair_values = {}
-
-        def dequant_pairs(c, first_bank):
-            for u in range(2):
-                pair_values[c, u] = bank(first_bank + u, "pair_values")
-            for e in (1, 0):
-                for u in range(2):
-                    pick_row(pair_values[c, u], 2 * u + e, origin[c] + (1 - e) * HALF, e == 1, e == 0)
-
-        def subtract_pair(c, u):
-            nc.vector.tensor_tensor(
-                out=r_pairs[c][:, u, :, :],
-                in0=g_rows(c, HALF, T)[:, 2 * u : 2 * u + 2, :].rearrange("p e t -> p t e"),
-                in1=pair_values[c, u][:].rearrange("p (e t) -> p t e", e=2),
-                op=mybir.AluOpType.subtract,
-            )
-
-        def pack_pairs(c, copy, word):
-            copy(
-                out=r_place[c, 1].rearrange("p t j -> p (t j)").bitcast(word).rearrange("p (t u) -> p t u", u=2),
-                in_=r_pairs[c][:].rearrange("p u t e -> p (u t e)").bitcast(word).rearrange("p (u t) -> p t u", u=2),
-            )
-
-        def quant_r(c, lo=0, hi=T):
-            quantize(gr_codes[c][:, lo:hi], gr_scales[c][:, lo:hi], r_packed(c, lo, hi), E4M3)
-
-        def cast_w(copy, c, n, count=1):
-            raw, first = w_loaded[c, n]
-            pack(copy, w_bf[c][:, n * P : (n + count) * P, :], raw[:, :, (n - first) * P : (n - first + count) * P])
-
-        def quant_w(c, n, count=1):
-            cols = slice(n * P, (n + count) * P)
-            quantize(w_codes[c][:, cols], w_scales[c][:, cols], w_bf[c][:, cols, :], E4M3)
-
-        first_tier = (gq_codes, gq_scales, E5M2)
-        second_tier = (gr_codes, gr_scales, E4M3)
-        acc = {}
-        columns_done = {}
-
-        def product(tier, c, n, lo=0, hi=T):
-            codes, scales, fmt = tier
-            if n not in acc:
-                acc[n] = bank(ACC_BANKS[n], "acc")
-                columns_done[n] = 0
-            cols = slice(n * P, (n + 1) * P)
-            nc.tensor.matmul_mx(
-                out=acc[n][:, lo:hi],
-                lhsT=w_codes[c][:, cols].bitcast(E4M3),
-                lhsT_scale=w_scales[c][:, cols],
-                rhs=codes[c][:, lo:hi].bitcast(fmt),
-                rhs_scale=scales[c][:, lo:hi],
-                start=columns_done[n] == 0,
-                stop=columns_done[n] + hi - lo == 2 * PASSES * T,
-            )
-            columns_done[n] = columns_done[n] + hi - lo
-
-        def compare(j):
+        def eye_group(j):
             shift = PACK - 1 - j
             nc.vector.tensor_scalar(
                 out=eye_bf[:, j * K_PASS : (j + 1) * K_PASS],
@@ -211,137 +96,208 @@ def tile_mix_tierg_none_kernel(tc, g, w, out):
             )
 
         def quant_eye(lo, hi):
-            nc.vector.quantize_mx(
-                out=eye_codes[:, lo * P : hi * P].bitcast(E4M3),
-                scales=eye_scales[:, lo * P : hi * P],
-                in_=eye_bf[:, lo * K_PASS : hi * K_PASS],
+            cols = slice(lo * P, hi * P)
+            quantize(eye_codes[:, cols], eye_scales[:, cols], eye_bf[:, lo * K_PASS : hi * K_PASS], E4M3)
+
+        def cast_g(copy, c, h, lo=0, hi=HALF):
+            pack(copy, g_bf[c][:, half_columns(h, lo, hi), :], g_raw[c, h][:, :, lo:hi])
+
+        def quant_g(c, h):
+            cols = half_columns(h)
+            quantize_packed(gq_codes[c][:, cols], gq_scales[c][:, cols], g_bf[c][:, cols, :], E5M2)
+
+        row_values = {}
+
+        def dequant(c, h, window, first_bank):
+            moving = slice(origin[c] + window, origin[c] + window + T)
+            for j in range(PACK):
+                target = bank(first_bank + j, "row_values")
+                nc.tensor.matmul_mx(
+                    out=target[:],
+                    lhsT=eye_codes[:, tile_columns(j)].bitcast(E4M3),
+                    lhsT_scale=eye_scales[:, tile_columns(j)],
+                    rhs=padded_codes[:, moving].bitcast(E5M2),
+                    rhs_scale=padded_scales[:, moving],
+                    start=True,
+                    stop=True,
+                )
+                row_values[c, h, j] = target[:, h * HALF - window : (h + 1) * HALF - window]
+
+        def subtract(c, h, rows):
+            for j in rows:
+                nc.vector.tensor_tensor(
+                    out=r_rows[c][:, j, half_columns(h)],
+                    in0=g_raw[c, h][:, j, :],
+                    in1=row_values[c, h, j],
+                    op=mybir.AluOpType.subtract,
+                )
+
+        def pack_r(copy, c, h, lo=0, hi=HALF):
+            pack(copy, r_bf[c, h][:, lo:hi, :], r_rows[c][:, :, half_columns(h, lo, hi)])
+
+        def gpsimd_pack_r(c, h):
+            hi = GPSIMD_COLUMNS[c, h]
+            nc.gpsimd.tensor_scalar(
+                out=r_bf[c, h][:, 0:hi, :],
+                in0=r_rows[c][:, :, half_columns(h, 0, hi)].rearrange("p j t -> p t j"),
+                scalar1=1.0,
+                scalar2=0.0,
+                op0=mybir.AluOpType.mult,
+                op1=mybir.AluOpType.add,
             )
 
-        unread = bank(BANKS - 1, "unread")
+        def quant_r(c, h):
+            cols = half_columns(h)
+            quantize_packed(gr_codes[c][:, cols], gr_scales[c][:, cols], r_bf[c, h], E4M3)
 
-        def warm_up(codes, scales):
+        def cast_w(copy, c, n, count=1):
+            side = n % PAIR
+            pack(copy, w_bf[c][:, tile_columns(n, count), :], w_raw[c][n // PAIR][:, :, tile_columns(side, count)])
+
+        def quant_w(c, n, count=1):
+            cols = tile_columns(n, count)
+            quantize_packed(w_codes[c][:, cols], w_scales[c][:, cols], w_bf[c][:, cols, :], E4M3)
+
+        first_tier = (gq_codes, gq_scales, E5M2)
+        second_tier = (gr_codes, gr_scales, E4M3)
+        acc = {}
+        columns_done = {}
+
+        def product(tier, c, n, cols=slice(0, T)):
+            codes, scales, fmt = tier
+            if n not in acc:
+                acc[n] = bank(n, "acc")
+                columns_done[n] = 0
+            width = cols.stop - cols.start
             nc.tensor.matmul_mx(
-                out=unread[:],
-                lhsT=codes.bitcast(E4M3),
-                lhsT_scale=scales,
-                rhs=all_codes[:, HALF : HALF + T].bitcast(E5M2),
-                rhs_scale=all_codes[:, HALF : HALF + T // 4].bitcast(U8),
-                start=True,
-                stop=True,
+                out=acc[n][:, cols],
+                lhsT=w_codes[c][:, tile_columns(n)].bitcast(E4M3),
+                lhsT_scale=w_scales[c][:, tile_columns(n)],
+                rhs=codes[c][:, cols].bitcast(fmt),
+                rhs_scale=scales[c][:, cols],
+                start=columns_done[n] == 0,
+                stop=columns_done[n] + width == 2 * PASSES * T,
             )
+            columns_done[n] = columns_done[n] + width
 
-        def both_tiers(c, n):
-            product(first_tier, c, n)
-            product(second_tier, c, n)
+        def both_tiers(c, *tile_numbers):
+            for n in tile_numbers:
+                product(first_tier, c, n)
+                product(second_tier, c, n)
 
-        def finish(copy, n, lo=0, hi=T):
-            copy(out=result[n][:, lo:hi], in_=acc[n][:, lo:hi])
-            nc.sync.dma_start(out=out[n * P : (n + 1) * P, lo:hi], in_=result[n][:, lo:hi])
+        def finish(copy, n, cols=slice(0, T)):
+            copy(out=result[n][:, cols], in_=acc[n][:, cols])
+            nc.sync.dma_start(out=out[tile_columns(n), cols], in_=result[n][:, cols])
 
-        load_g(0, 0, 256)
-        load_g(0, 256, 512)
-        load_g(1, 256, 512)
-        load_g(1, 0, 256)
-        load_w(0, 0, 2)
-        load_w(0, 2, 2)
-        load_w(0, 4, 2)
-        load_w(1, 0, 2)
-        load_w(1, 2, 2)
-        load_w(1, 4, 2)
-        load_w(0, 6, 2)
-        load_w(1, 6, 2)
-        nc.gpsimd.iota(ramp[:].bitcast(F32), [[1, (K_PASS + PACK) // 2]], base=0, channel_multiplier=-2, allow_small_or_imprecise_dtypes=True)
-        nc.vector.memset(all_codes[:, HALF : T + HALF], 0)
-        for repeat in range(2):
-            warm_up(all_codes[:, T : T + P], all_codes[:, T : T + P // 4].bitcast(U8))
-        compare(0)
-        compare(1)
+        for c, h in halves:
+            nc.sync.dma_start(out=g_raw[c, h][:], in_=pass_rows(g, c)[:, :, half_columns(h)])
+        last_pair = TILES // PAIR - 1
+        for pairs in (range(last_pair), range(last_pair, last_pair + 1)):
+            for c in range(PASSES):
+                for q in pairs:
+                    nc.sync.dma_start(out=w_raw[c][q][:], in_=pass_rows(w, c)[:, :, tile_columns(PAIR * q, PAIR)])
+
+        words = (K_PASS + PACK) // 2
+        nc.gpsimd.iota(ramp[:].bitcast(F32), [[1, words]], base=0, channel_multiplier=-2, allow_small_or_imprecise_dtypes=True)
+        zeros = padded_codes[:, HALF : HALF + T]
+        nc.vector.memset(zeros, 0)
+        unread = bank(TILES - 1, "unread")
+
+        def warm_ups(codes, scales):
+            for repeat in range(WARM_UPS):
+                nc.tensor.matmul_mx(
+                    out=unread[:],
+                    lhsT=codes.bitcast(E4M3),
+                    lhsT_scale=scales,
+                    rhs=zeros.bitcast(E5M2),
+                    rhs_scale=zeros[:, 0 : T // PACK].bitcast(U8),
+                    start=True,
+                    stop=True,
+                )
+
+        warm_ups(padded_codes[:, T : T + P], padded_codes[:, T : T + P // PACK].bitcast(U8))
+        eye_group(0)
+        eye_group(1)
         quant_eye(0, 2)
-        for repeat in range(2):
-            warm_up(eye_codes[:, 0:P], eye_scales[:, 0:P])
-        nc.vector.memset(all_scales[:, T : T + HALF].bitcast(U32), 0)
-        cast_g(scalar_copy, 0, G_SPLIT, HALF)
-        cast_g(vector_copy, 0, 0, G_SPLIT)
-        compare(2)
-        compare(3)
-        quant_g(0, 0, HALF)
+        warm_ups(eye_codes[:, tile_columns(0)], eye_scales[:, tile_columns(0)])
+        nc.vector.memset(padded_scales[:, pad].bitcast(U32), 0)
+
+        cast_g(scalar_copy, 0, 0, G_SPLIT, HALF)
+        cast_g(vector_copy, 0, 0, 0, G_SPLIT)
+        eye_group(2)
+        eye_group(3)
+        quant_g(0, 0)
         quant_eye(2, 4)
-        dequant(0, 0, -HALF, (0, 1, 2, 3))
-        cast_g(scalar_copy, 0, HALF + G_SPLIT, T)
-        cast_g(vector_copy, 0, HALF, HALF + G_SPLIT)
-        subtract(0, 0, 0)
-        quant_g(0, HALF, T)
-        for j in range(1, PACK):
-            subtract(0, j, 0)
-        dequant(0, 1, 0, (4, 5, 6, 7))
-        cast_g(scalar_copy, 1, HALF, T)
-        cast_g(scalar_copy, 1, 0, HALF)
-        gpsimd_pack_r(0, 0, 112)
-        for j in range(PACK):
-            subtract(0, j, 1)
-        quant_g(1, HALF, T)
-        dequant(1, 1, HALF, (0, 1, 2, 3))
-        pack_r(vector_copy, 0, 112, HALF)
-        quant_g(1, 0, HALF)
-        dequant(1, 0, 0, (4, 5, 6, 7))
-        quant_r(0, 0, HALF)
-        gpsimd_pack_r(0, HALF, HALF + 144)
-        for j in range(PACK):
-            subtract(1, j, 1)
-        cast_w(scalar_copy, 0, 0, 2)
-        quant_w(0, 0, 2)
-        product(first_tier, 0, 0)
-        product(first_tier, 0, 1)
-        product(second_tier, 0, 0, 0, HALF)
-        product(second_tier, 0, 1, 0, HALF)
-        pack_r(vector_copy, 0, HALF + 144, T)
-        subtract(1, 0, 0)
-        quant_r(0, HALF, T)
-        product(second_tier, 0, 0, HALF, T)
-        product(second_tier, 0, 1, HALF, T)
-        cast_w(scalar_copy, 0, 2, 2)
-        quant_w(0, 2, 2)
-        both_tiers(0, 2)
-        both_tiers(0, 3)
-        gpsimd_pack_r(1, HALF, HALF + 96)
-        for j in range(1, PACK):
-            subtract(1, j, 0)
-        cast_w(scalar_copy, 0, 4, 2)
-        quant_w(0, 4, 2)
-        both_tiers(0, 4)
-        both_tiers(0, 5)
-        cast_w(scalar_copy, 1, 0, 2)
-        pack_r(scalar_copy, 1, T - 96, T)
-        pack_r(vector_copy, 1, HALF + 96, T - 96)
-        pack_r(vector_copy, 1, 0, HALF - 0)
-        quant_w(1, 0, 2)
-        product(first_tier, 1, 0)
-        product(first_tier, 1, 1)
-        quant_r(1, HALF, T)
-        product(second_tier, 1, 0, HALF, T)
-        quant_r(1, 0, HALF)
-        product(second_tier, 1, 0, 0, HALF)
+        dequant(0, 0, window=-HALF, first_bank=0)
+        cast_g(scalar_copy, 0, 1, G_SPLIT, HALF)
+        cast_g(vector_copy, 0, 1, 0, G_SPLIT)
+        subtract(0, 0, range(1))
+        quant_g(0, 1)
+        subtract(0, 0, range(1, PACK))
+        dequant(0, 1, window=0, first_bank=PACK)
+
+        cast_g(scalar_copy, 1, 1)
+        cast_g(scalar_copy, 1, 0)
+        gpsimd_pack_r(0, 0)
+        subtract(0, 1, range(PACK))
+        quant_g(1, 1)
+        dequant(1, 1, window=HALF, first_bank=0)
+        pack_r(vector_copy, 0, 0, GPSIMD_COLUMNS[0, 0], HALF)
+        quant_g(1, 0)
+        dequant(1, 0, window=0, first_bank=PACK)
+        quant_r(0, 0)
+        gpsimd_pack_r(0, 1)
+        subtract(1, 1, range(PACK))
+
+        cast_w(scalar_copy, 0, 0, PAIR)
+        quant_w(0, 0, PAIR)
+        for n in range(PAIR):
+            product(first_tier, 0, n)
+        for n in range(PAIR):
+            product(second_tier, 0, n, half_columns(0))
+        pack_r(vector_copy, 0, 1, GPSIMD_COLUMNS[0, 1], HALF)
+        subtract(1, 0, range(1))
+        quant_r(0, 1)
+        for n in range(PAIR):
+            product(second_tier, 0, n, half_columns(1))
+        cast_w(scalar_copy, 0, 2, PAIR)
+        quant_w(0, 2, PAIR)
+        both_tiers(0, 2, 3)
+        gpsimd_pack_r(1, 1)
+        subtract(1, 0, range(1, PACK))
+        cast_w(scalar_copy, 0, 4, PAIR)
+        quant_w(0, 4, PAIR)
+        both_tiers(0, 4, 5)
+
+        cast_w(scalar_copy, 1, 0, PAIR)
+        pack_r(scalar_copy, 1, 1, GPSIMD_COLUMNS[1, 1], HALF)
+        pack_r(vector_copy, 1, 0)
+        quant_w(1, 0, PAIR)
+        for n in range(PAIR):
+            product(first_tier, 1, n)
+        for h in (1, 0):
+            quant_r(1, h)
+            product(second_tier, 1, 0, half_columns(h))
         product(second_tier, 1, 1)
-        cast_w(scalar_copy, 1, 2)
-        quant_w(1, 2)
-        both_tiers(1, 2)
-        cast_w(scalar_copy, 1, 3)
-        quant_w(1, 3)
-        both_tiers(1, 3)
+        for n in (2, 3):
+            cast_w(scalar_copy, 1, n)
+            quant_w(1, n)
+            both_tiers(1, n)
+
         cast_w(scalar_copy, 1, 5)
         cast_w(vector_copy, 1, 4)
-        finish(scalar_copy, 0, 0, HALF)
-        finish(scalar_copy, 0, HALF, T)
+        for h in range(2):
+            finish(scalar_copy, 0, half_columns(h))
         finish(scalar_copy, 1)
         cast_w(vector_copy, 0, 6)
-        quant_w(1, 4, 2)
-        both_tiers(1, 4)
-        both_tiers(1, 5)
+        quant_w(1, 4, PAIR)
+        both_tiers(1, 4, 5)
         cast_w(vector_copy, 0, 7)
         finish(scalar_copy, 2)
         finish(scalar_copy, 3)
+
         cast_w(vector_copy, 1, 6)
-        quant_w(0, 6, 2)
+        quant_w(0, 6, PAIR)
         both_tiers(0, 6)
         quant_w(1, 6)
         cast_w(vector_copy, 1, 7)
@@ -352,5 +308,5 @@ def tile_mix_tierg_none_kernel(tc, g, w, out):
         finish(scalar_copy, 4)
         finish(scalar_copy, 5)
         finish(vector_copy, 6)
-        finish(scalar_copy, 7, 0, HALF)
-        finish(scalar_copy, 7, HALF, T)
+        for h in range(2):
+            finish(scalar_copy, 7, half_columns(h))

@@ -22,7 +22,8 @@ PAIR = 2
 RUN = 4
 WARM_UPS = 2
 G_SPLIT = 160
-GPSIMD_COLUMNS = {(0, 0): 144, (0, 1): 176, (1, 1): 128}
+GPSIMD_COLUMNS = {(0, 0): 112, (0, 1): 144, (1, 1): 96}
+SCALAR_COLUMNS = 96
 
 
 def tile_mix_tierg_none_kernel(tc, g, w, out):
@@ -270,7 +271,8 @@ def tile_mix_tierg_none_kernel(tc, g, w, out):
         both_tiers(0, 4, 5)
 
         cast_w(scalar_copy, 1, 0, PAIR)
-        pack_r(scalar_copy, 1, 1, GPSIMD_COLUMNS[1, 1], HALF)
+        pack_r(scalar_copy, 1, 1, HALF - SCALAR_COLUMNS, HALF)
+        pack_r(vector_copy, 1, 1, GPSIMD_COLUMNS[1, 1], HALF - SCALAR_COLUMNS)
         pack_r(vector_copy, 1, 0)
         quant_w(1, 0, PAIR)
         for n in range(PAIR):

@@ -20,10 +20,12 @@ HALF = T // 2
 TILES = N // P
 PAIR = 2
 RUN = 4
+MX_ALIGN = 64
+DMA_ALIGN = 256
 WARM_UPS = 2
 G_SPLIT = 160
-GPSIMD_COLUMNS = {(0, 0): 112, (0, 1): 144, (1, 1): 96}
-SCALAR_COLUMNS = 96
+GPSIMD_COLUMNS = {(0, 0): 128, (0, 1): 160, (1, 1): 128}
+SCALAR_COLUMNS = 64
 
 
 def tile_mix_tierg_none_kernel(tc, g, w, out):
@@ -35,14 +37,13 @@ def tile_mix_tierg_none_kernel(tc, g, w, out):
         ps = ctx.enter_context(tc.psum_pool(name="ps", bufs=1))
         ctx.enter_context(tc.manual_schedule())
 
-        def tile(label, shape, dtype):
-            return sb.tile(shape, dtype, name=label, align_bytes=64)
+        def tile(label, shape, dtype, align=MX_ALIGN):
+            return sb.tile(shape, dtype, name=label, align_bytes=align)
 
-        def tiles(label, count, shape, dtype):
-            return [tile(label + str(i), shape, dtype) for i in range(count)]
+        def tiles(label, count, shape, dtype, align=MX_ALIGN):
+            return [tile(label + str(i), shape, dtype, align) for i in range(count)]
 
         halves = ((0, 0), (0, 1), (1, 1), (1, 0))
-        g_raw = {(c, h): tile("g_raw" + str(2 * c + h), [P, PACK, HALF], F32) for c, h in halves}
         g_bf = tiles("g_bf", PASSES, [P, T, PACK], BF16)
         padded_codes = tile("gq_codes", [P, 2 * T + HALF], U32)
         padded_scales = tile("gq_scales", [P, 2 * T + HALF], U8)
@@ -51,19 +52,20 @@ def tile_mix_tierg_none_kernel(tc, g, w, out):
         gq_codes = [padded_codes[:, origin[c] : origin[c] + T] for c in range(PASSES)]
         gq_scales = [padded_scales[:, origin[c] : origin[c] + T] for c in range(PASSES)]
         r_rows = tiles("r_rows", PASSES, [P, PACK, T], BF16)
+        eye_codes = tile("eye_codes", [P, K_PASS], U32)
+        eye_scales = tile("eye_scales", [P, K_PASS], U8)
         r_own = tiles("r_bf", PASSES, [P, HALF, PACK], BF16)
         r_bf = {(0, 0): r_own[0][:], (0, 1): g_bf[1][:, 0:HALF, :], (1, 1): g_bf[1][:, 0:HALF, :], (1, 0): r_own[1][:]}
         gr_codes = tiles("gr_codes", PASSES, [P, T], U32)
         gr_scales = tiles("gr_scales", PASSES, [P, T], U8)
-        w_raw = [tiles("w_raw" + str(c), TILES // PAIR, [P, PACK, PAIR * P], F32) for c in range(PASSES)]
         w_bf = tiles("w_bf", PASSES, [P, N, PACK], BF16)
         w_codes = tiles("w_codes", PASSES, [P, N], U32)
         w_scales = tiles("w_scales", PASSES, [P, N], U8)
-        result = tiles("result", TILES, [P, T], F32)
         ramp = tile("ramp", [P, K_PASS + PACK], BF16)
         eye_bf = tile("eye_bf", [P, PACK * K_PASS], BF16)
-        eye_codes = tile("eye_codes", [P, K_PASS], U32)
-        eye_scales = tile("eye_scales", [P, K_PASS], U8)
+        g_raw = {(c, h): tile("g_raw" + str(2 * c + h), [P, PACK, HALF], F32, DMA_ALIGN) for c, h in halves}
+        w_raw = [tiles("w_raw" + str(c), TILES // PAIR, [P, PACK, PAIR * P], F32, DMA_ALIGN) for c in range(PASSES)]
+        result = tiles("result", TILES, [P, T], F32, DMA_ALIGN)
 
         def bank(b, label):
             return ps.tile([P, T], F32, name=label, tag="bank" + str(b))

@@ -20,7 +20,7 @@ HALF = T // 2
 TILES = N // P
 PAIR = 2
 RUN = 4
-MX_ALIGN = 64
+MX_ALIGN = 256
 DMA_ALIGN = 256
 WARM_UPS = 2
 G_SPLIT = 160

@@ -8,6 +8,7 @@ FLOPS = 2 * 2 * K * N * T
 F32 = mybir.dt.float32
 BF16 = mybir.dt.bfloat16
 U32 = mybir.dt.uint32
+I32 = mybir.dt.int32
 U8 = mybir.dt.uint8
 E4M3 = mybir.dt.float8_e4m3fn_x4
 E5M2 = mybir.dt.float8_e5m2_x4
@@ -24,8 +25,6 @@ MX_ALIGN = 256
 DMA_ALIGN = 256
 WARM_UPS = 2
 G_SPLIT = 160
-GPSIMD_COLUMNS = {(0, 0): 128, (0, 1): 160, (1, 1): 128}
-SCALAR_COLUMNS = 64
 
 
 def tile_mix_tierg_none_kernel(tc, g, w, out):
@@ -43,24 +42,25 @@ def tile_mix_tierg_none_kernel(tc, g, w, out):
         def tiles(label, count, shape, dtype, align=MX_ALIGN):
             return [tile(label + str(i), shape, dtype, align) for i in range(count)]
 
-        halves = ((0, 0), (0, 1), (1, 1), (1, 0))
+        halves = ((0, 0), (0, 1), (1, 0), (1, 1))
         g_bf = tiles("g_bf", PASSES, [P, T, PACK], BF16)
-        padded_codes = tile("gq_codes", [P, 2 * T + HALF], U32)
-        padded_scales = tile("gq_scales", [P, 2 * T + HALF], U8)
-        pad = slice(T, T + HALF)
-        origin = (T + HALF, 0)
+        padded_codes = tile("gq_codes", [P, 7 * HALF], U32)
+        padded_scales = tile("gq_scales", [P, 7 * HALF], U8)
+        origin = (5 * HALF, 2 * HALF)
+        waiting = slice(HALF, 2 * HALF)
         gq_codes = [padded_codes[:, origin[c] : origin[c] + T] for c in range(PASSES)]
         gq_scales = [padded_scales[:, origin[c] : origin[c] + T] for c in range(PASSES)]
-        r_rows = tiles("r_rows", PASSES, [P, PACK, T], BF16)
+        r_rows = tile("r_rows", [P, PACK, T], BF16)
+        r_pairs = tiles("r_pairs", 2, [P, 2, HALF, 2], BF16)
         eye_codes = tile("eye_codes", [P, K_PASS], U32)
         eye_scales = tile("eye_scales", [P, K_PASS], U8)
         r_own = tiles("r_bf", PASSES, [P, HALF, PACK], BF16)
-        r_bf = {(0, 0): r_own[0][:], (0, 1): g_bf[1][:, 0:HALF, :], (1, 1): g_bf[1][:, 0:HALF, :], (1, 0): r_own[1][:]}
         gr_codes = tiles("gr_codes", PASSES, [P, T], U32)
         gr_scales = tiles("gr_scales", PASSES, [P, T], U8)
         w_bf = tiles("w_bf", PASSES, [P, N, PACK], BF16)
         w_codes = tiles("w_codes", PASSES, [P, N], U32)
         w_scales = tiles("w_scales", PASSES, [P, N], U8)
+        r_bf = {(0, 0): r_own[0][:], (0, 1): g_bf[1][:, HALF:T, :], (1, 0): w_bf[0][:, HALF:T, :], (1, 1): r_own[1][:]}
         ramp = tile("ramp", [P, K_PASS + PACK], BF16)
         eye_bf = tile("eye_bf", [P, PACK * K_PASS], BF16)
         g_raw = {(c, h): tile("g_raw" + str(2 * c + h), [P, PACK, HALF], F32, DMA_ALIGN) for c, h in halves}
@@ -107,7 +107,13 @@ def tile_mix_tierg_none_kernel(tc, g, w, out):
 
         def quant_g(c, h):
             cols = half_columns(h)
-            quantize_packed(gq_codes[c][:, cols], gq_scales[c][:, cols], g_bf[c][:, cols, :], E5M2)
+            place = waiting if (c, h) == (1, 0) else slice(origin[c] + cols.start, origin[c] + cols.stop)
+            quantize_packed(padded_codes[:, place], padded_scales[:, place], g_bf[c][:, cols, :], E5M2)
+
+        def move_to_its_pass():
+            place = slice(origin[1], origin[1] + HALF)
+            vector_copy(out=padded_codes[:, place].bitcast(I32), in_=padded_codes[:, waiting].bitcast(I32))
+            vector_copy(out=padded_scales[:, place].bitcast(I32), in_=padded_scales[:, waiting].bitcast(I32))
 
         row_values = {}
 
@@ -126,23 +132,69 @@ def tile_mix_tierg_none_kernel(tc, g, w, out):
                 )
                 row_values[c, h, j] = target[:, h * HALF - window : (h + 1) * HALF - window]
 
+        def dequant_pairs(h, at, first_bank):
+            for u in range(2):
+                target = bank(first_bank + u, "row_values")
+                for side in range(2):
+                    moving = slice(at - side * HALF, at - side * HALF + T)
+                    nc.tensor.matmul_mx(
+                        out=target[:],
+                        lhsT=eye_codes[:, tile_columns(2 * u + side)].bitcast(E4M3),
+                        lhsT_scale=eye_scales[:, tile_columns(2 * u + side)],
+                        rhs=padded_codes[:, moving].bitcast(E5M2),
+                        rhs_scale=padded_scales[:, moving],
+                        start=side == 0,
+                        stop=side == 1,
+                    )
+                row_values[1, h, u] = target[:].rearrange("p (j t) -> p t j", j=2)
+
+        def subtract_pairs(h, pairs):
+            for u in pairs:
+                nc.vector.tensor_tensor(
+                    out=r_pairs[h][:, u, :, :],
+                    in0=g_raw[1, h][:, 2 * u : 2 * u + 2, :].rearrange("p j t -> p t j"),
+                    in1=row_values[1, h, u],
+                    op=mybir.AluOpType.subtract,
+                )
+
+        def pairs_views(h, lo, hi):
+            dst = r_bf[1, h][:, lo:hi, :].rearrange("p t (u j) -> p t u j", u=2)
+            return dst, r_pairs[h][:, :, lo:hi, :].rearrange("p u t j -> p t u j")
+
+        def pack_pairs(copy, h, lo=0, hi=HALF):
+            dst, src = pairs_views(h, lo, hi)
+            copy(out=dst, in_=src)
+
         def subtract(c, h, rows):
             for j in rows:
                 nc.vector.tensor_tensor(
-                    out=r_rows[c][:, j, half_columns(h)],
+                    out=r_rows[:, j, half_columns(h)],
                     in0=g_raw[c, h][:, j, :],
                     in1=row_values[c, h, j],
                     op=mybir.AluOpType.subtract,
                 )
 
         def pack_r(copy, c, h, lo=0, hi=HALF):
-            pack(copy, r_bf[c, h][:, lo:hi, :], r_rows[c][:, :, half_columns(h, lo, hi)])
+            pack(copy, r_bf[c, h][:, lo:hi, :], r_rows[:, :, half_columns(h, lo, hi)])
 
-        def gpsimd_pack_r(c, h):
-            hi = GPSIMD_COLUMNS[c, h]
+        def gpsimd_pack_r(c, h, lo, hi):
+            if c == 0:
+                dst, src = r_bf[c, h][:, lo:hi, :], r_rows[:, :, half_columns(h, lo, hi)].rearrange("p j t -> p t j")
+            else:
+                dst, src = pairs_views(h, lo, hi)
             nc.gpsimd.tensor_scalar(
-                out=r_bf[c, h][:, 0:hi, :],
-                in0=r_rows[c][:, :, half_columns(h, 0, hi)].rearrange("p j t -> p t j"),
+                out=dst,
+                in0=src,
+                scalar1=1.0,
+                scalar2=0.0,
+                op0=mybir.AluOpType.mult,
+                op1=mybir.AluOpType.add,
+            )
+
+        def gpsimd_cast_g(c, h, lo, hi):
+            nc.gpsimd.tensor_scalar(
+                out=g_bf[c][:, half_columns(h, lo, hi), :],
+                in0=g_raw[c, h][:, :, lo:hi].rearrange("p j t -> p t j"),
                 scalar1=1.0,
                 scalar2=0.0,
                 op0=mybir.AluOpType.mult,
@@ -169,7 +221,7 @@ def tile_mix_tierg_none_kernel(tc, g, w, out):
         def product(tier, c, n, cols=slice(0, T)):
             codes, scales, fmt = tier
             if n not in acc:
-                acc[n] = bank(n, "acc")
+                acc[n] = bank((n + PACK) % TILES, "acc")
                 columns_done[n] = 0
             width = cols.stop - cols.start
             nc.tensor.matmul_mx(
@@ -202,8 +254,8 @@ def tile_mix_tierg_none_kernel(tc, g, w, out):
 
         words = (K_PASS + PACK) // 2
         nc.gpsimd.iota(ramp[:].bitcast(F32), [[1, words]], base=0, channel_multiplier=-2, allow_small_or_imprecise_dtypes=True)
-        zeros = padded_codes[:, HALF : HALF + T]
-        nc.vector.memset(zeros, 0)
+        zeros = padded_codes[:, 3 * HALF : 3 * HALF + T]
+        nc.vector.memset(padded_codes[:, 2 * HALF : 5 * HALF], 0)
         unread = bank(TILES - 1, "unread")
 
         def warm_ups(codes, scales):
@@ -218,73 +270,79 @@ def tile_mix_tierg_none_kernel(tc, g, w, out):
                     stop=True,
                 )
 
-        warm_ups(padded_codes[:, T : T + P], padded_codes[:, T : T + P // PACK].bitcast(U8))
+        warm_ups(zeros[:, 0:P], zeros[:, 0 : P // PACK].bitcast(U8))
         eye_group(0)
         eye_group(1)
+        nc.vector.memset(padded_scales[:, 0 : 5 * HALF].bitcast(U32), 0)
         quant_eye(0, 2)
         warm_ups(eye_codes[:, tile_columns(0)], eye_scales[:, tile_columns(0)])
-        nc.vector.memset(padded_scales[:, pad].bitcast(U32), 0)
+        nc.vector.memset(padded_codes[:, 0:HALF], 0)
 
-        cast_g(scalar_copy, 0, 0, G_SPLIT, HALF)
-        cast_g(vector_copy, 0, 0, 0, G_SPLIT)
         eye_group(2)
         eye_group(3)
-        quant_g(0, 0)
+        cast_g(scalar_copy, 0, 0, G_SPLIT, HALF)
+        cast_g(vector_copy, 0, 0, 0, G_SPLIT)
         quant_eye(2, 4)
+        quant_g(0, 0)
         dequant(0, 0, window=-HALF, first_bank=0)
         cast_g(scalar_copy, 0, 1, G_SPLIT, HALF)
         cast_g(vector_copy, 0, 1, 0, G_SPLIT)
-        subtract(0, 0, range(1))
+        subtract(0, 0, range(0))
         quant_g(0, 1)
-        subtract(0, 0, range(1, PACK))
         dequant(0, 1, window=0, first_bank=PACK)
-
-        cast_g(scalar_copy, 1, 1)
-        cast_g(scalar_copy, 1, 0)
-        gpsimd_pack_r(0, 0)
-        subtract(0, 1, range(PACK))
-        quant_g(1, 1)
-        dequant(1, 1, window=HALF, first_bank=0)
-        pack_r(vector_copy, 0, 0, GPSIMD_COLUMNS[0, 0], HALF)
+        gpsimd_cast_g(1, 0, 0, 96)
+        cast_g(scalar_copy, 1, 0, 96, HALF)
+        subtract(0, 0, range(0, PACK))
         quant_g(1, 0)
-        dequant(1, 0, window=0, first_bank=PACK)
+        dequant_pairs(0, at=HALF, first_bank=0)
+        cast_g(scalar_copy, 1, 1)
+        gpsimd_pack_r(0, 0, 0, 192)
+        subtract(0, 1, range(PACK))
+        pack_r(vector_copy, 0, 0, 192, HALF)
+        quant_g(1, 1)
+        dequant_pairs(1, at=origin[1] + HALF, first_bank=2)
         quant_r(0, 0)
-        gpsimd_pack_r(0, 1)
-        subtract(1, 1, range(PACK))
-
+        gpsimd_pack_r(0, 1, 0, 128)
+        gpsimd_pack_r(0, 1, 128, 256)
+        subtract_pairs(0, range(1))
         cast_w(scalar_copy, 0, 0, PAIR)
         quant_w(0, 0, PAIR)
         for n in range(PAIR):
             product(first_tier, 0, n)
         for n in range(PAIR):
             product(second_tier, 0, n, half_columns(0))
-        pack_r(vector_copy, 0, 1, GPSIMD_COLUMNS[0, 1], HALF)
-        subtract(1, 0, range(1))
+        subtract_pairs(0, range(1, 2))
+        cast_w(scalar_copy, 0, 2, PAIR)
+        quant_w(0, 2, PAIR)
+        for n in (2, 3):
+            product(first_tier, 0, n)
         quant_r(0, 1)
         for n in range(PAIR):
             product(second_tier, 0, n, half_columns(1))
-        cast_w(scalar_copy, 0, 2, PAIR)
-        quant_w(0, 2, PAIR)
-        both_tiers(0, 2, 3)
-        gpsimd_pack_r(1, 1)
-        subtract(1, 0, range(1, PACK))
+        for n in (2, 3):
+            product(second_tier, 0, n)
+        gpsimd_pack_r(1, 0, 0, 112)
+        gpsimd_pack_r(1, 0, 112, 208)
+        subtract_pairs(1, range(1))
         cast_w(scalar_copy, 0, 4, PAIR)
         quant_w(0, 4, PAIR)
         both_tiers(0, 4, 5)
-
+        subtract_pairs(1, range(1, 2))
         cast_w(scalar_copy, 1, 0, PAIR)
-        pack_r(scalar_copy, 1, 1, HALF - SCALAR_COLUMNS, HALF)
-        pack_r(vector_copy, 1, 1, GPSIMD_COLUMNS[1, 1], HALF - SCALAR_COLUMNS)
-        pack_r(vector_copy, 1, 0)
+        pack_pairs(scalar_copy, 0, 208, HALF)
+        cast_w(scalar_copy, 1, 2)
+        pack_pairs(scalar_copy, 1, HALF - 96, HALF)
+        cast_w(scalar_copy, 1, 3)
+        move_to_its_pass()
         quant_w(1, 0, PAIR)
+        pack_pairs(vector_copy, 1, 0, HALF - 96)
         for n in range(PAIR):
             product(first_tier, 1, n)
-        for h in (1, 0):
+        for h in (0, 1):
             quant_r(1, h)
             product(second_tier, 1, 0, half_columns(h))
         product(second_tier, 1, 1)
         for n in (2, 3):
-            cast_w(scalar_copy, 1, n)
             quant_w(1, n)
             both_tiers(1, n)
 

@@ -21,10 +21,16 @@ HALF = T // 2
 TILES = N // P
 PAIR = 2
 RUN = 4
-MX_ALIGN = 256
-DMA_ALIGN = 256
+ALIGN = 256
+PLACES = 7
+WAITING = HALF
+ORIGIN = (5 * HALF, 2 * HALF)
 WARM_UPS = 2
 G_SPLIT = 160
+GPSIMD_CAST = 96
+GPSIMD_FIRST = 192
+GPSIMD_LAST = 104
+SCALAR_COLUMNS = 96
 
 
 def tile_mix_tierg_none_kernel(tc, g, w, out):
@@ -36,20 +42,18 @@ def tile_mix_tierg_none_kernel(tc, g, w, out):
         ps = ctx.enter_context(tc.psum_pool(name="ps", bufs=1))
         ctx.enter_context(tc.manual_schedule())
 
-        def tile(label, shape, dtype, align=MX_ALIGN):
-            return sb.tile(shape, dtype, name=label, align_bytes=align)
+        def tile(label, shape, dtype):
+            return sb.tile(shape, dtype, name=label, align_bytes=ALIGN)
 
-        def tiles(label, count, shape, dtype, align=MX_ALIGN):
-            return [tile(label + str(i), shape, dtype, align) for i in range(count)]
+        def tiles(label, count, shape, dtype):
+            return [tile(label + str(i), shape, dtype) for i in range(count)]
 
         halves = ((0, 0), (0, 1), (1, 0), (1, 1))
         g_bf = tiles("g_bf", PASSES, [P, T, PACK], BF16)
-        padded_codes = tile("gq_codes", [P, 7 * HALF], U32)
-        padded_scales = tile("gq_scales", [P, 7 * HALF], U8)
-        origin = (5 * HALF, 2 * HALF)
-        waiting = slice(HALF, 2 * HALF)
-        gq_codes = [padded_codes[:, origin[c] : origin[c] + T] for c in range(PASSES)]
-        gq_scales = [padded_scales[:, origin[c] : origin[c] + T] for c in range(PASSES)]
+        padded_codes = tile("gq_codes", [P, PLACES * HALF], U32)
+        padded_scales = tile("gq_scales", [P, PLACES * HALF], U8)
+        gq_codes = [padded_codes[:, ORIGIN[c] : ORIGIN[c] + T] for c in range(PASSES)]
+        gq_scales = [padded_scales[:, ORIGIN[c] : ORIGIN[c] + T] for c in range(PASSES)]
         r_rows = tile("r_rows", [P, PACK, T], BF16)
         r_pairs = tiles("r_pairs", 2, [P, 2, HALF, 2], BF16)
         eye_codes = tile("eye_codes", [P, K_PASS], U32)
@@ -63,9 +67,9 @@ def tile_mix_tierg_none_kernel(tc, g, w, out):
         r_bf = {(0, 0): r_own[0][:], (0, 1): g_bf[1][:, HALF:T, :], (1, 0): w_bf[0][:, HALF:T, :], (1, 1): r_own[1][:]}
         ramp = tile("ramp", [P, K_PASS + PACK], BF16)
         eye_bf = tile("eye_bf", [P, PACK * K_PASS], BF16)
-        g_raw = {(c, h): tile("g_raw" + str(2 * c + h), [P, PACK, HALF], F32, DMA_ALIGN) for c, h in halves}
-        w_raw = [tiles("w_raw" + str(c), TILES // PAIR, [P, PACK, PAIR * P], F32, DMA_ALIGN) for c in range(PASSES)]
-        result = tiles("result", TILES, [P, T], F32, DMA_ALIGN)
+        g_raw = {(c, h): tile("g_raw" + str(2 * c + h), [P, PACK, HALF], F32) for c, h in halves}
+        w_raw = [tiles("w_raw" + str(c), TILES // PAIR, [P, PACK, PAIR * P], F32) for c in range(PASSES)]
+        result = tiles("result", TILES, [P, T], F32)
 
         def bank(b, label):
             return ps.tile([P, T], F32, name=label, tag="bank" + str(b))
@@ -105,100 +109,64 @@ def tile_mix_tierg_none_kernel(tc, g, w, out):
         def cast_g(copy, c, h, lo=0, hi=HALF):
             pack(copy, g_bf[c][:, half_columns(h, lo, hi), :], g_raw[c, h][:, :, lo:hi])
 
-        def quant_g(c, h):
+        def quant_g(c, h, first_word):
             cols = half_columns(h)
-            place = waiting if (c, h) == (1, 0) else slice(origin[c] + cols.start, origin[c] + cols.stop)
-            quantize_packed(padded_codes[:, place], padded_scales[:, place], g_bf[c][:, cols, :], E5M2)
+            quantize_packed(padded_codes[:, first_word : first_word + HALF], gq_scales[c][:, cols], g_bf[c][:, cols, :], E5M2)
 
-        def move_to_its_pass():
-            place = slice(origin[1], origin[1] + HALF)
-            vector_copy(out=padded_codes[:, place].bitcast(I32), in_=padded_codes[:, waiting].bitcast(I32))
-            vector_copy(out=padded_scales[:, place].bitcast(I32), in_=padded_scales[:, waiting].bitcast(I32))
+        def leave_waiting_place():
+            vector_copy(out=gq_codes[1][:, half_columns(0)].bitcast(I32), in_=padded_codes[:, WAITING : WAITING + HALF].bitcast(I32))
 
         row_values = {}
 
-        def dequant(c, h, window, first_bank):
-            moving = slice(origin[c] + window, origin[c] + window + T)
-            for j in range(PACK):
-                target = bank(first_bank + j, "row_values")
-                nc.tensor.matmul_mx(
-                    out=target[:],
-                    lhsT=eye_codes[:, tile_columns(j)].bitcast(E4M3),
-                    lhsT_scale=eye_scales[:, tile_columns(j)],
-                    rhs=padded_codes[:, moving].bitcast(E5M2),
-                    rhs_scale=padded_scales[:, moving],
-                    start=True,
-                    stop=True,
-                )
-                row_values[c, h, j] = target[:, h * HALF - window : (h + 1) * HALF - window]
-
-        def dequant_pairs(h, at, first_bank):
-            for u in range(2):
-                target = bank(first_bank + u, "row_values")
-                for side in range(2):
-                    moving = slice(at - side * HALF, at - side * HALF + T)
-                    nc.tensor.matmul_mx(
-                        out=target[:],
-                        lhsT=eye_codes[:, tile_columns(2 * u + side)].bitcast(E4M3),
-                        lhsT_scale=eye_scales[:, tile_columns(2 * u + side)],
-                        rhs=padded_codes[:, moving].bitcast(E5M2),
-                        rhs_scale=padded_scales[:, moving],
-                        start=side == 0,
-                        stop=side == 1,
-                    )
-                row_values[1, h, u] = target[:].rearrange("p (j t) -> p t j", j=2)
-
-        def subtract_pairs(h, pairs):
-            for u in pairs:
-                nc.vector.tensor_tensor(
-                    out=r_pairs[h][:, u, :, :],
-                    in0=g_raw[1, h][:, 2 * u : 2 * u + 2, :].rearrange("p j t -> p t j"),
-                    in1=row_values[1, h, u],
-                    op=mybir.AluOpType.subtract,
-                )
-
-        def pairs_views(h, lo, hi):
-            dst = r_bf[1, h][:, lo:hi, :].rearrange("p t (u j) -> p t u j", u=2)
-            return dst, r_pairs[h][:, :, lo:hi, :].rearrange("p u t j -> p t u j")
-
-        def pack_pairs(copy, h, lo=0, hi=HALF):
-            dst, src = pairs_views(h, lo, hi)
-            copy(out=dst, in_=src)
-
-        def subtract(c, h, rows):
-            for j in rows:
-                nc.vector.tensor_tensor(
-                    out=r_rows[:, j, half_columns(h)],
-                    in0=g_raw[c, h][:, j, :],
-                    in1=row_values[c, h, j],
-                    op=mybir.AluOpType.subtract,
-                )
-
-        def pack_r(copy, c, h, lo=0, hi=HALF):
-            pack(copy, r_bf[c, h][:, lo:hi, :], r_rows[:, :, half_columns(h, lo, hi)])
-
-        def gpsimd_pack_r(c, h, lo, hi):
-            if c == 0:
-                dst, src = r_bf[c, h][:, lo:hi, :], r_rows[:, :, half_columns(h, lo, hi)].rearrange("p j t -> p t j")
-            else:
-                dst, src = pairs_views(h, lo, hi)
-            nc.gpsimd.tensor_scalar(
-                out=dst,
-                in0=src,
-                scalar1=1.0,
-                scalar2=0.0,
-                op0=mybir.AluOpType.mult,
-                op1=mybir.AluOpType.add,
+        def dequant_row(target, j, first_word, first_scale, start, stop):
+            nc.tensor.matmul_mx(
+                out=target[:],
+                lhsT=eye_codes[:, tile_columns(j)].bitcast(E4M3),
+                lhsT_scale=eye_scales[:, tile_columns(j)],
+                rhs=padded_codes[:, first_word : first_word + T].bitcast(E5M2),
+                rhs_scale=padded_scales[:, first_scale : first_scale + T],
+                start=start,
+                stop=stop,
             )
 
-        def gpsimd_cast_g(c, h, lo, hi):
-            nc.gpsimd.tensor_scalar(
-                out=g_bf[c][:, half_columns(h, lo, hi), :],
-                in0=g_raw[c, h][:, :, lo:hi].rearrange("p j t -> p t j"),
-                scalar1=1.0,
-                scalar2=0.0,
-                op0=mybir.AluOpType.mult,
-                op1=mybir.AluOpType.add,
+        def dequant_rows(h, first_bank):
+            window = ORIGIN[0] + (h - 1) * HALF
+            for j in range(PACK):
+                target = bank(first_bank + j, "row_values")
+                dequant_row(target, j, window, window, True, True)
+                row_values[0, h, j] = target[:, half_columns(1)]
+
+        def dequant_pairs(h, first_word, first_bank, order):
+            targets = [bank(first_bank + u, "row_values") for u in range(2)]
+            for u, i in order:
+                dequant_row(targets[u], 2 * u + i, first_word - i * HALF, ORIGIN[1] + (h - i) * HALF, i == 0, i == 1)
+            for u in range(2):
+                row_values[1, h, u] = targets[u][:].rearrange("p (i t) -> p t i", i=2)
+
+        def subtract(dst, g_values, gq_values):
+            nc.vector.tensor_tensor(out=dst, in0=g_values, in1=gq_values, op=mybir.AluOpType.subtract)
+
+        def subtract_rows(h):
+            for j in range(PACK):
+                subtract(r_rows[:, j, half_columns(h)], g_raw[0, h][:, j, :], row_values[0, h, j])
+
+        def subtract_pair(h, u):
+            two_rows = g_raw[1, h][:, 2 * u : 2 * u + 2, :].rearrange("p i t -> p t i")
+            subtract(r_pairs[h][:, u, :, :], two_rows, row_values[1, h, u])
+
+        def gpsimd_copy(out, in_):
+            nc.gpsimd.tensor_scalar(out=out, in0=in_, scalar1=1.0, scalar2=0.0, op0=mybir.AluOpType.mult, op1=mybir.AluOpType.add)
+
+        def gpsimd_pack(dst, src):
+            gpsimd_copy(dst, src.rearrange("p j t -> p t j"))
+
+        def gpsimd_pack_rows(h, lo, hi):
+            gpsimd_pack(r_bf[0, h][:, lo:hi, :], r_rows[:, :, half_columns(h, lo, hi)])
+
+        def pack_pairs(copy, h, lo, hi):
+            copy(
+                out=r_bf[1, h][:, lo:hi, :].rearrange("p t (u i) -> p t u i", u=2),
+                in_=r_pairs[h][:, :, lo:hi, :].rearrange("p u t i -> p t u i"),
             )
 
         def quant_r(c, h):
@@ -254,8 +222,8 @@ def tile_mix_tierg_none_kernel(tc, g, w, out):
 
         words = (K_PASS + PACK) // 2
         nc.gpsimd.iota(ramp[:].bitcast(F32), [[1, words]], base=0, channel_multiplier=-2, allow_small_or_imprecise_dtypes=True)
-        zeros = padded_codes[:, 3 * HALF : 3 * HALF + T]
-        nc.vector.memset(padded_codes[:, 2 * HALF : 5 * HALF], 0)
+        nc.vector.memset(padded_codes[:, ORIGIN[1] : ORIGIN[0]], 0)
+        zeros = padded_codes[:, ORIGIN[0] - T : ORIGIN[0]]
         unread = bank(TILES - 1, "unread")
 
         def warm_ups(codes, scales):
@@ -273,45 +241,44 @@ def tile_mix_tierg_none_kernel(tc, g, w, out):
         warm_ups(zeros[:, 0:P], zeros[:, 0 : P // PACK].bitcast(U8))
         eye_group(0)
         eye_group(1)
-        nc.vector.memset(padded_scales[:, 0 : 5 * HALF].bitcast(U32), 0)
+        nc.vector.memset(padded_scales[:, WAITING : ORIGIN[0]].bitcast(U32), 0)
         quant_eye(0, 2)
         warm_ups(eye_codes[:, tile_columns(0)], eye_scales[:, tile_columns(0)])
-        nc.vector.memset(padded_codes[:, 0:HALF], 0)
-
+        nc.vector.memset(padded_codes[:, 0:WAITING], 0)
         eye_group(2)
         eye_group(3)
+
         cast_g(scalar_copy, 0, 0, G_SPLIT, HALF)
         cast_g(vector_copy, 0, 0, 0, G_SPLIT)
         quant_eye(2, 4)
-        quant_g(0, 0)
-        dequant(0, 0, window=-HALF, first_bank=0)
+        quant_g(0, 0, ORIGIN[0])
+        dequant_rows(0, first_bank=0)
         cast_g(scalar_copy, 0, 1, G_SPLIT, HALF)
         cast_g(vector_copy, 0, 1, 0, G_SPLIT)
-        subtract(0, 0, range(0))
-        quant_g(0, 1)
-        dequant(0, 1, window=0, first_bank=PACK)
-        gpsimd_cast_g(1, 0, 0, 96)
-        cast_g(scalar_copy, 1, 0, 96, HALF)
-        subtract(0, 0, range(0, PACK))
-        quant_g(1, 0)
-        dequant_pairs(0, at=HALF, first_bank=0)
+        quant_g(0, 1, ORIGIN[0] + HALF)
+        dequant_rows(1, first_bank=PACK)
+
+        gpsimd_pack(g_bf[1][:, 0:GPSIMD_CAST, :], g_raw[1, 0][:, :, 0:GPSIMD_CAST])
+        cast_g(scalar_copy, 1, 0, GPSIMD_CAST, HALF)
+        subtract_rows(0)
+        quant_g(1, 0, WAITING)
+        dequant_pairs(0, WAITING, first_bank=0, order=[(u, i) for i in range(2) for u in range(2)])
         cast_g(scalar_copy, 1, 1)
-        gpsimd_pack_r(0, 0, 0, 192)
-        subtract(0, 1, range(PACK))
-        pack_r(vector_copy, 0, 0, 192, HALF)
-        quant_g(1, 1)
-        dequant_pairs(1, at=origin[1] + HALF, first_bank=2)
+        gpsimd_pack_rows(0, 0, GPSIMD_FIRST)
+        subtract_rows(1)
+        pack(vector_copy, r_bf[0, 0][:, GPSIMD_FIRST:HALF, :], r_rows[:, :, GPSIMD_FIRST:HALF])
+        quant_g(1, 1, ORIGIN[1] + HALF)
+        dequant_pairs(1, ORIGIN[1] + HALF, first_bank=2, order=[(u, i) for u in range(2) for i in range(2)])
         quant_r(0, 0)
-        gpsimd_pack_r(0, 1, 0, 128)
-        gpsimd_pack_r(0, 1, 128, 256)
-        subtract_pairs(0, range(1))
-        cast_w(scalar_copy, 0, 0, PAIR)
-        quant_w(0, 0, PAIR)
+
+        gpsimd_pack_rows(1, 0, HALF // 2)
+        gpsimd_pack_rows(1, HALF // 2, HALF)
         for n in range(PAIR):
+            cast_w(scalar_copy, 0, n)
+            quant_w(0, n)
             product(first_tier, 0, n)
-        for n in range(PAIR):
             product(second_tier, 0, n, half_columns(0))
-        subtract_pairs(0, range(1, 2))
+            subtract_pair(0, n)
         cast_w(scalar_copy, 0, 2, PAIR)
         quant_w(0, 2, PAIR)
         for n in (2, 3):
@@ -321,27 +288,28 @@ def tile_mix_tierg_none_kernel(tc, g, w, out):
             product(second_tier, 0, n, half_columns(1))
         for n in (2, 3):
             product(second_tier, 0, n)
-        gpsimd_pack_r(1, 0, 0, 112)
-        gpsimd_pack_r(1, 0, 112, 208)
-        subtract_pairs(1, range(1))
+        pack_pairs(gpsimd_copy, 0, 0, GPSIMD_LAST)
+        pack_pairs(gpsimd_copy, 0, GPSIMD_LAST, 2 * GPSIMD_LAST)
+        subtract_pair(1, 0)
         cast_w(scalar_copy, 0, 4, PAIR)
         quant_w(0, 4, PAIR)
         both_tiers(0, 4, 5)
-        subtract_pairs(1, range(1, 2))
+        subtract_pair(1, 1)
+
         cast_w(scalar_copy, 1, 0, PAIR)
-        pack_pairs(scalar_copy, 0, 208, HALF)
+        pack_pairs(scalar_copy, 0, 2 * GPSIMD_LAST, HALF)
         cast_w(scalar_copy, 1, 2)
-        pack_pairs(scalar_copy, 1, HALF - 96, HALF)
+        pack_pairs(scalar_copy, 1, HALF - SCALAR_COLUMNS, HALF)
         cast_w(scalar_copy, 1, 3)
-        move_to_its_pass()
+        leave_waiting_place()
         quant_w(1, 0, PAIR)
-        pack_pairs(vector_copy, 1, 0, HALF - 96)
+        pack_pairs(vector_copy, 1, 0, HALF - SCALAR_COLUMNS)
         for n in range(PAIR):
             product(first_tier, 1, n)
-        for h in (0, 1):
+        for h in range(2):
             quant_r(1, h)
-            product(second_tier, 1, 0, half_columns(h))
-        product(second_tier, 1, 1)
+            for n in range(PAIR):
+                product(second_tier, 1, n, half_columns(h))
         for n in (2, 3):
             quant_w(1, n)
             both_tiers(1, n)

@@ -30,7 +30,6 @@ G_SPLIT = 160
 GPSIMD_CAST = 96
 GPSIMD_FIRST = 192
 GPSIMD_LAST = 104
-SCALAR_COLUMNS = 96
 
 
 def tile_mix_tierg_none_kernel(tc, g, w, out):
@@ -298,12 +297,9 @@ def tile_mix_tierg_none_kernel(tc, g, w, out):
 
         cast_w(scalar_copy, 1, 0, PAIR)
         pack_pairs(scalar_copy, 0, 2 * GPSIMD_LAST, HALF)
-        cast_w(scalar_copy, 1, 2)
-        pack_pairs(scalar_copy, 1, HALF - SCALAR_COLUMNS, HALF)
-        cast_w(scalar_copy, 1, 3)
         leave_waiting_place()
         quant_w(1, 0, PAIR)
-        pack_pairs(vector_copy, 1, 0, HALF - SCALAR_COLUMNS)
+        pack_pairs(vector_copy, 1, 0, HALF)
         for n in range(PAIR):
             product(first_tier, 1, n)
         for h in range(2):
@@ -311,6 +307,7 @@ def tile_mix_tierg_none_kernel(tc, g, w, out):
             for n in range(PAIR):
                 product(second_tier, 1, n, half_columns(h))
         for n in (2, 3):
+            cast_w(scalar_copy, 1, n)
             quant_w(1, n)
             both_tiers(1, n)
 
@@ -319,20 +316,21 @@ def tile_mix_tierg_none_kernel(tc, g, w, out):
         for h in range(2):
             finish(scalar_copy, 0, half_columns(h))
         finish(scalar_copy, 1)
-        cast_w(vector_copy, 0, 6)
         quant_w(1, 4, PAIR)
         both_tiers(1, 4, 5)
-        cast_w(vector_copy, 0, 7)
         finish(scalar_copy, 2)
         finish(scalar_copy, 3)
 
-        cast_w(vector_copy, 1, 6)
-        quant_w(0, 6, PAIR)
+        cast_w(vector_copy, 0, 6)
+        cast_w(vector_copy, 0, 7)
+        quant_w(0, 6)
         both_tiers(0, 6)
+        cast_w(vector_copy, 1, 6)
+        quant_w(0, 7)
         quant_w(1, 6)
-        cast_w(vector_copy, 1, 7)
         both_tiers(1, 6)
         both_tiers(0, 7)
+        cast_w(vector_copy, 1, 7)
         quant_w(1, 7)
         both_tiers(1, 7)
         finish(scalar_copy, 4)

@@ -22,14 +22,12 @@ TILES = N // P
 PAIR = 2
 RUN = 4
 ALIGN = 256
-PLACES = 7
-WAITING = HALF
+PLACES = 9
 ORIGIN = (5 * HALF, 2 * HALF)
+WAITING = (7 * HALF, HALF)
 WARM_UPS = 2
 G_SPLIT = 160
 GPSIMD_CAST = 96
-GPSIMD_FIRST = 192
-GPSIMD_LAST = 104
 
 
 def tile_mix_tierg_none_kernel(tc, g, w, out):
@@ -48,22 +46,21 @@ def tile_mix_tierg_none_kernel(tc, g, w, out):
             return [tile(label + str(i), shape, dtype) for i in range(count)]
 
         halves = ((0, 0), (0, 1), (1, 0), (1, 1))
-        g_bf = tiles("g_bf", PASSES, [P, T, PACK], BF16)
+        g_bf = {(c, h): tile("g_bf" + str(2 * c + h), [P, HALF, PACK], BF16) for c, h in halves}
         padded_codes = tile("gq_codes", [P, PLACES * HALF], U32)
         padded_scales = tile("gq_scales", [P, PLACES * HALF], U8)
         gq_codes = [padded_codes[:, ORIGIN[c] : ORIGIN[c] + T] for c in range(PASSES)]
         gq_scales = [padded_scales[:, ORIGIN[c] : ORIGIN[c] + T] for c in range(PASSES)]
-        r_rows = tile("r_rows", [P, PACK, T], BF16)
-        r_pairs = tiles("r_pairs", 2, [P, 2, HALF, 2], BF16)
+        r_pairs = {(c, h): tile("r_pairs" + str(2 * c + h), [P, 2, HALF, 2], BF16) for c, h in halves}
         eye_codes = tile("eye_codes", [P, K_PASS], U32)
         eye_scales = tile("eye_scales", [P, K_PASS], U8)
         r_own = tiles("r_bf", PASSES, [P, HALF, PACK], BF16)
         gr_codes = tiles("gr_codes", PASSES, [P, T], U32)
         gr_scales = tiles("gr_scales", PASSES, [P, T], U8)
-        w_bf = tiles("w_bf", PASSES, [P, N, PACK], BF16)
+        w_bf = [tiles("w_bf" + str(c), TILES // PAIR, [P, PAIR * P, PACK], BF16) for c in range(PASSES)]
         w_codes = tiles("w_codes", PASSES, [P, N], U32)
         w_scales = tiles("w_scales", PASSES, [P, N], U8)
-        r_bf = {(0, 0): r_own[0][:], (0, 1): g_bf[1][:, HALF:T, :], (1, 0): w_bf[0][:, HALF:T, :], (1, 1): r_own[1][:]}
+        r_bf = {(0, 0): r_own[0][:], (0, 1): g_bf[1, 1][:], (1, 0): w_bf[0][1][:], (1, 1): r_own[1][:]}
         ramp = tile("ramp", [P, K_PASS + PACK], BF16)
         eye_bf = tile("eye_bf", [P, PACK * K_PASS], BF16)
         g_raw = {(c, h): tile("g_raw" + str(2 * c + h), [P, PACK, HALF], F32) for c, h in halves}
@@ -73,8 +70,8 @@ def tile_mix_tierg_none_kernel(tc, g, w, out):
         def bank(b, label):
             return ps.tile([P, T], F32, name=label, tag="bank" + str(b))
 
-        def half_columns(h, lo=0, hi=HALF):
-            return slice(h * HALF + lo, h * HALF + hi)
+        def half_columns(h):
+            return slice(h * HALF, (h + 1) * HALF)
 
         def tile_columns(n, count=1):
             return slice(n * P, (n + count) * P)
@@ -106,14 +103,11 @@ def tile_mix_tierg_none_kernel(tc, g, w, out):
             quantize(eye_codes[:, cols], eye_scales[:, cols], eye_bf[:, lo * K_PASS : hi * K_PASS], E4M3)
 
         def cast_g(copy, c, h, lo=0, hi=HALF):
-            pack(copy, g_bf[c][:, half_columns(h, lo, hi), :], g_raw[c, h][:, :, lo:hi])
+            pack(copy, g_bf[c, h][:, lo:hi, :], g_raw[c, h][:, :, lo:hi])
 
-        def quant_g(c, h, first_word):
-            cols = half_columns(h)
-            quantize_packed(padded_codes[:, first_word : first_word + HALF], gq_scales[c][:, cols], g_bf[c][:, cols, :], E5M2)
-
-        def leave_waiting_place():
-            vector_copy(out=gq_codes[1][:, half_columns(0)].bitcast(I32), in_=padded_codes[:, WAITING : WAITING + HALF].bitcast(I32))
+        def quant_g(c, h, first_word, first_scale):
+            codes = padded_codes[:, first_word : first_word + HALF]
+            quantize_packed(codes, padded_scales[:, first_scale : first_scale + HALF], g_bf[c, h][:], E5M2)
 
         row_values = {}
 
@@ -128,45 +122,32 @@ def tile_mix_tierg_none_kernel(tc, g, w, out):
                 stop=stop,
             )
 
-        def dequant_rows(h, first_bank):
-            window = ORIGIN[0] + (h - 1) * HALF
-            for j in range(PACK):
-                target = bank(first_bank + j, "row_values")
-                dequant_row(target, j, window, window, True, True)
-                row_values[0, h, j] = target[:, half_columns(1)]
+        bank_by_bank = [(u, i) for u in range(2) for i in range(2)]
+        row_by_row = [(u, i) for i in range(2) for u in range(2)]
 
-        def dequant_pairs(h, first_word, first_bank, order):
+        def dequant_pairs(c, h, first_word, first_scale, first_bank, order):
             targets = [bank(first_bank + u, "row_values") for u in range(2)]
             for u, i in order:
-                dequant_row(targets[u], 2 * u + i, first_word - i * HALF, ORIGIN[1] + (h - i) * HALF, i == 0, i == 1)
+                dequant_row(targets[u], 2 * u + i, first_word - i * HALF, first_scale - i * HALF, i == 0, i == 1)
             for u in range(2):
-                row_values[1, h, u] = targets[u][:].rearrange("p (i t) -> p t i", i=2)
+                row_values[c, h, u] = targets[u][:].rearrange("p (i t) -> p t i", i=2)
 
-        def subtract(dst, g_values, gq_values):
-            nc.vector.tensor_tensor(out=dst, in0=g_values, in1=gq_values, op=mybir.AluOpType.subtract)
-
-        def subtract_rows(h):
-            for j in range(PACK):
-                subtract(r_rows[:, j, half_columns(h)], g_raw[0, h][:, j, :], row_values[0, h, j])
-
-        def subtract_pair(h, u):
-            two_rows = g_raw[1, h][:, 2 * u : 2 * u + 2, :].rearrange("p i t -> p t i")
-            subtract(r_pairs[h][:, u, :, :], two_rows, row_values[1, h, u])
-
-        def gpsimd_copy(out, in_):
-            nc.gpsimd.tensor_scalar(out=out, in0=in_, scalar1=1.0, scalar2=0.0, op0=mybir.AluOpType.mult, op1=mybir.AluOpType.add)
-
-        def gpsimd_pack(dst, src):
-            gpsimd_copy(dst, src.rearrange("p j t -> p t j"))
-
-        def gpsimd_pack_rows(h, lo, hi):
-            gpsimd_pack(r_bf[0, h][:, lo:hi, :], r_rows[:, :, half_columns(h, lo, hi)])
-
-        def pack_pairs(copy, h, lo, hi):
-            copy(
-                out=r_bf[1, h][:, lo:hi, :].rearrange("p t (u i) -> p t u i", u=2),
-                in_=r_pairs[h][:, :, lo:hi, :].rearrange("p u t i -> p t u i"),
+        def subtract_pair(c, h, u):
+            nc.vector.tensor_tensor(
+                out=r_pairs[c, h][:, u, :, :],
+                in0=g_raw[c, h][:, 2 * u : 2 * u + 2, :].rearrange("p i t -> p t i"),
+                in1=row_values[c, h, u],
+                op=mybir.AluOpType.subtract,
             )
+
+        def gpsimd_pack_pairs(c, h):
+            nc.gpsimd.tensor_copy(
+                out=r_bf[c, h].bitcast(U32),
+                in_=r_pairs[c, h][:].rearrange("p u t i -> p u (t i)").bitcast(U32).rearrange("p u t -> p t u"),
+            )
+
+        def leave_waiting_place(c, h):
+            nc.gpsimd.tensor_copy(out=gq_codes[c][:, half_columns(h)], in_=padded_codes[:, WAITING[c] : WAITING[c] + HALF])
 
         def quant_r(c, h):
             cols = half_columns(h)
@@ -174,11 +155,11 @@ def tile_mix_tierg_none_kernel(tc, g, w, out):
 
         def cast_w(copy, c, n, count=1):
             side = n % PAIR
-            pack(copy, w_bf[c][:, tile_columns(n, count), :], w_raw[c][n // PAIR][:, :, tile_columns(side, count)])
+            pack(copy, w_bf[c][n // PAIR][:, tile_columns(side, count), :], w_raw[c][n // PAIR][:, :, tile_columns(side, count)])
 
         def quant_w(c, n, count=1):
             cols = tile_columns(n, count)
-            quantize_packed(w_codes[c][:, cols], w_scales[c][:, cols], w_bf[c][:, cols, :], E4M3)
+            quantize_packed(w_codes[c][:, cols], w_scales[c][:, cols], w_bf[c][n // PAIR][:, tile_columns(n % PAIR, count), :], E4M3)
 
         first_tier = (gq_codes, gq_scales, E5M2)
         second_tier = (gr_codes, gr_scales, E4M3)
@@ -240,45 +221,56 @@ def tile_mix_tierg_none_kernel(tc, g, w, out):
         warm_ups(zeros[:, 0:P], zeros[:, 0 : P // PACK].bitcast(U8))
         eye_group(0)
         eye_group(1)
-        nc.vector.memset(padded_scales[:, WAITING : ORIGIN[0]].bitcast(U32), 0)
+        nc.vector.memset(padded_scales[:, WAITING[1] :].bitcast(U32), 0)
         quant_eye(0, 2)
         warm_ups(eye_codes[:, tile_columns(0)], eye_scales[:, tile_columns(0)])
-        nc.vector.memset(padded_codes[:, 0:WAITING], 0)
+        nc.vector.memset(padded_codes[:, WAITING[0] - HALF :].rearrange("p (place word) -> p place word", word=HALF)[:, 0:3:2, :], 0)
         eye_group(2)
         eye_group(3)
 
         cast_g(scalar_copy, 0, 0, G_SPLIT, HALF)
         cast_g(vector_copy, 0, 0, 0, G_SPLIT)
         quant_eye(2, 4)
-        quant_g(0, 0, ORIGIN[0])
-        dequant_rows(0, first_bank=0)
+        quant_g(0, 0, ORIGIN[0], ORIGIN[0])
+        dequant_pairs(0, 0, ORIGIN[0], ORIGIN[0], 0, bank_by_bank)
         cast_g(scalar_copy, 0, 1, G_SPLIT, HALF)
         cast_g(vector_copy, 0, 1, 0, G_SPLIT)
-        quant_g(0, 1, ORIGIN[0] + HALF)
-        dequant_rows(1, first_bank=PACK)
+        nc.vector.memset(padded_codes[:, 0 : WAITING[1]], 0)
+        quant_g(0, 1, WAITING[0], WAITING[0])
+        dequant_pairs(0, 1, WAITING[0], WAITING[0], 2, bank_by_bank)
 
-        gpsimd_pack(g_bf[1][:, 0:GPSIMD_CAST, :], g_raw[1, 0][:, :, 0:GPSIMD_CAST])
+        nc.gpsimd.tensor_scalar(
+            out=g_bf[1, 0][:, 0:GPSIMD_CAST, :],
+            in0=g_raw[1, 0][:, :, 0:GPSIMD_CAST].rearrange("p j t -> p t j"),
+            scalar1=1.0,
+            scalar2=0.0,
+            op0=mybir.AluOpType.mult,
+            op1=mybir.AluOpType.add,
+        )
         cast_g(scalar_copy, 1, 0, GPSIMD_CAST, HALF)
-        subtract_rows(0)
-        quant_g(1, 0, WAITING)
-        dequant_pairs(0, WAITING, first_bank=0, order=[(u, i) for i in range(2) for u in range(2)])
+        for u in range(2):
+            subtract_pair(0, 0, u)
+        quant_g(1, 0, WAITING[1], ORIGIN[1])
+        dequant_pairs(1, 0, WAITING[1], ORIGIN[1], 0, row_by_row)
         cast_g(scalar_copy, 1, 1)
-        gpsimd_pack_rows(0, 0, GPSIMD_FIRST)
-        subtract_rows(1)
-        pack(vector_copy, r_bf[0, 0][:, GPSIMD_FIRST:HALF, :], r_rows[:, :, GPSIMD_FIRST:HALF])
-        quant_g(1, 1, ORIGIN[1] + HALF)
-        dequant_pairs(1, ORIGIN[1] + HALF, first_bank=2, order=[(u, i) for u in range(2) for i in range(2)])
+        gpsimd_pack_pairs(0, 0)
+        leave_waiting_place(0, 1)
+        for u in range(2):
+            subtract_pair(0, 1, u)
+        vector_copy(out=gq_scales[0][:, half_columns(1)].bitcast(I32), in_=padded_scales[:, WAITING[0] : WAITING[0] + HALF].bitcast(I32))
+        quant_g(1, 1, ORIGIN[1] + HALF, ORIGIN[1] + HALF)
+        dequant_pairs(1, 1, ORIGIN[1] + HALF, ORIGIN[1] + HALF, 2, bank_by_bank)
         quant_r(0, 0)
 
-        gpsimd_pack_rows(1, 0, HALF // 2)
-        gpsimd_pack_rows(1, HALF // 2, HALF)
+        gpsimd_pack_pairs(0, 1)
         for n in range(PAIR):
             cast_w(scalar_copy, 0, n)
+        cast_w(scalar_copy, 0, 2, PAIR)
+        for n in range(PAIR):
             quant_w(0, n)
             product(first_tier, 0, n)
             product(second_tier, 0, n, half_columns(0))
-            subtract_pair(0, n)
-        cast_w(scalar_copy, 0, 2, PAIR)
+            subtract_pair(1, 0, n)
         quant_w(0, 2, PAIR)
         for n in (2, 3):
             product(first_tier, 0, n)
@@ -287,19 +279,17 @@ def tile_mix_tierg_none_kernel(tc, g, w, out):
             product(second_tier, 0, n, half_columns(1))
         for n in (2, 3):
             product(second_tier, 0, n)
-        pack_pairs(gpsimd_copy, 0, 0, GPSIMD_LAST)
-        pack_pairs(gpsimd_copy, 0, GPSIMD_LAST, 2 * GPSIMD_LAST)
-        subtract_pair(1, 0)
+        gpsimd_pack_pairs(1, 0)
+        leave_waiting_place(1, 0)
+        subtract_pair(1, 1, 0)
         cast_w(scalar_copy, 0, 4, PAIR)
         quant_w(0, 4, PAIR)
         both_tiers(0, 4, 5)
-        subtract_pair(1, 1)
+        subtract_pair(1, 1, 1)
 
         cast_w(scalar_copy, 1, 0, PAIR)
-        pack_pairs(scalar_copy, 0, 2 * GPSIMD_LAST, HALF)
-        leave_waiting_place()
         quant_w(1, 0, PAIR)
-        pack_pairs(vector_copy, 1, 0, HALF)
+        vector_copy(out=r_bf[1, 1].rearrange("p t (u i) -> p t u i", u=2), in_=r_pairs[1, 1][:].rearrange("p u t i -> p t u i"))
         for n in range(PAIR):
             product(first_tier, 1, n)
         for h in range(2):

@@ -8,7 +8,6 @@ FLOPS = 2 * 2 * K * N * T
 F32 = mybir.dt.float32
 BF16 = mybir.dt.bfloat16
 U32 = mybir.dt.uint32
-I32 = mybir.dt.int32
 U8 = mybir.dt.uint8
 E4M3 = mybir.dt.float8_e4m3fn_x4
 E5M2 = mybir.dt.float8_e5m2_x4
@@ -17,17 +16,13 @@ P = 128
 PACK = 4
 K_PASS = P * PACK
 PASSES = K // K_PASS
-HALF = T // 2
+QUARTERS = T // P
 TILES = N // P
-PAIR = 2
 RUN = 4
+SUB_RUN = 4
 ALIGN = 256
-PLACES = 9
-ORIGIN = (5 * HALF, 2 * HALF)
-WAITING = (7 * HALF, HALF)
-WARM_UPS = 2
-G_SPLIT = 160
-GPSIMD_CAST = 96
+WARM_UPS = 4
+W_LOADS = ((0, 0, 4), (1, 0, 4), (0, 4, 4), (1, 4, 2), (1, 6, 2))
 
 
 def tile_mix_tierg_none_kernel(tc, g, w, out):
@@ -45,42 +40,39 @@ def tile_mix_tierg_none_kernel(tc, g, w, out):
         def tiles(label, count, shape, dtype):
             return [tile(label + str(i), shape, dtype) for i in range(count)]
 
-        halves = ((0, 0), (0, 1), (1, 0), (1, 1))
-        g_bf = {(c, h): tile("g_bf" + str(2 * c + h), [P, HALF, PACK], BF16) for c, h in halves}
-        padded_codes = tile("gq_codes", [P, PLACES * HALF], U32)
-        padded_scales = tile("gq_scales", [P, PLACES * HALF], U8)
-        gq_codes = [padded_codes[:, ORIGIN[c] : ORIGIN[c] + T] for c in range(PASSES)]
-        gq_scales = [padded_scales[:, ORIGIN[c] : ORIGIN[c] + T] for c in range(PASSES)]
-        r_pairs = {(c, h): tile("r_pairs" + str(2 * c + h), [P, 2, HALF, 2], BF16) for c, h in halves}
-        eye_codes = tile("eye_codes", [P, K_PASS], U32)
-        eye_scales = tile("eye_scales", [P, K_PASS], U8)
-        r_own = tiles("r_bf", PASSES, [P, HALF, PACK], BF16)
+        g_raw = tiles("g_raw", PASSES, [P, PACK, T], F32)
+        g_bf = tiles("g_bf", PASSES, [P, T, PACK], BF16)
+        gq_codes = tiles("gq_codes", PASSES, [P, T], U32)
+        gq_scales = tiles("gq_scales", PASSES, [P, T], U8)
+        r_bf = tiles("r_bf", PASSES, [P, T, PACK], BF16)
         gr_codes = tiles("gr_codes", PASSES, [P, T], U32)
         gr_scales = tiles("gr_scales", PASSES, [P, T], U8)
-        w_bf = [tiles("w_bf" + str(c), TILES // PAIR, [P, PAIR * P, PACK], BF16) for c in range(PASSES)]
+        w_bf = tiles("w_bf", PASSES, [P, N, PACK], BF16)
         w_codes = tiles("w_codes", PASSES, [P, N], U32)
         w_scales = tiles("w_scales", PASSES, [P, N], U8)
-        r_bf = {(0, 0): r_own[0][:], (0, 1): g_bf[1, 1][:], (1, 0): w_bf[0][1][:], (1, 1): r_own[1][:]}
         ramp = tile("ramp", [P, K_PASS + PACK], BF16)
         eye_bf = tile("eye_bf", [P, PACK * K_PASS], BF16)
-        g_raw = {(c, h): tile("g_raw" + str(2 * c + h), [P, PACK, HALF], F32) for c, h in halves}
-        w_raw = [tiles("w_raw" + str(c), TILES // PAIR, [P, PACK, PAIR * P], F32) for c in range(PASSES)]
+        eye_codes = tile("eye_codes", [P, K_PASS], U32)
+        eye_scales = tile("eye_scales", [P, K_PASS], U8)
         result = tiles("result", TILES, [P, T], F32)
 
         def bank(b, label):
             return ps.tile([P, T], F32, name=label, tag="bank" + str(b))
 
-        def half_columns(h):
-            return slice(h * HALF, (h + 1) * HALF)
-
-        def tile_columns(n, count=1):
-            return slice(n * P, (n + count) * P)
+        def columns(first, count=1):
+            return slice(first * P, (first + count) * P)
 
         def pass_rows(x, c):
             return x[c * K_PASS : (c + 1) * K_PASS, :].rearrange("(p j) x -> p j x", j=PACK)
 
+        def from_rows(x, run):
+            return x.rearrange("p j (c i) -> p c j i", i=run)
+
+        def to_packed(x, run):
+            return x.rearrange("p (c i) j -> p c j i", i=run)
+
         def pack(copy, dst, src):
-            copy(out=dst.rearrange("p (c i) j -> p c j i", i=RUN), in_=src.rearrange("p j (c i) -> p c j i", i=RUN))
+            copy(out=to_packed(dst, RUN), in_=from_rows(src, RUN))
 
         def quantize(codes, scales, values, fmt):
             nc.vector.quantize_mx(out=codes.bitcast(fmt), scales=scales, in_=values)
@@ -98,233 +90,202 @@ def tile_mix_tierg_none_kernel(tc, g, w, out):
                 op0=mybir.AluOpType.is_equal,
             )
 
-        def quant_eye(lo, hi):
-            cols = slice(lo * P, hi * P)
-            quantize(eye_codes[:, cols], eye_scales[:, cols], eye_bf[:, lo * K_PASS : hi * K_PASS], E4M3)
+        def quant_eye(first, count):
+            cols = columns(first, count)
+            quantize(eye_codes[:, cols], eye_scales[:, cols], eye_bf[:, first * K_PASS : (first + count) * K_PASS], E4M3)
 
-        def cast_g(copy, c, h, lo=0, hi=HALF):
-            pack(copy, g_bf[c, h][:, lo:hi, :], g_raw[c, h][:, :, lo:hi])
+        def cast_g(copy, c, q, count=1):
+            cols = columns(q, count)
+            pack(copy, g_bf[c][:, cols, :], g_raw[c][:, :, cols])
 
-        def quant_g(c, h, first_word, first_scale):
-            codes = padded_codes[:, first_word : first_word + HALF]
-            quantize_packed(codes, padded_scales[:, first_scale : first_scale + HALF], g_bf[c, h][:], E5M2)
+        def gpsimd_pack(dst, src):
+            nc.gpsimd.tensor_scalar(
+                out=dst, in0=src.rearrange("p j t -> p t j"), scalar1=1.0, scalar2=0.0, op0=mybir.AluOpType.mult, op1=mybir.AluOpType.add
+            )
+
+        def cast_g_columns(copy, c, lo, hi):
+            pack(copy, g_bf[c][:, lo:hi, :], g_raw[c][:, :, lo:hi])
+
+        def quant_g(c, q, count=1):
+            cols = columns(q, count)
+            quantize_packed(gq_codes[c][:, cols], gq_scales[c][:, cols], g_bf[c][:, cols, :], E5M2)
 
         row_values = {}
 
-        def dequant_row(target, j, first_word, first_scale, start, stop):
-            nc.tensor.matmul_mx(
-                out=target[:],
-                lhsT=eye_codes[:, tile_columns(j)].bitcast(E4M3),
-                lhsT_scale=eye_scales[:, tile_columns(j)],
-                rhs=padded_codes[:, first_word : first_word + T].bitcast(E5M2),
-                rhs_scale=padded_scales[:, first_scale : first_scale + T],
-                start=start,
-                stop=stop,
-            )
+        def dequant(c, q):
+            target = bank(QUARTERS * c + q, "row_values")
+            for j in range(PACK):
+                nc.tensor.matmul_mx(
+                    out=target[:, columns(j)],
+                    lhsT=eye_codes[:, columns(j)].bitcast(E4M3),
+                    lhsT_scale=eye_scales[:, columns(j)],
+                    rhs=gq_codes[c][:, columns(q)].bitcast(E5M2),
+                    rhs_scale=gq_scales[c][:, columns(q)],
+                    start=True,
+                    stop=True,
+                )
+            row_values[c, q] = target[:].rearrange("p (j t) -> p j t", j=PACK)
 
-        bank_by_bank = [(u, i) for u in range(2) for i in range(2)]
-        row_by_row = [(u, i) for i in range(2) for u in range(2)]
-
-        def dequant_pairs(c, h, first_word, first_scale, first_bank, order):
-            targets = [bank(first_bank + u, "row_values") for u in range(2)]
-            for u, i in order:
-                dequant_row(targets[u], 2 * u + i, first_word - i * HALF, first_scale - i * HALF, i == 0, i == 1)
-            for u in range(2):
-                row_values[c, h, u] = targets[u][:].rearrange("p (i t) -> p t i", i=2)
-
-        def subtract_pair(c, h, u):
+        def subtract(c, q):
             nc.vector.tensor_tensor(
-                out=r_pairs[c, h][:, u, :, :],
-                in0=g_raw[c, h][:, 2 * u : 2 * u + 2, :].rearrange("p i t -> p t i"),
-                in1=row_values[c, h, u],
+                out=to_packed(r_bf[c][:, columns(q), :], SUB_RUN),
+                in0=from_rows(g_raw[c][:, :, columns(q)], SUB_RUN),
+                in1=from_rows(row_values[c, q], SUB_RUN),
                 op=mybir.AluOpType.subtract,
             )
 
-        def gpsimd_pack_pairs(c, h):
-            nc.gpsimd.tensor_copy(
-                out=r_bf[c, h].bitcast(U32),
-                in_=r_pairs[c, h][:].rearrange("p u t i -> p u (t i)").bitcast(U32).rearrange("p u t -> p t u"),
-            )
+        def quant_r(c, q, count=1):
+            cols = columns(q, count)
+            quantize_packed(gr_codes[c][:, cols], gr_scales[c][:, cols], r_bf[c][:, cols, :], E4M3)
 
-        def leave_waiting_place(c, h):
-            nc.gpsimd.tensor_copy(out=gq_codes[c][:, half_columns(h)], in_=padded_codes[:, WAITING[c] : WAITING[c] + HALF])
-
-        def quant_r(c, h):
-            cols = half_columns(h)
-            quantize_packed(gr_codes[c][:, cols], gr_scales[c][:, cols], r_bf[c, h], E4M3)
+        w_raw = {}
 
         def cast_w(copy, c, n, count=1):
-            side = n % PAIR
-            pack(copy, w_bf[c][n // PAIR][:, tile_columns(side, count), :], w_raw[c][n // PAIR][:, :, tile_columns(side, count)])
+            raw, first = w_raw[c, n]
+            pack(copy, w_bf[c][:, columns(n, count), :], raw[:, :, columns(n - first, count)])
+
+        def cast_w_columns(copy, c, n, lo, hi):
+            raw, first = w_raw[c, n]
+            pack(copy, w_bf[c][:, n * P + lo : n * P + hi, :], raw[:, :, (n - first) * P + lo : (n - first) * P + hi])
 
         def quant_w(c, n, count=1):
-            cols = tile_columns(n, count)
-            quantize_packed(w_codes[c][:, cols], w_scales[c][:, cols], w_bf[c][n // PAIR][:, tile_columns(n % PAIR, count), :], E4M3)
+            cols = columns(n, count)
+            quantize_packed(w_codes[c][:, cols], w_scales[c][:, cols], w_bf[c][:, cols, :], E4M3)
 
         first_tier = (gq_codes, gq_scales, E5M2)
         second_tier = (gr_codes, gr_scales, E4M3)
         acc = {}
-        columns_done = {}
+        passes_done = {}
 
-        def product(tier, c, n, cols=slice(0, T)):
+        def product(tier, c, n, h=None):
             codes, scales, fmt = tier
-            if n not in acc:
-                acc[n] = bank((n + PACK) % TILES, "acc")
-                columns_done[n] = 0
-            width = cols.stop - cols.start
+            cols = slice(0, T) if h is None else columns(2 * h, 2)
+            if (n, h) not in acc:
+                acc[n, h] = bank(n - QUARTERS if h == 1 else n, "acc")
+                passes_done[n, h] = 0
             nc.tensor.matmul_mx(
-                out=acc[n][:, cols],
-                lhsT=w_codes[c][:, tile_columns(n)].bitcast(E4M3),
-                lhsT_scale=w_scales[c][:, tile_columns(n)],
+                out=acc[n, h][:, cols],
+                lhsT=w_codes[c][:, columns(n)].bitcast(E4M3),
+                lhsT_scale=w_scales[c][:, columns(n)],
                 rhs=codes[c][:, cols].bitcast(fmt),
                 rhs_scale=scales[c][:, cols],
-                start=columns_done[n] == 0,
-                stop=columns_done[n] + width == 2 * PASSES * T,
+                start=passes_done[n, h] == 0,
+                stop=passes_done[n, h] == 2 * PASSES - 1,
             )
-            columns_done[n] = columns_done[n] + width
+            passes_done[n, h] = passes_done[n, h] + 1
 
         def both_tiers(c, *tile_numbers):
             for n in tile_numbers:
                 product(first_tier, c, n)
                 product(second_tier, c, n)
 
-        def finish(copy, n, cols=slice(0, T)):
-            copy(out=result[n][:, cols], in_=acc[n][:, cols])
-            nc.sync.dma_start(out=out[tile_columns(n), cols], in_=result[n][:, cols])
+        def finish(copy, n, h=None):
+            cols = slice(0, T) if h is None else columns(2 * h, 2)
+            copy(out=result[n][:, cols], in_=acc[n, h][:, cols])
+            nc.sync.dma_start(out=out[columns(n), cols], in_=result[n][:, cols])
 
-        for c, h in halves:
-            nc.sync.dma_start(out=g_raw[c, h][:], in_=pass_rows(g, c)[:, :, half_columns(h)])
-        last_pair = TILES // PAIR - 1
-        for pairs in (range(last_pair), range(last_pair, last_pair + 1)):
-            for c in range(PASSES):
-                for q in pairs:
-                    nc.sync.dma_start(out=w_raw[c][q][:], in_=pass_rows(w, c)[:, :, tile_columns(PAIR * q, PAIR)])
+        for c in range(PASSES):
+            nc.sync.dma_start(out=g_raw[c][:], in_=pass_rows(g, c))
+        for c, first, count in W_LOADS:
+            raw = tile("w_raw" + str(c) + str(first), [P, PACK, count * P], F32)
+            nc.sync.dma_start(out=raw[:], in_=pass_rows(w, c)[:, :, columns(first, count)])
+            for n in range(first, first + count):
+                w_raw[c, n] = (raw, first)
 
         words = (K_PASS + PACK) // 2
         nc.gpsimd.iota(ramp[:].bitcast(F32), [[1, words]], base=0, channel_multiplier=-2, allow_small_or_imprecise_dtypes=True)
-        nc.vector.memset(padded_codes[:, ORIGIN[1] : ORIGIN[0]], 0)
-        zeros = padded_codes[:, ORIGIN[0] - T : ORIGIN[0]]
-        unread = bank(TILES - 1, "unread")
-
-        def warm_ups(codes, scales):
-            for repeat in range(WARM_UPS):
-                nc.tensor.matmul_mx(
-                    out=unread[:],
-                    lhsT=codes.bitcast(E4M3),
-                    lhsT_scale=scales,
-                    rhs=zeros.bitcast(E5M2),
-                    rhs_scale=zeros[:, 0 : T // PACK].bitcast(U8),
-                    start=True,
-                    stop=True,
-                )
-
-        warm_ups(zeros[:, 0:P], zeros[:, 0 : P // PACK].bitcast(U8))
-        eye_group(0)
-        eye_group(1)
-        nc.vector.memset(padded_scales[:, WAITING[1] :].bitcast(U32), 0)
+        for j in range(PACK):
+            eye_group(j)
         quant_eye(0, 2)
-        warm_ups(eye_codes[:, tile_columns(0)], eye_scales[:, tile_columns(0)])
-        nc.vector.memset(padded_codes[:, WAITING[0] - HALF :].rearrange("p (place word) -> p place word", word=HALF)[:, 0:3:2, :], 0)
-        eye_group(2)
-        eye_group(3)
+        quant_eye(2, 2)
 
-        cast_g(scalar_copy, 0, 0, G_SPLIT, HALF)
-        cast_g(vector_copy, 0, 0, 0, G_SPLIT)
-        quant_eye(2, 4)
-        quant_g(0, 0, ORIGIN[0], ORIGIN[0])
-        dequant_pairs(0, 0, ORIGIN[0], ORIGIN[0], 0, bank_by_bank)
-        cast_g(scalar_copy, 0, 1, G_SPLIT, HALF)
-        cast_g(vector_copy, 0, 1, 0, G_SPLIT)
-        nc.vector.memset(padded_codes[:, 0 : WAITING[1]], 0)
-        quant_g(0, 1, WAITING[0], WAITING[0])
-        dequant_pairs(0, 1, WAITING[0], WAITING[0], 2, bank_by_bank)
+        unread = bank(TILES - 1, "unread")
+        for repeat in range(WARM_UPS):
+            nc.tensor.matmul_mx(
+                out=unread[:],
+                lhsT=eye_codes[:, columns(0)].bitcast(E4M3),
+                lhsT_scale=eye_scales[:, columns(0)],
+                rhs=eye_codes[:].bitcast(E4M3),
+                rhs_scale=eye_scales[:],
+                start=True,
+                stop=True,
+            )
 
-        nc.gpsimd.tensor_scalar(
-            out=g_bf[1, 0][:, 0:GPSIMD_CAST, :],
-            in0=g_raw[1, 0][:, :, 0:GPSIMD_CAST].rearrange("p j t -> p t j"),
-            scalar1=1.0,
-            scalar2=0.0,
-            op0=mybir.AluOpType.mult,
-            op1=mybir.AluOpType.add,
-        )
-        cast_g(scalar_copy, 1, 0, GPSIMD_CAST, HALF)
-        for u in range(2):
-            subtract_pair(0, 0, u)
-        quant_g(1, 0, WAITING[1], ORIGIN[1])
-        dequant_pairs(1, 0, WAITING[1], ORIGIN[1], 0, row_by_row)
-        cast_g(scalar_copy, 1, 1)
-        gpsimd_pack_pairs(0, 0)
-        leave_waiting_place(0, 1)
-        for u in range(2):
-            subtract_pair(0, 1, u)
-        vector_copy(out=gq_scales[0][:, half_columns(1)].bitcast(I32), in_=padded_scales[:, WAITING[0] : WAITING[0] + HALF].bitcast(I32))
-        quant_g(1, 1, ORIGIN[1] + HALF, ORIGIN[1] + HALF)
-        dequant_pairs(1, 1, ORIGIN[1] + HALF, ORIGIN[1] + HALF, 2, bank_by_bank)
-        quant_r(0, 0)
-
-        gpsimd_pack_pairs(0, 1)
-        for n in range(PAIR):
+        cast_g(scalar_copy, 0, 3)
+        cast_g(vector_copy, 0, 0)
+        cast_g(vector_copy, 0, 1)
+        quant_g(0, 0)
+        dequant(0, 0)
+        cast_g(vector_copy, 0, 2)
+        quant_g(0, 1)
+        dequant(0, 1)
+        quant_g(0, 3)
+        quant_g(0, 2)
+        dequant(0, 2)
+        dequant(0, 3)
+        cast_g(scalar_copy, 1, 0)
+        gpsimd_pack(g_bf[1][:, columns(1), :], g_raw[1][:, :, columns(1)])
+        cast_g(scalar_copy, 1, 2, 2)
+        subtract(0, 0)
+        subtract(0, 1)
+        quant_g(1, 0)
+        dequant(1, 0)
+        subtract(0, 2)
+        quant_g(1, 1)
+        dequant(1, 1)
+        subtract(0, 3)
+        quant_g(1, 2, 2)
+        dequant(1, 2)
+        dequant(1, 3)
+        quant_r(0, 0, 4)
+        for n in range(4):
             cast_w(scalar_copy, 0, n)
-        cast_w(scalar_copy, 0, 2, PAIR)
-        for n in range(PAIR):
+        for n in range(4):
             quant_w(0, n)
-            product(first_tier, 0, n)
-            product(second_tier, 0, n, half_columns(0))
-            subtract_pair(1, 0, n)
-        quant_w(0, 2, PAIR)
-        for n in (2, 3):
-            product(first_tier, 0, n)
-        quant_r(0, 1)
-        for n in range(PAIR):
-            product(second_tier, 0, n, half_columns(1))
-        for n in (2, 3):
-            product(second_tier, 0, n)
-        gpsimd_pack_pairs(1, 0)
-        leave_waiting_place(1, 0)
-        subtract_pair(1, 1, 0)
-        cast_w(scalar_copy, 0, 4, PAIR)
-        quant_w(0, 4, PAIR)
-        both_tiers(0, 4, 5)
-        subtract_pair(1, 1, 1)
-
-        cast_w(scalar_copy, 1, 0, PAIR)
-        quant_w(1, 0, PAIR)
-        vector_copy(out=r_bf[1, 1].rearrange("p t (u i) -> p t u i", u=2), in_=r_pairs[1, 1][:].rearrange("p u t i -> p t u i"))
-        for n in range(PAIR):
-            product(first_tier, 1, n)
-        for h in range(2):
-            quant_r(1, h)
-            for n in range(PAIR):
-                product(second_tier, 1, n, half_columns(h))
-        for n in (2, 3):
-            cast_w(scalar_copy, 1, n)
-            quant_w(1, n)
-            both_tiers(1, n)
-
-        cast_w(scalar_copy, 1, 5)
-        cast_w(vector_copy, 1, 4)
-        for h in range(2):
-            finish(scalar_copy, 0, half_columns(h))
-        finish(scalar_copy, 1)
-        quant_w(1, 4, PAIR)
-        both_tiers(1, 4, 5)
-        finish(scalar_copy, 2)
-        finish(scalar_copy, 3)
-
+            both_tiers(0, n)
+            subtract(1, n)
+        cast_w(scalar_copy, 1, 0)
+        cast_w(scalar_copy, 1, 1)
+        cast_w(scalar_copy, 1, 2)
+        quant_w(1, 0)
+        product(first_tier, 1, 0)
+        quant_w(1, 1)
+        product(first_tier, 1, 1)
+        quant_r(1, 0, 4)
+        product(second_tier, 1, 0)
+        product(second_tier, 1, 1)
+        cast_w(vector_copy, 1, 3)
+        quant_w(1, 2)
+        quant_w(1, 3)
+        both_tiers(1, 2, 3)
+        cast_w(scalar_copy, 0, 5)
+        cast_w(vector_copy, 0, 4)
         cast_w(vector_copy, 0, 6)
-        cast_w(vector_copy, 0, 7)
+        quant_w(0, 4)
+        quant_w(0, 5)
+        both_tiers(0, 4, 5)
+        for n in range(4):
+            finish(scalar_copy, n)
+        cast_w(vector_copy, 1, 4)
         quant_w(0, 6)
+        cast_w(vector_copy, 1, 5)
+        quant_w(1, 4)
+        cast_w(vector_copy, 0, 7)
+        quant_w(1, 5)
+        both_tiers(1, 4, 5)
         both_tiers(0, 6)
         cast_w(vector_copy, 1, 6)
         quant_w(0, 7)
+        cast_w(vector_copy, 1, 7)
         quant_w(1, 6)
         both_tiers(1, 6)
-        both_tiers(0, 7)
-        cast_w(vector_copy, 1, 7)
         quant_w(1, 7)
-        both_tiers(1, 7)
+        for h in range(2):
+            for c in range(PASSES):
+                product(first_tier, c, 7, h)
+                product(second_tier, c, 7, h)
         finish(scalar_copy, 4)
         finish(scalar_copy, 5)
         finish(vector_copy, 6)
-        for h in range(2):
-            finish(scalar_copy, 7, half_columns(h))
+        finish(scalar_copy, 7, 0)
+        finish(vector_copy, 7, 1)

@@ -19,10 +19,10 @@ PASSES = K // K_PASS
 QUARTERS = T // P
 TILES = N // P
 RUN = 4
-SUB_RUN = 4
+SUB_RUN = 2
 ALIGN = 256
 WARM_UPS = 4
-W_LOADS = ((0, 0, 4), (1, 0, 4), (0, 4, 4), (1, 4, 2), (1, 6, 2))
+W_LOADS = ((0, 0, 2), (0, 2, 2), (0, 4, 2), (1, 0, 2), (1, 2, 2), (1, 4, 2), (0, 6, 2), (1, 6, 2))
 
 
 def tile_mix_tierg_none_kernel(tc, g, w, out):
@@ -40,14 +40,14 @@ def tile_mix_tierg_none_kernel(tc, g, w, out):
         def tiles(label, count, shape, dtype):
             return [tile(label + str(i), shape, dtype) for i in range(count)]
 
-        g_raw = tiles("g_raw", PASSES, [P, PACK, T], F32)
-        g_bf = tiles("g_bf", PASSES, [P, T, PACK], BF16)
+        g_raw = [tiles("g_raw" + str(c), 2, [P, PACK, T // 2], F32) for c in range(PASSES)]
+        g_bf = [tiles("g_bf" + str(c), QUARTERS, [P, P, PACK], BF16) for c in range(PASSES)]
         gq_codes = tiles("gq_codes", PASSES, [P, T], U32)
         gq_scales = tiles("gq_scales", PASSES, [P, T], U8)
         r_bf = tiles("r_bf", PASSES, [P, T, PACK], BF16)
         gr_codes = tiles("gr_codes", PASSES, [P, T], U32)
         gr_scales = tiles("gr_scales", PASSES, [P, T], U8)
-        w_bf = tiles("w_bf", PASSES, [P, N, PACK], BF16)
+        w_bf = [tiles("w_bf" + str(c), TILES, [P, P, PACK], BF16) for c in range(PASSES)]
         w_codes = tiles("w_codes", PASSES, [P, N], U32)
         w_scales = tiles("w_scales", PASSES, [P, N], U8)
         ramp = tile("ramp", [P, K_PASS + PACK], BF16)
@@ -64,6 +64,9 @@ def tile_mix_tierg_none_kernel(tc, g, w, out):
 
         def pass_rows(x, c):
             return x[c * K_PASS : (c + 1) * K_PASS, :].rearrange("(p j) x -> p j x", j=PACK)
+
+        def raw_quarter(c, q):
+            return g_raw[c][q // 2][:, :, columns(q % 2)]
 
         def from_rows(x, run):
             return x.rearrange("p j (c i) -> p c j i", i=run)
@@ -94,21 +97,11 @@ def tile_mix_tierg_none_kernel(tc, g, w, out):
             cols = columns(first, count)
             quantize(eye_codes[:, cols], eye_scales[:, cols], eye_bf[:, first * K_PASS : (first + count) * K_PASS], E4M3)
 
-        def cast_g(copy, c, q, count=1):
-            cols = columns(q, count)
-            pack(copy, g_bf[c][:, cols, :], g_raw[c][:, :, cols])
+        def cast_g(copy, c, q):
+            pack(copy, g_bf[c][q][:], raw_quarter(c, q))
 
-        def gpsimd_pack(dst, src):
-            nc.gpsimd.tensor_scalar(
-                out=dst, in0=src.rearrange("p j t -> p t j"), scalar1=1.0, scalar2=0.0, op0=mybir.AluOpType.mult, op1=mybir.AluOpType.add
-            )
-
-        def cast_g_columns(copy, c, lo, hi):
-            pack(copy, g_bf[c][:, lo:hi, :], g_raw[c][:, :, lo:hi])
-
-        def quant_g(c, q, count=1):
-            cols = columns(q, count)
-            quantize_packed(gq_codes[c][:, cols], gq_scales[c][:, cols], g_bf[c][:, cols, :], E5M2)
+        def quant_g(c, q):
+            quantize_packed(gq_codes[c][:, columns(q)], gq_scales[c][:, columns(q)], g_bf[c][q][:], E5M2)
 
         row_values = {}
 
@@ -129,7 +122,7 @@ def tile_mix_tierg_none_kernel(tc, g, w, out):
         def subtract(c, q):
             nc.vector.tensor_tensor(
                 out=to_packed(r_bf[c][:, columns(q), :], SUB_RUN),
-                in0=from_rows(g_raw[c][:, :, columns(q)], SUB_RUN),
+                in0=from_rows(raw_quarter(c, q), SUB_RUN),
                 in1=from_rows(row_values[c, q], SUB_RUN),
                 op=mybir.AluOpType.subtract,
             )
@@ -140,17 +133,12 @@ def tile_mix_tierg_none_kernel(tc, g, w, out):
 
         w_raw = {}
 
-        def cast_w(copy, c, n, count=1):
+        def cast_w(copy, c, n):
             raw, first = w_raw[c, n]
-            pack(copy, w_bf[c][:, columns(n, count), :], raw[:, :, columns(n - first, count)])
+            pack(copy, w_bf[c][n][:], raw[:, :, columns(n - first)])
 
-        def cast_w_columns(copy, c, n, lo, hi):
-            raw, first = w_raw[c, n]
-            pack(copy, w_bf[c][:, n * P + lo : n * P + hi, :], raw[:, :, (n - first) * P + lo : (n - first) * P + hi])
-
-        def quant_w(c, n, count=1):
-            cols = columns(n, count)
-            quantize_packed(w_codes[c][:, cols], w_scales[c][:, cols], w_bf[c][:, cols, :], E4M3)
+        def quant_w(c, n):
+            quantize_packed(w_codes[c][:, columns(n)], w_scales[c][:, columns(n)], w_bf[c][n][:], E4M3)
 
         first_tier = (gq_codes, gq_scales, E5M2)
         second_tier = (gr_codes, gr_scales, E4M3)
@@ -185,7 +173,8 @@ def tile_mix_tierg_none_kernel(tc, g, w, out):
             nc.sync.dma_start(out=out[columns(n), cols], in_=result[n][:, cols])
 
         for c in range(PASSES):
-            nc.sync.dma_start(out=g_raw[c][:], in_=pass_rows(g, c))
+            for h in range(2):
+                nc.sync.dma_start(out=g_raw[c][h][:], in_=pass_rows(g, c)[:, :, columns(2 * h, 2)])
         for c, first, count in W_LOADS:
             raw = tile("w_raw" + str(c) + str(first), [P, PACK, count * P], F32)
             nc.sync.dma_start(out=raw[:], in_=pass_rows(w, c)[:, :, columns(first, count)])
@@ -211,22 +200,20 @@ def tile_mix_tierg_none_kernel(tc, g, w, out):
                 stop=True,
             )
 
-        cast_g(scalar_copy, 0, 3)
+        cast_g(scalar_copy, 0, 1)
         cast_g(vector_copy, 0, 0)
-        cast_g(vector_copy, 0, 1)
-        quant_g(0, 0)
-        dequant(0, 0)
+        for q in range(2):
+            quant_g(0, q)
+            dequant(0, q)
+        cast_g(scalar_copy, 0, 3)
         cast_g(vector_copy, 0, 2)
-        quant_g(0, 1)
-        dequant(0, 1)
-        quant_g(0, 3)
         quant_g(0, 2)
         dequant(0, 2)
-        dequant(0, 3)
-        cast_g(scalar_copy, 1, 0)
-        gpsimd_pack(g_bf[1][:, columns(1), :], g_raw[1][:, :, columns(1)])
-        cast_g(scalar_copy, 1, 2, 2)
         subtract(0, 0)
+        quant_g(0, 3)
+        dequant(0, 3)
+        for q in range(QUARTERS):
+            cast_g(scalar_copy, 1, q)
         subtract(0, 1)
         quant_g(1, 0)
         dequant(1, 0)
@@ -234,45 +221,42 @@ def tile_mix_tierg_none_kernel(tc, g, w, out):
         quant_g(1, 1)
         dequant(1, 1)
         subtract(0, 3)
-        quant_g(1, 2, 2)
+        quant_g(1, 2)
         dequant(1, 2)
+        quant_r(0, 0, 2)
+        quant_g(1, 3)
         dequant(1, 3)
-        quant_r(0, 0, 4)
-        for n in range(4):
+        quant_r(0, 2, 2)
+        for n in range(6):
             cast_w(scalar_copy, 0, n)
         for n in range(4):
             quant_w(0, n)
             both_tiers(0, n)
             subtract(1, n)
-        cast_w(scalar_copy, 1, 0)
-        cast_w(scalar_copy, 1, 1)
-        cast_w(scalar_copy, 1, 2)
-        quant_w(1, 0)
-        product(first_tier, 1, 0)
-        quant_w(1, 1)
-        product(first_tier, 1, 1)
-        quant_r(1, 0, 4)
-        product(second_tier, 1, 0)
-        product(second_tier, 1, 1)
-        cast_w(vector_copy, 1, 3)
-        quant_w(1, 2)
-        quant_w(1, 3)
-        both_tiers(1, 2, 3)
-        cast_w(scalar_copy, 0, 5)
-        cast_w(vector_copy, 0, 4)
-        cast_w(vector_copy, 0, 6)
         quant_w(0, 4)
         quant_w(0, 5)
         both_tiers(0, 4, 5)
-        for n in range(4):
-            finish(scalar_copy, n)
+        quant_r(1, 0, 2)
+        for n in range(3):
+            cast_w(scalar_copy, 1, n)
+        quant_w(1, 0)
+        quant_r(1, 2, 2)
+        cast_w(vector_copy, 1, 3)
+        quant_w(1, 1)
+        both_tiers(1, 0, 1)
+        quant_w(1, 2)
         cast_w(vector_copy, 1, 4)
-        quant_w(0, 6)
+        quant_w(1, 3)
+        both_tiers(1, 2, 3)
         cast_w(vector_copy, 1, 5)
         quant_w(1, 4)
-        cast_w(vector_copy, 0, 7)
+        cast_w(vector_copy, 0, 6)
         quant_w(1, 5)
         both_tiers(1, 4, 5)
+        for n in range(6):
+            finish(scalar_copy, n)
+        cast_w(vector_copy, 0, 7)
+        quant_w(0, 6)
         both_tiers(0, 6)
         cast_w(vector_copy, 1, 6)
         quant_w(0, 7)
@@ -284,8 +268,6 @@ def tile_mix_tierg_none_kernel(tc, g, w, out):
             for c in range(PASSES):
                 product(first_tier, c, 7, h)
                 product(second_tier, c, 7, h)
-        finish(scalar_copy, 4)
-        finish(scalar_copy, 5)
         finish(vector_copy, 6)
         finish(scalar_copy, 7, 0)
         finish(vector_copy, 7, 1)

@@ -21,8 +21,8 @@ TILES = N // P
 RUN = 4
 SUB_RUN = 2
 ALIGN = 256
-WARM_UPS = 4
-W_LOADS = ((0, 0, 2), (0, 2, 2), (0, 4, 2), (1, 0, 2), (1, 2, 2), (1, 4, 2), (0, 6, 2), (1, 6, 2))
+WARM_UPS = 2
+W_LOADS = ((0, 0, 2), (0, 2, 2), (0, 4, 2), (1, 0, 2), (1, 2, 2), (1, 4, 2), (0, 6, 2), (1, 6, 1), (1, 7, 1))
 
 
 def tile_mix_tierg_none_kernel(tc, g, w, out):
@@ -119,13 +119,16 @@ def tile_mix_tierg_none_kernel(tc, g, w, out):
                 )
             row_values[c, q] = target[:].rearrange("p (j t) -> p j t", j=PACK)
 
-        def subtract(c, q):
+        def subtract(c, q, part=slice(0, P)):
             nc.vector.tensor_tensor(
-                out=to_packed(r_bf[c][:, columns(q), :], SUB_RUN),
-                in0=from_rows(raw_quarter(c, q), SUB_RUN),
-                in1=from_rows(row_values[c, q], SUB_RUN),
+                out=to_packed(r_bf[c][:, columns(q), :][:, part, :], SUB_RUN),
+                in0=from_rows(raw_quarter(c, q)[:, :, part], SUB_RUN),
+                in1=from_rows(row_values[c, q][:, :, part], SUB_RUN),
                 op=mybir.AluOpType.subtract,
             )
+
+        first_part = slice(0, P // 2)
+        second_part = slice(P // 2, P)
 
         def quant_r(c, q, count=1):
             cols = columns(q, count)
@@ -172,33 +175,46 @@ def tile_mix_tierg_none_kernel(tc, g, w, out):
             copy(out=result[n][:, cols], in_=acc[n, h][:, cols])
             nc.sync.dma_start(out=out[columns(n), cols], in_=result[n][:, cols])
 
-        for c in range(PASSES):
-            for h in range(2):
-                nc.sync.dma_start(out=g_raw[c][h][:], in_=pass_rows(g, c)[:, :, columns(2 * h, 2)])
-        for c, first, count in W_LOADS:
+        def load_g(c, h):
+            nc.sync.dma_start(out=g_raw[c][h][:], in_=pass_rows(g, c)[:, :, columns(2 * h, 2)])
+
+        def load_w(c, first, count):
             raw = tile("w_raw" + str(c) + str(first), [P, PACK, count * P], F32)
             nc.sync.dma_start(out=raw[:], in_=pass_rows(w, c)[:, :, columns(first, count)])
             for n in range(first, first + count):
                 w_raw[c, n] = (raw, first)
 
+        load_g(0, 0)
+        load_g(0, 1)
+        load_g(1, 0)
+        load_w(*W_LOADS[0])
+        load_g(1, 1)
+        for load in W_LOADS[1:]:
+            load_w(*load)
+
         words = (K_PASS + PACK) // 2
         nc.gpsimd.iota(ramp[:].bitcast(F32), [[1, words]], base=0, channel_multiplier=-2, allow_small_or_imprecise_dtypes=True)
+        unread = bank(TILES - 1, "unread")
+
+        def warm_ups(words, scale_bytes):
+            for repeat in range(WARM_UPS):
+                nc.tensor.matmul_mx(
+                    out=unread[:],
+                    lhsT=words[:, columns(0)].bitcast(E4M3),
+                    lhsT_scale=scale_bytes[:, columns(0)],
+                    rhs=words.bitcast(E4M3),
+                    rhs_scale=scale_bytes,
+                    start=True,
+                    stop=True,
+                )
+
+        nc.vector.memset(gr_codes[1][:], 0)
+        warm_ups(gr_codes[1][:], gr_codes[1][:, columns(0)].bitcast(U8))
         for j in range(PACK):
             eye_group(j)
         quant_eye(0, 2)
         quant_eye(2, 2)
-
-        unread = bank(TILES - 1, "unread")
-        for repeat in range(WARM_UPS):
-            nc.tensor.matmul_mx(
-                out=unread[:],
-                lhsT=eye_codes[:, columns(0)].bitcast(E4M3),
-                lhsT_scale=eye_scales[:, columns(0)],
-                rhs=eye_codes[:].bitcast(E4M3),
-                rhs_scale=eye_scales[:],
-                start=True,
-                stop=True,
-            )
+        warm_ups(eye_codes[:], eye_scales[:])
 
         cast_g(scalar_copy, 0, 1)
         cast_g(vector_copy, 0, 0)
@@ -212,8 +228,16 @@ def tile_mix_tierg_none_kernel(tc, g, w, out):
         subtract(0, 0)
         quant_g(0, 3)
         dequant(0, 3)
-        for q in range(QUARTERS):
+        for q in range(2):
             cast_g(scalar_copy, 1, q)
+        for n in range(2):
+            cast_w(scalar_copy, 0, n)
+        for q in range(2, 4):
+            cast_g(scalar_copy, 1, q)
+        for n in range(2, 6):
+            cast_w(scalar_copy, 0, n)
+        for n in range(3):
+            cast_w(scalar_copy, 1, n)
         subtract(0, 1)
         quant_g(1, 0)
         dequant(1, 0)
@@ -221,29 +245,38 @@ def tile_mix_tierg_none_kernel(tc, g, w, out):
         quant_g(1, 1)
         dequant(1, 1)
         subtract(0, 3)
-        quant_g(1, 2)
-        dequant(1, 2)
+        quant_w(0, 0)
+        product(first_tier, 0, 0)
         quant_r(0, 0, 2)
+        quant_w(0, 1)
+        product(first_tier, 0, 1)
+        quant_r(0, 2, 2)
+        quant_g(1, 2)
+        product(second_tier, 0, 0)
+        dequant(1, 2)
+        product(second_tier, 0, 1)
+        subtract(1, 0)
         quant_g(1, 3)
         dequant(1, 3)
-        quant_r(0, 2, 2)
-        for n in range(6):
-            cast_w(scalar_copy, 0, n)
-        for n in range(4):
-            quant_w(0, n)
-            both_tiers(0, n)
-            subtract(1, n)
+        subtract(1, 1, first_part)
+        quant_w(0, 2)
+        both_tiers(0, 2)
+        subtract(1, 1, second_part)
+        subtract(1, 2, first_part)
+        quant_w(0, 3)
+        both_tiers(0, 3)
+        subtract(1, 2, second_part)
         quant_w(0, 4)
+        both_tiers(0, 4)
+        subtract(1, 3)
         quant_w(0, 5)
-        both_tiers(0, 4, 5)
+        both_tiers(0, 5)
         quant_r(1, 0, 2)
-        for n in range(3):
-            cast_w(scalar_copy, 1, n)
         quant_w(1, 0)
         quant_r(1, 2, 2)
-        cast_w(vector_copy, 1, 3)
         quant_w(1, 1)
         both_tiers(1, 0, 1)
+        cast_w(vector_copy, 1, 3)
         quant_w(1, 2)
         cast_w(vector_copy, 1, 4)
         quant_w(1, 3)
@@ -255,14 +288,14 @@ def tile_mix_tierg_none_kernel(tc, g, w, out):
         both_tiers(1, 4, 5)
         for n in range(6):
             finish(scalar_copy, n)
-        cast_w(vector_copy, 0, 7)
+        cast_w(vector_copy, 1, 6)
         quant_w(0, 6)
         both_tiers(0, 6)
-        cast_w(vector_copy, 1, 6)
-        quant_w(0, 7)
-        cast_w(vector_copy, 1, 7)
+        cast_w(vector_copy, 0, 7)
         quant_w(1, 6)
         both_tiers(1, 6)
+        cast_w(vector_copy, 1, 7)
+        quant_w(0, 7)
         quant_w(1, 7)
         for h in range(2):
             for c in range(PASSES):

@@ -44,6 +44,7 @@ def tile_mix_tierg_none_kernel(tc, g, w, out):
         g_bf = [tiles("g_bf" + str(c), QUARTERS, [P, P, PACK], BF16) for c in range(PASSES)]
         gq_codes = tiles("gq_codes", PASSES, [P, T], U32)
         gq_scales = tiles("gq_scales", PASSES, [P, T], U8)
+        r_pairs = [tiles("r_pairs" + str(c), QUARTERS, [P, 2, P, 2], BF16) for c in range(PASSES)]
         r_bf = tiles("r_bf", PASSES, [P, T, PACK], BF16)
         gr_codes = tiles("gr_codes", PASSES, [P, T], U32)
         gr_scales = tiles("gr_scales", PASSES, [P, T], U8)
@@ -130,6 +131,24 @@ def tile_mix_tierg_none_kernel(tc, g, w, out):
         first_part = slice(0, P // 2)
         second_part = slice(P // 2, P)
 
+        def in_pairs(x):
+            return x.rearrange("p (u i) t -> p u t i", i=2)
+
+        def subtract_pairs(c, q):
+            nc.vector.tensor_tensor(
+                out=r_pairs[c][q][:], in0=in_pairs(raw_quarter(c, q)), in1=in_pairs(row_values[c, q]), op=mybir.AluOpType.subtract
+            )
+
+        def pack_pairs(c, q):
+            nc.gpsimd.tensor_copy(
+                out=r_bf[c][:, columns(q), :].bitcast(U32),
+                in_=r_pairs[c][q][:].rearrange("p u t i -> p u (t i)").bitcast(U32).rearrange("p u t -> p t u"),
+            )
+
+        def remainder(c, q):
+            subtract_pairs(c, q)
+            pack_pairs(c, q)
+
         def quant_r(c, q, count=1):
             cols = columns(q, count)
             quantize_packed(gr_codes[c][:, cols], gr_scales[c][:, cols], r_bf[c][:, cols, :], E4M3)
@@ -146,24 +165,28 @@ def tile_mix_tierg_none_kernel(tc, g, w, out):
         first_tier = (gq_codes, gq_scales, E5M2)
         second_tier = (gr_codes, gr_scales, E4M3)
         acc = {}
-        passes_done = {}
+        halves_left = {}
 
-        def product(tier, c, n, h=None):
+        def product(tier, c, n, h=None, split=False):
             codes, scales, fmt = tier
             cols = slice(0, T) if h is None else columns(2 * h, 2)
-            if (n, h) not in acc:
-                acc[n, h] = bank(n - QUARTERS if h == 1 else n, "acc")
-                passes_done[n, h] = 0
+            key = (n, h if split else None)
+            if key not in acc:
+                acc[key] = bank(n - QUARTERS if split and h == 1 else n, "acc")
+                halves_left[key] = 2 * PASSES * (1 if split else 2)
+                first = True
+            else:
+                first = False
+            halves_left[key] = halves_left[key] - (2 if h is None else 1)
             nc.tensor.matmul_mx(
-                out=acc[n, h][:, cols],
+                out=acc[key][:, cols],
                 lhsT=w_codes[c][:, columns(n)].bitcast(E4M3),
                 lhsT_scale=w_scales[c][:, columns(n)],
                 rhs=codes[c][:, cols].bitcast(fmt),
                 rhs_scale=scales[c][:, cols],
-                start=passes_done[n, h] == 0,
-                stop=passes_done[n, h] == 2 * PASSES - 1,
+                start=first,
+                stop=halves_left[key] == 0,
             )
-            passes_done[n, h] = passes_done[n, h] + 1
 
         def both_tiers(c, *tile_numbers):
             for n in tile_numbers:
@@ -225,7 +248,7 @@ def tile_mix_tierg_none_kernel(tc, g, w, out):
         cast_g(vector_copy, 0, 2)
         quant_g(0, 2)
         dequant(0, 2)
-        subtract(0, 0)
+        remainder(0, 0)
         quant_g(0, 3)
         dequant(0, 3)
         for q in range(2):
@@ -238,30 +261,32 @@ def tile_mix_tierg_none_kernel(tc, g, w, out):
             cast_w(scalar_copy, 0, n)
         for n in range(3):
             cast_w(scalar_copy, 1, n)
-        subtract(0, 1)
+        remainder(0, 1)
         quant_g(1, 0)
         dequant(1, 0)
-        subtract(0, 2)
+        remainder(0, 2)
         quant_g(1, 1)
         dequant(1, 1)
-        subtract(0, 3)
+        quant_r(0, 0)
+        remainder(0, 3)
         quant_w(0, 0)
         product(first_tier, 0, 0)
-        quant_r(0, 0, 2)
+        quant_r(0, 1)
+        remainder(1, 0)
         quant_w(0, 1)
+        product(second_tier, 0, 0, 0)
         product(first_tier, 0, 1)
-        quant_r(0, 2, 2)
         quant_g(1, 2)
-        product(second_tier, 0, 0)
+        product(second_tier, 0, 1, 0)
         dequant(1, 2)
-        product(second_tier, 0, 1)
-        subtract(1, 0)
+        subtract(1, 1)
         quant_g(1, 3)
         dequant(1, 3)
-        subtract(1, 1, first_part)
+        quant_r(0, 2, 2)
+        for n in range(2):
+            product(second_tier, 0, n, 1)
         quant_w(0, 2)
         both_tiers(0, 2)
-        subtract(1, 1, second_part)
         subtract(1, 2, first_part)
         quant_w(0, 3)
         both_tiers(0, 3)
@@ -299,8 +324,8 @@ def tile_mix_tierg_none_kernel(tc, g, w, out):
         quant_w(1, 7)
         for h in range(2):
             for c in range(PASSES):
-                product(first_tier, c, 7, h)
-                product(second_tier, c, 7, h)
+                product(first_tier, c, 7, h, True)
+                product(second_tier, c, 7, h, True)
         finish(vector_copy, 6)
         finish(scalar_copy, 7, 0)
         finish(vector_copy, 7, 1)

@@ -22,7 +22,7 @@ RUN = 4
 SUB_RUN = 2
 ALIGN = 256
 WARM_UPS = 2
-W_LOADS = ((0, 0, 2), (0, 2, 2), (0, 4, 2), (1, 0, 2), (1, 2, 2), (1, 4, 2), (0, 6, 2), (1, 6, 1), (1, 7, 1))
+LOADS = (("g", 0, 0, 2), ("g", 0, 2, 2), ("g", 1, 0, 2), ("g", 1, 2, 2), ("w", 0, 0, 2), ("w", 0, 2, 2), ("w", 0, 4, 2), ("w", 1, 0, 2), ("w", 1, 2, 2), ("w", 1, 4, 2), ("w", 0, 6, 2), ("w", 1, 6, 1), ("w", 1, 7, 1))
 
 
 def tile_mix_tierg_none_kernel(tc, g, w, out):
@@ -40,7 +40,6 @@ def tile_mix_tierg_none_kernel(tc, g, w, out):
         def tiles(label, count, shape, dtype):
             return [tile(label + str(i), shape, dtype) for i in range(count)]
 
-        g_raw = [tiles("g_raw" + str(c), 2, [P, PACK, T // 2], F32) for c in range(PASSES)]
         g_bf = [tiles("g_bf" + str(c), QUARTERS, [P, P, PACK], BF16) for c in range(PASSES)]
         gq_codes = tiles("gq_codes", PASSES, [P, T], U32)
         gq_scales = tiles("gq_scales", PASSES, [P, T], U8)
@@ -55,7 +54,7 @@ def tile_mix_tierg_none_kernel(tc, g, w, out):
         eye_bf = tile("eye_bf", [P, PACK * K_PASS], BF16)
         eye_codes = tile("eye_codes", [P, K_PASS], U32)
         eye_scales = tile("eye_scales", [P, K_PASS], U8)
-        result = tiles("result", TILES, [P, T], F32)
+        result = tiles("result", TILES // 2, [P, 2, T], F32)
 
         def bank(b, label):
             return ps.tile([P, T], F32, name=label, tag="bank" + str(b))
@@ -66,8 +65,11 @@ def tile_mix_tierg_none_kernel(tc, g, w, out):
         def pass_rows(x, c):
             return x[c * K_PASS : (c + 1) * K_PASS, :].rearrange("(p j) x -> p j x", j=PACK)
 
+        g_raw = {}
+
         def raw_quarter(c, q):
-            return g_raw[c][q // 2][:, :, columns(q % 2)]
+            raw, first = g_raw[c, q]
+            return raw[:, :, columns(q - first)]
 
         def from_rows(x, run):
             return x.rearrange("p j (c i) -> p c j i", i=run)
@@ -193,27 +195,34 @@ def tile_mix_tierg_none_kernel(tc, g, w, out):
                 product(first_tier, c, n)
                 product(second_tier, c, n)
 
-        def finish(copy, n, h=None):
+        def empty(copy, n, h=None):
             cols = slice(0, T) if h is None else columns(2 * h, 2)
-            copy(out=result[n][:, cols], in_=acc[n, h][:, cols])
-            nc.sync.dma_start(out=out[columns(n), cols], in_=result[n][:, cols])
+            copy(out=result[n // 2][:, n % 2, cols], in_=acc[n, h][:, cols])
 
-        def load_g(c, h):
-            nc.sync.dma_start(out=g_raw[c][h][:], in_=pass_rows(g, c)[:, :, columns(2 * h, 2)])
+        def finish(copy, n, h=None):
+            empty(copy, n, h)
+            cols = slice(0, T) if h is None else columns(2 * h, 2)
+            nc.sync.dma_start(out=out[columns(n), cols], in_=result[n // 2][:, n % 2, cols])
 
-        def load_w(c, first, count):
-            raw = tile("w_raw" + str(c) + str(first), [P, PACK, count * P], F32)
-            nc.sync.dma_start(out=raw[:], in_=pass_rows(w, c)[:, :, columns(first, count)])
-            for n in range(first, first + count):
-                w_raw[c, n] = (raw, first)
+        def finish_in_halves(copy, n):
+            for h in range(2):
+                cols = columns(2 * h, 2)
+                copy(out=result[n // 2][:, n % 2, cols], in_=acc[n, None][:, cols])
+                nc.sync.dma_start(out=out[columns(n), cols], in_=result[n // 2][:, n % 2, cols])
 
-        load_g(0, 0)
-        load_g(0, 1)
-        load_g(1, 0)
-        load_w(*W_LOADS[0])
-        load_g(1, 1)
-        for load in W_LOADS[1:]:
-            load_w(*load)
+        def finish_pair(copy, n):
+            empty(copy, n)
+            empty(copy, n + 1)
+            nc.sync.dma_start(out=out[columns(n, 2), :].rearrange("(i p) t -> p i t", i=2), in_=result[n // 2][:])
+
+        def load(x, label, where, c, first, count):
+            raw = tile(label + str(c) + str(first), [P, PACK, count * P], F32)
+            nc.sync.dma_start(out=raw[:], in_=pass_rows(x, c)[:, :, columns(first, count)])
+            for i in range(first, first + count):
+                where[c, i] = (raw, first)
+
+        for name, c, first, count in LOADS:
+            load(*{"g": (g, "g_raw", g_raw), "w": (w, "w_raw", w_raw)}[name], c, first, count)
 
         words = (K_PASS + PACK) // 2
         nc.gpsimd.iota(ramp[:].bitcast(F32), [[1, words]], base=0, channel_multiplier=-2, allow_small_or_imprecise_dtypes=True)
@@ -251,13 +260,9 @@ def tile_mix_tierg_none_kernel(tc, g, w, out):
         remainder(0, 0)
         quant_g(0, 3)
         dequant(0, 3)
-        for q in range(2):
+        for q in range(QUARTERS):
             cast_g(scalar_copy, 1, q)
-        for n in range(2):
-            cast_w(scalar_copy, 0, n)
-        for q in range(2, 4):
-            cast_g(scalar_copy, 1, q)
-        for n in range(2, 6):
+        for n in range(6):
             cast_w(scalar_copy, 0, n)
         for n in range(3):
             cast_w(scalar_copy, 1, n)
@@ -268,23 +273,18 @@ def tile_mix_tierg_none_kernel(tc, g, w, out):
         quant_g(1, 1)
         dequant(1, 1)
         quant_r(0, 0)
-        remainder(0, 3)
-        quant_w(0, 0)
-        product(first_tier, 0, 0)
-        quant_r(0, 1)
-        remainder(1, 0)
-        quant_w(0, 1)
-        product(second_tier, 0, 0, 0)
-        product(first_tier, 0, 1)
+        subtract(0, 3)
         quant_g(1, 2)
-        product(second_tier, 0, 1, 0)
         dequant(1, 2)
-        subtract(1, 1)
         quant_g(1, 3)
         dequant(1, 3)
-        quant_r(0, 2, 2)
-        for n in range(2):
-            product(second_tier, 0, n, 1)
+        quant_r(0, 1, 3)
+        quant_w(0, 0)
+        both_tiers(0, 0)
+        remainder(1, 0)
+        quant_w(0, 1)
+        both_tiers(0, 1)
+        subtract(1, 1)
         quant_w(0, 2)
         both_tiers(0, 2)
         subtract(1, 2, first_part)
@@ -293,9 +293,10 @@ def tile_mix_tierg_none_kernel(tc, g, w, out):
         subtract(1, 2, second_part)
         quant_w(0, 4)
         both_tiers(0, 4)
-        subtract(1, 3)
+        subtract(1, 3, first_part)
         quant_w(0, 5)
         both_tiers(0, 5)
+        subtract(1, 3, second_part)
         quant_r(1, 0, 2)
         quant_w(1, 0)
         quant_r(1, 2, 2)
@@ -315,17 +316,29 @@ def tile_mix_tierg_none_kernel(tc, g, w, out):
             finish(scalar_copy, n)
         cast_w(vector_copy, 1, 6)
         quant_w(0, 6)
-        both_tiers(0, 6)
+        product(first_tier, 0, 6, 0, True)
+        product(second_tier, 0, 6, 0, True)
+        product(first_tier, 0, 6, 1, True)
+        product(second_tier, 0, 6, 1, True)
         cast_w(vector_copy, 0, 7)
         quant_w(1, 6)
-        both_tiers(1, 6)
+        product(first_tier, 1, 6, 0, True)
+        product(second_tier, 1, 6, 0, True)
+        product(first_tier, 1, 6, 1, True)
+        product(second_tier, 1, 6, 1, True)
         cast_w(vector_copy, 1, 7)
         quant_w(0, 7)
         quant_w(1, 7)
-        for h in range(2):
-            for c in range(PASSES):
-                product(first_tier, c, 7, h, True)
-                product(second_tier, c, 7, h, True)
-        finish(vector_copy, 6)
+        product(first_tier, 0, 7, 0, True)
+        product(second_tier, 0, 7, 0, True)
+        product(first_tier, 1, 7, 0, True)
+        product(second_tier, 1, 7, 0, True)
+        product(first_tier, 0, 7, 1, True)
+        product(second_tier, 0, 7, 1, True)
+        product(first_tier, 1, 7, 1, True)
+        product(second_tier, 1, 7, 1, True)
+        empty(scalar_copy, 6, 0)
+        empty(vector_copy, 6, 1)
+        nc.sync.dma_start(out=out[columns(6), :], in_=result[3][:, 0, :])
         finish(scalar_copy, 7, 0)
         finish(vector_copy, 7, 1)

@@ -21,8 +21,26 @@ TILES = N // P
 RUN = 4
 SUB_RUN = 2
 ALIGN = 256
+LOAD_ALIGN = 4096
+STORE_ALIGN = 2048
 WARM_UPS = 2
-LOADS = (("g", 0, 0, 2), ("g", 0, 2, 2), ("g", 1, 0, 2), ("g", 1, 2, 2), ("w", 0, 0, 2), ("w", 0, 2, 2), ("w", 0, 4, 2), ("w", 1, 0, 2), ("w", 1, 2, 2), ("w", 1, 4, 2), ("w", 0, 6, 2), ("w", 1, 6, 1), ("w", 1, 7, 1))
+SPLIT = {6: 2, 7: 2}
+PAIRED = ((0, 0), (0, 1), (0, 2), (1, 0))
+LOADS = (
+    ("g", 0, 0, 2),
+    ("g", 0, 2, 2),
+    ("g", 1, 0, 2),
+    ("g", 1, 2, 2),
+    ("w", 0, 0, 2),
+    ("w", 0, 2, 2),
+    ("w", 0, 4, 2),
+    ("w", 1, 0, 2),
+    ("w", 1, 2, 2),
+    ("w", 1, 4, 2),
+    ("w", 0, 6, 2),
+    ("w", 1, 6, 1),
+    ("w", 1, 7, 1),
+)
 
 
 def tile_mix_tierg_none_kernel(tc, g, w, out):
@@ -30,6 +48,8 @@ def tile_mix_tierg_none_kernel(tc, g, w, out):
     vector_copy = nc.vector.tensor_copy
     scalar_copy = nc.scalar.copy
     with ExitStack() as ctx:
+        loaded = ctx.enter_context(tc.tile_pool(name="loaded", bufs=1))
+        stored = ctx.enter_context(tc.tile_pool(name="stored", bufs=1))
         sb = ctx.enter_context(tc.tile_pool(name="sb", bufs=1))
         ps = ctx.enter_context(tc.psum_pool(name="ps", bufs=1))
         ctx.enter_context(tc.manual_schedule())
@@ -43,7 +63,7 @@ def tile_mix_tierg_none_kernel(tc, g, w, out):
         g_bf = [tiles("g_bf" + str(c), QUARTERS, [P, P, PACK], BF16) for c in range(PASSES)]
         gq_codes = tiles("gq_codes", PASSES, [P, T], U32)
         gq_scales = tiles("gq_scales", PASSES, [P, T], U8)
-        r_pairs = [tiles("r_pairs" + str(c), QUARTERS, [P, 2, P, 2], BF16) for c in range(PASSES)]
+        r_pairs = {(c, q): tile("r_pairs" + str(c) + str(q), [P, 2, P, 2], BF16) for c, q in PAIRED}
         r_bf = tiles("r_bf", PASSES, [P, T, PACK], BF16)
         gr_codes = tiles("gr_codes", PASSES, [P, T], U32)
         gr_scales = tiles("gr_scales", PASSES, [P, T], U8)
@@ -54,7 +74,7 @@ def tile_mix_tierg_none_kernel(tc, g, w, out):
         eye_bf = tile("eye_bf", [P, PACK * K_PASS], BF16)
         eye_codes = tile("eye_codes", [P, K_PASS], U32)
         eye_scales = tile("eye_scales", [P, K_PASS], U8)
-        result = tiles("result", TILES // 2, [P, 2, T], F32)
+        result = [stored.tile([P, T], F32, name="result" + str(n), align_bytes=STORE_ALIGN) for n in range(TILES)]
 
         def bank(b, label):
             return ps.tile([P, T], F32, name=label, tag="bank" + str(b))
@@ -130,26 +150,27 @@ def tile_mix_tierg_none_kernel(tc, g, w, out):
                 op=mybir.AluOpType.subtract,
             )
 
-        first_part = slice(0, P // 2)
-        second_part = slice(P // 2, P)
+        first_half = slice(0, P // 2)
+        second_half = slice(P // 2, P)
 
         def in_pairs(x):
             return x.rearrange("p (u i) t -> p u t i", i=2)
 
-        def subtract_pairs(c, q):
+        def subtract_by_pairs(c, q):
             nc.vector.tensor_tensor(
-                out=r_pairs[c][q][:], in0=in_pairs(raw_quarter(c, q)), in1=in_pairs(row_values[c, q]), op=mybir.AluOpType.subtract
+                out=r_pairs[c, q][:],
+                in0=in_pairs(raw_quarter(c, q)),
+                in1=in_pairs(row_values[c, q]),
+                op=mybir.AluOpType.subtract,
             )
-
-        def pack_pairs(c, q):
             nc.gpsimd.tensor_copy(
                 out=r_bf[c][:, columns(q), :].bitcast(U32),
-                in_=r_pairs[c][q][:].rearrange("p u t i -> p u (t i)").bitcast(U32).rearrange("p u t -> p t u"),
+                in_=r_pairs[c, q][:].rearrange("p u t i -> p u (t i)").bitcast(U32).rearrange("p u t -> p t u"),
             )
 
-        def remainder(c, q):
-            subtract_pairs(c, q)
-            pack_pairs(c, q)
+        def quant_and_dequant_g(c, q):
+            quant_g(c, q)
+            dequant(c, q)
 
         def quant_r(c, q, count=1):
             cols = columns(q, count)
@@ -167,56 +188,52 @@ def tile_mix_tierg_none_kernel(tc, g, w, out):
         first_tier = (gq_codes, gq_scales, E5M2)
         second_tier = (gr_codes, gr_scales, E4M3)
         acc = {}
-        halves_left = {}
+        quarters_left = {}
 
-        def product(tier, c, n, h=None, split=False):
+        def product(tier, c, n, q=0, count=QUARTERS):
             codes, scales, fmt = tier
-            cols = slice(0, T) if h is None else columns(2 * h, 2)
-            key = (n, h if split else None)
-            if key not in acc:
-                acc[key] = bank(n - QUARTERS if split and h == 1 else n, "acc")
-                halves_left[key] = 2 * PASSES * (1 if split else 2)
-                first = True
-            else:
-                first = False
-            halves_left[key] = halves_left[key] - (2 if h is None else 1)
+            split = SPLIT.get(n, QUARTERS)
+            key = (n, q >= split)
+            first = key not in acc
+            if first:
+                acc[key] = bank(n - QUARTERS if q >= split else n, "acc")
+                quarters_left[key] = 2 * PASSES * (QUARTERS - split if q >= split else split)
+            quarters_left[key] = quarters_left[key] - count
             nc.tensor.matmul_mx(
-                out=acc[key][:, cols],
+                out=acc[key][:, columns(q, count)],
                 lhsT=w_codes[c][:, columns(n)].bitcast(E4M3),
                 lhsT_scale=w_scales[c][:, columns(n)],
-                rhs=codes[c][:, cols].bitcast(fmt),
-                rhs_scale=scales[c][:, cols],
+                rhs=codes[c][:, columns(q, count)].bitcast(fmt),
+                rhs_scale=scales[c][:, columns(q, count)],
                 start=first,
-                stop=halves_left[key] == 0,
+                stop=quarters_left[key] == 0,
             )
+
+        def part_of_both_tiers(c, n, q, count):
+            product(first_tier, c, n, q, count)
+            product(second_tier, c, n, q, count)
 
         def both_tiers(c, *tile_numbers):
             for n in tile_numbers:
                 product(first_tier, c, n)
                 product(second_tier, c, n)
 
-        def empty(copy, n, h=None):
-            cols = slice(0, T) if h is None else columns(2 * h, 2)
-            copy(out=result[n // 2][:, n % 2, cols], in_=acc[n, h][:, cols])
+        def quant_w_and_multiply(c, n):
+            quant_w(c, n)
+            both_tiers(c, n)
 
-        def finish(copy, n, h=None):
-            empty(copy, n, h)
-            cols = slice(0, T) if h is None else columns(2 * h, 2)
-            nc.sync.dma_start(out=out[columns(n), cols], in_=result[n // 2][:, n % 2, cols])
+        def empty(copy, n, q=0, count=QUARTERS):
+            copy(out=result[n][:, columns(q, count)], in_=acc[n, q >= SPLIT.get(n, QUARTERS)][:, columns(q, count)])
 
-        def finish_in_halves(copy, n):
-            for h in range(2):
-                cols = columns(2 * h, 2)
-                copy(out=result[n // 2][:, n % 2, cols], in_=acc[n, None][:, cols])
-                nc.sync.dma_start(out=out[columns(n), cols], in_=result[n // 2][:, n % 2, cols])
+        def store(n, q=0, count=QUARTERS):
+            nc.sync.dma_start(out=out[columns(n), columns(q, count)], in_=result[n][:, columns(q, count)])
 
-        def finish_pair(copy, n):
-            empty(copy, n)
-            empty(copy, n + 1)
-            nc.sync.dma_start(out=out[columns(n, 2), :].rearrange("(i p) t -> p i t", i=2), in_=result[n // 2][:])
+        def finish(copy, n, q=0, count=QUARTERS):
+            empty(copy, n, q, count)
+            store(n, q, count)
 
         def load(x, label, where, c, first, count):
-            raw = tile(label + str(c) + str(first), [P, PACK, count * P], F32)
+            raw = loaded.tile([P, PACK, count * P], F32, name=label + str(c) + str(first), align_bytes=LOAD_ALIGN)
             nc.sync.dma_start(out=raw[:], in_=pass_rows(x, c)[:, :, columns(first, count)])
             for i in range(first, first + count):
                 where[c, i] = (raw, first)
@@ -250,56 +267,47 @@ def tile_mix_tierg_none_kernel(tc, g, w, out):
 
         cast_g(scalar_copy, 0, 1)
         cast_g(vector_copy, 0, 0)
-        for q in range(2):
-            quant_g(0, q)
-            dequant(0, q)
+        quant_and_dequant_g(0, 0)
+        quant_and_dequant_g(0, 1)
         cast_g(scalar_copy, 0, 3)
         cast_g(vector_copy, 0, 2)
-        quant_g(0, 2)
-        dequant(0, 2)
-        remainder(0, 0)
-        quant_g(0, 3)
-        dequant(0, 3)
+        quant_and_dequant_g(0, 2)
+
         for q in range(QUARTERS):
             cast_g(scalar_copy, 1, q)
         for n in range(6):
             cast_w(scalar_copy, 0, n)
         for n in range(3):
             cast_w(scalar_copy, 1, n)
-        remainder(0, 1)
-        quant_g(1, 0)
-        dequant(1, 0)
-        remainder(0, 2)
-        quant_g(1, 1)
-        dequant(1, 1)
+
+        subtract_by_pairs(0, 0)
+        quant_and_dequant_g(0, 3)
+        subtract_by_pairs(0, 1)
+        quant_and_dequant_g(1, 0)
+        subtract_by_pairs(0, 2)
+        quant_and_dequant_g(1, 1)
         quant_r(0, 0)
         subtract(0, 3)
-        quant_g(1, 2)
-        dequant(1, 2)
-        quant_g(1, 3)
-        dequant(1, 3)
+        quant_and_dequant_g(1, 2)
+        quant_and_dequant_g(1, 3)
         quant_r(0, 1, 3)
-        quant_w(0, 0)
-        both_tiers(0, 0)
-        remainder(1, 0)
-        quant_w(0, 1)
-        both_tiers(0, 1)
+
+        quant_w_and_multiply(0, 0)
+        subtract_by_pairs(1, 0)
+        quant_w_and_multiply(0, 1)
         subtract(1, 1)
-        quant_w(0, 2)
-        both_tiers(0, 2)
-        subtract(1, 2, first_part)
-        quant_w(0, 3)
-        both_tiers(0, 3)
-        subtract(1, 2, second_part)
-        quant_w(0, 4)
-        both_tiers(0, 4)
-        subtract(1, 3, first_part)
-        quant_w(0, 5)
-        both_tiers(0, 5)
-        subtract(1, 3, second_part)
+        quant_w_and_multiply(0, 2)
+        subtract(1, 2, first_half)
+        quant_w_and_multiply(0, 3)
+        subtract(1, 2, second_half)
+        quant_w_and_multiply(0, 4)
+        subtract(1, 3, first_half)
+        quant_w_and_multiply(0, 5)
+        subtract(1, 3, second_half)
         quant_r(1, 0, 2)
         quant_w(1, 0)
         quant_r(1, 2, 2)
+
         quant_w(1, 1)
         both_tiers(1, 0, 1)
         cast_w(vector_copy, 1, 3)
@@ -314,31 +322,23 @@ def tile_mix_tierg_none_kernel(tc, g, w, out):
         both_tiers(1, 4, 5)
         for n in range(6):
             finish(scalar_copy, n)
+
         cast_w(vector_copy, 1, 6)
         quant_w(0, 6)
-        product(first_tier, 0, 6, 0, True)
-        product(second_tier, 0, 6, 0, True)
-        product(first_tier, 0, 6, 1, True)
-        product(second_tier, 0, 6, 1, True)
+        for q in (0, 2):
+            part_of_both_tiers(0, 6, q, 2)
         cast_w(vector_copy, 0, 7)
         quant_w(1, 6)
-        product(first_tier, 1, 6, 0, True)
-        product(second_tier, 1, 6, 0, True)
-        product(first_tier, 1, 6, 1, True)
-        product(second_tier, 1, 6, 1, True)
+        for q in (0, 2):
+            part_of_both_tiers(1, 6, q, 2)
         cast_w(vector_copy, 1, 7)
         quant_w(0, 7)
         quant_w(1, 7)
-        product(first_tier, 0, 7, 0, True)
-        product(second_tier, 0, 7, 0, True)
-        product(first_tier, 1, 7, 0, True)
-        product(second_tier, 1, 7, 0, True)
-        product(first_tier, 0, 7, 1, True)
-        product(second_tier, 0, 7, 1, True)
-        product(first_tier, 1, 7, 1, True)
-        product(second_tier, 1, 7, 1, True)
-        empty(scalar_copy, 6, 0)
-        empty(vector_copy, 6, 1)
-        nc.sync.dma_start(out=out[columns(6), :], in_=result[3][:, 0, :])
-        finish(scalar_copy, 7, 0)
-        finish(vector_copy, 7, 1)
+        for q in (0, 2):
+            for c in range(PASSES):
+                part_of_both_tiers(c, 7, q, 2)
+        empty(scalar_copy, 6, 0, 2)
+        empty(vector_copy, 6, 2, 2)
+        store(6)
+        finish(scalar_copy, 7, 0, 2)
+        finish(vector_copy, 7, 2, 2)

@@ -21,11 +21,8 @@ TILES = N // P
 RUN = 4
 SUB_RUN = 2
 ALIGN = 256
-LOAD_ALIGN = 4096
-STORE_ALIGN = 2048
 WARM_UPS = 2
 SPLIT = {6: 2, 7: 2}
-PAIRED = ((0, 0), (0, 1), (0, 2), (1, 0))
 LOADS = (
     ("g", 0, 0, 2),
     ("g", 0, 2, 2),
@@ -48,8 +45,6 @@ def tile_mix_tierg_none_kernel(tc, g, w, out):
     vector_copy = nc.vector.tensor_copy
     scalar_copy = nc.scalar.copy
     with ExitStack() as ctx:
-        loaded = ctx.enter_context(tc.tile_pool(name="loaded", bufs=1))
-        stored = ctx.enter_context(tc.tile_pool(name="stored", bufs=1))
         sb = ctx.enter_context(tc.tile_pool(name="sb", bufs=1))
         ps = ctx.enter_context(tc.psum_pool(name="ps", bufs=1))
         ctx.enter_context(tc.manual_schedule())
@@ -63,7 +58,6 @@ def tile_mix_tierg_none_kernel(tc, g, w, out):
         g_bf = [tiles("g_bf" + str(c), QUARTERS, [P, P, PACK], BF16) for c in range(PASSES)]
         gq_codes = tiles("gq_codes", PASSES, [P, T], U32)
         gq_scales = tiles("gq_scales", PASSES, [P, T], U8)
-        r_pairs = {(c, q): tile("r_pairs" + str(c) + str(q), [P, 2, P, 2], BF16) for c, q in PAIRED}
         r_bf = tiles("r_bf", PASSES, [P, T, PACK], BF16)
         gr_codes = tiles("gr_codes", PASSES, [P, T], U32)
         gr_scales = tiles("gr_scales", PASSES, [P, T], U8)
@@ -74,7 +68,7 @@ def tile_mix_tierg_none_kernel(tc, g, w, out):
         eye_bf = tile("eye_bf", [P, PACK * K_PASS], BF16)
         eye_codes = tile("eye_codes", [P, K_PASS], U32)
         eye_scales = tile("eye_scales", [P, K_PASS], U8)
-        result = [stored.tile([P, T], F32, name="result" + str(n), align_bytes=STORE_ALIGN) for n in range(TILES)]
+        result = tiles("result", TILES, [P, T], F32)
 
         def bank(b, label):
             return ps.tile([P, T], F32, name=label, tag="bank" + str(b))
@@ -153,26 +147,11 @@ def tile_mix_tierg_none_kernel(tc, g, w, out):
         first_half = slice(0, P // 2)
         second_half = slice(P // 2, P)
 
-        def in_pairs(x):
-            return x.rearrange("p (u i) t -> p u t i", i=2)
-
-        def subtract_by_pairs(c, q):
-            nc.vector.tensor_tensor(
-                out=r_pairs[c, q][:],
-                in0=in_pairs(raw_quarter(c, q)),
-                in1=in_pairs(row_values[c, q]),
-                op=mybir.AluOpType.subtract,
-            )
-            nc.gpsimd.tensor_copy(
-                out=r_bf[c][:, columns(q), :].bitcast(U32),
-                in_=r_pairs[c, q][:].rearrange("p u t i -> p u (t i)").bitcast(U32).rearrange("p u t -> p t u"),
-            )
-
         def quant_and_dequant_g(c, q):
             quant_g(c, q)
             dequant(c, q)
 
-        def quant_r(c, q, count=1):
+        def quant_r(c, q, count):
             cols = columns(q, count)
             quantize_packed(gr_codes[c][:, cols], gr_scales[c][:, cols], r_bf[c][:, cols, :], E4M3)
 
@@ -233,7 +212,7 @@ def tile_mix_tierg_none_kernel(tc, g, w, out):
             store(n, q, count)
 
         def load(x, label, where, c, first, count):
-            raw = loaded.tile([P, PACK, count * P], F32, name=label + str(c) + str(first), align_bytes=LOAD_ALIGN)
+            raw = tile(label + str(c) + str(first), [P, PACK, count * P], F32)
             nc.sync.dma_start(out=raw[:], in_=pass_rows(x, c)[:, :, columns(first, count)])
             for i in range(first, first + count):
                 where[c, i] = (raw, first)
@@ -280,20 +259,20 @@ def tile_mix_tierg_none_kernel(tc, g, w, out):
         for n in range(3):
             cast_w(scalar_copy, 1, n)
 
-        subtract_by_pairs(0, 0)
+        subtract(0, 0)
         quant_and_dequant_g(0, 3)
-        subtract_by_pairs(0, 1)
+        subtract(0, 1)
         quant_and_dequant_g(1, 0)
-        subtract_by_pairs(0, 2)
+        subtract(0, 2)
         quant_and_dequant_g(1, 1)
-        quant_r(0, 0)
+        quant_r(0, 0, 2)
         subtract(0, 3)
         quant_and_dequant_g(1, 2)
         quant_and_dequant_g(1, 3)
-        quant_r(0, 1, 3)
+        quant_r(0, 2, 2)
 
         quant_w_and_multiply(0, 0)
-        subtract_by_pairs(1, 0)
+        subtract(1, 0)
         quant_w_and_multiply(0, 1)
         subtract(1, 1)
         quant_w_and_multiply(0, 2)

@@ -299,7 +299,9 @@ def tile_mix_tierg_none_kernel(tc, g, w, out):
         cast_w(vector_copy, 0, 6)
         quant_w(1, 5)
         both_tiers(1, 4, 5)
-        for n in range(6):
+        for q in (0, 2):
+            finish(scalar_copy, 0, q, 2)
+        for n in range(1, 6):
             finish(scalar_copy, n)
 
         cast_w(vector_copy, 1, 6)

@@ -21,7 +21,6 @@ TILES = N // P
 RUN = 4
 SUB_RUN = 2
 ALIGN = 256
-WARM_UPS = 2
 SPLIT = {6: 2, 7: 2}
 LOADS = (
     ("g", 0, 0, 2),
@@ -224,25 +223,31 @@ def tile_mix_tierg_none_kernel(tc, g, w, out):
         nc.gpsimd.iota(ramp[:].bitcast(F32), [[1, words]], base=0, channel_multiplier=-2, allow_small_or_imprecise_dtypes=True)
         unread = bank(TILES - 1, "unread")
 
-        def warm_ups(words, scale_bytes):
-            for repeat in range(WARM_UPS):
-                nc.tensor.matmul_mx(
-                    out=unread[:],
-                    lhsT=words[:, columns(0)].bitcast(E4M3),
-                    lhsT_scale=scale_bytes[:, columns(0)],
-                    rhs=words.bitcast(E4M3),
-                    rhs_scale=scale_bytes,
-                    start=True,
-                    stop=True,
-                )
+        def warm_up(stationary, moving):
+            nc.tensor.matmul_mx(
+                out=unread[:],
+                lhsT=stationary[0][:, columns(0)].bitcast(E4M3),
+                lhsT_scale=stationary[1][:, columns(0)],
+                rhs=moving[0].bitcast(E4M3),
+                rhs_scale=moving[1],
+                start=True,
+                stop=True,
+            )
 
+        zeros = (gr_codes[1][:], gr_codes[1][:, columns(0)].bitcast(U8))
+        eye = (eye_codes[:], eye_scales[:])
         nc.vector.memset(gr_codes[1][:], 0)
-        warm_ups(gr_codes[1][:], gr_codes[1][:, columns(0)].bitcast(U8))
-        for j in range(PACK):
-            eye_group(j)
-        quant_eye(0, 2)
+        warm_up(zeros, zeros)
+        warm_up(zeros, zeros)
+        eye_group(0)
+        eye_group(1)
+        quant_eye(0, 1)
+        warm_up(eye, zeros)
+        eye_group(2)
+        eye_group(3)
+        quant_eye(1, 1)
         quant_eye(2, 2)
-        warm_ups(eye_codes[:], eye_scales[:])
+        warm_up(eye, eye)
 
         cast_g(scalar_copy, 0, 1)
         cast_g(vector_copy, 0, 0)

from contextlib import ExitStack

import concourse.mybir as mybir

K, N, T = 1024, 1024, 512
FLOPS = 2 * 2 * K * N * T

F32 = mybir.dt.float32
BF16 = mybir.dt.bfloat16
U32 = mybir.dt.uint32
U8 = mybir.dt.uint8
E4M3 = mybir.dt.float8_e4m3fn_x4
E5M2 = mybir.dt.float8_e5m2_x4

P = 128
PACK = 4
K_PASS = P * PACK
PASSES = K // K_PASS
QUARTERS = T // P
TILES = N // P
RUN = 4
SUB_RUN = 2
ALIGN = 256
SPLIT = {6: 2, 7: 2}
LOADS = (
    ("g", 0, 0, 2),
    ("g", 0, 2, 2),
    ("g", 1, 0, 2),
    ("g", 1, 2, 2),
    ("w", 0, 0, 2),
    ("w", 0, 2, 2),
    ("w", 0, 4, 2),
    ("w", 1, 0, 2),
    ("w", 1, 2, 2),
    ("w", 1, 4, 2),
    ("w", 0, 6, 2),
    ("w", 1, 6, 1),
    ("w", 1, 7, 1),
)


def tile_mix_tierg_none_kernel(tc, g, w, out):
    nc = tc.nc
    vector_copy = nc.vector.tensor_copy
    scalar_copy = nc.scalar.copy
    with ExitStack() as ctx:
        sb = ctx.enter_context(tc.tile_pool(name="sb", bufs=1))
        ps = ctx.enter_context(tc.psum_pool(name="ps", bufs=1))
        ctx.enter_context(tc.manual_schedule())

        def tile(label, shape, dtype):
            return sb.tile(shape, dtype, name=label, align_bytes=ALIGN)

        def tiles(label, count, shape, dtype):
            return [tile(label + str(i), shape, dtype) for i in range(count)]

        g_bf = [tiles("g_bf" + str(c), QUARTERS, [P, P, PACK], BF16) for c in range(PASSES)]
        gq_codes = tiles("gq_codes", PASSES, [P, T], U32)
        gq_scales = tiles("gq_scales", PASSES, [P, T], U8)
        r_bf = tiles("r_bf", PASSES, [P, T, PACK], BF16)
        gr_codes = tiles("gr_codes", PASSES, [P, T], U32)
        gr_scales = tiles("gr_scales", PASSES, [P, T], U8)
        w_bf = [tiles("w_bf" + str(c), TILES, [P, P, PACK], BF16) for c in range(PASSES)]
        w_codes = tiles("w_codes", PASSES, [P, N], U32)
        w_scales = tiles("w_scales", PASSES, [P, N], U8)
        ramp = tile("ramp", [P, K_PASS + PACK], BF16)
        eye_bf = tile("eye_bf", [P, PACK * K_PASS], BF16)
        eye_codes = tile("eye_codes", [P, K_PASS], U32)
        eye_scales = tile("eye_scales", [P, K_PASS], U8)
        result = tiles("result", TILES, [P, T], F32)

        def bank(b, label):
            return ps.tile([P, T], F32, name=label, tag="bank" + str(b))

        def columns(first, count=1):
            return slice(first * P, (first + count) * P)

        def pass_rows(x, c):
            return x[c * K_PASS : (c + 1) * K_PASS, :].rearrange("(p j) x -> p j x", j=PACK)

        g_raw = {}

        def raw_quarter(c, q):
            raw, first = g_raw[c, q]
            return raw[:, :, columns(q - first)]

        def from_rows(x, run):
            return x.rearrange("p j (c i) -> p c j i", i=run)

        def to_packed(x, run):
            return x.rearrange("p (c i) j -> p c j i", i=run)

        def pack(copy, dst, src):
            copy(out=to_packed(dst, RUN), in_=from_rows(src, RUN))

        def quantize(codes, scales, values, fmt):
            nc.vector.quantize_mx(out=codes.bitcast(fmt), scales=scales, in_=values)

        def quantize_packed(codes, scales, values, fmt):
            quantize(codes, scales, values.rearrange("p c j -> p (c j)"), fmt)

        def eye_group(j):
            shift = PACK - 1 - j
            nc.vector.tensor_scalar(
                out=eye_bf[:, j * K_PASS : (j + 1) * K_PASS],
                in0=ramp[:, shift : shift + K_PASS],
                scalar1=1.0,
                scalar2=None,
                op0=mybir.AluOpType.is_equal,
            )

        def quant_eye(first, count):
            cols = columns(first, count)
            quantize(eye_codes[:, cols], eye_scales[:, cols], eye_bf[:, first * K_PASS : (first + count) * K_PASS], E4M3)

        def cast_g(copy, c, q):
            pack(copy, g_bf[c][q][:], raw_quarter(c, q))

        def quant_g(c, q):
            quantize_packed(gq_codes[c][:, columns(q)], gq_scales[c][:, columns(q)], g_bf[c][q][:], E5M2)

        row_values = {}

        def dequant(c, q):
            target = bank(QUARTERS * c + q, "row_values")
            for j in range(PACK):
                nc.tensor.matmul_mx(
                    out=target[:, columns(j)],
                    lhsT=eye_codes[:, columns(j)].bitcast(E4M3),
                    lhsT_scale=eye_scales[:, columns(j)],
                    rhs=gq_codes[c][:, columns(q)].bitcast(E5M2),
                    rhs_scale=gq_scales[c][:, columns(q)],
                    start=True,
                    stop=True,
                )
            row_values[c, q] = target[:].rearrange("p (j t) -> p j t", j=PACK)

        def subtract(c, q, part=slice(0, P)):
            nc.vector.tensor_tensor(
                out=to_packed(r_bf[c][:, columns(q), :][:, part, :], SUB_RUN),
                in0=from_rows(raw_quarter(c, q)[:, :, part], SUB_RUN),
                in1=from_rows(row_values[c, q][:, :, part], SUB_RUN),
                op=mybir.AluOpType.subtract,
            )

        first_half = slice(0, P // 2)
        second_half = slice(P // 2, P)

        def quant_and_dequant_g(c, q):
            quant_g(c, q)
            dequant(c, q)

        def quant_r(c, q, count):
            cols = columns(q, count)
            quantize_packed(gr_codes[c][:, cols], gr_scales[c][:, cols], r_bf[c][:, cols, :], E4M3)

        w_raw = {}

        def cast_w(copy, c, n):
            raw, first = w_raw[c, n]
            pack(copy, w_bf[c][n][:], raw[:, :, columns(n - first)])

        def quant_w(c, n):
            quantize_packed(w_codes[c][:, columns(n)], w_scales[c][:, columns(n)], w_bf[c][n][:], E4M3)

        first_tier = (gq_codes, gq_scales, E5M2)
        second_tier = (gr_codes, gr_scales, E4M3)
        acc = {}
        quarters_left = {}

        def product(tier, c, n, q=0, count=QUARTERS):
            codes, scales, fmt = tier
            split = SPLIT.get(n, QUARTERS)
            key = (n, q >= split)
            first = key not in acc
            if first:
                acc[key] = bank(n - QUARTERS if q >= split else n, "acc")
                quarters_left[key] = 2 * PASSES * (QUARTERS - split if q >= split else split)
            quarters_left[key] = quarters_left[key] - count
            nc.tensor.matmul_mx(
                out=acc[key][:, columns(q, count)],
                lhsT=w_codes[c][:, columns(n)].bitcast(E4M3),
                lhsT_scale=w_scales[c][:, columns(n)],
                rhs=codes[c][:, columns(q, count)].bitcast(fmt),
                rhs_scale=scales[c][:, columns(q, count)],
                start=first,
                stop=quarters_left[key] == 0,
            )

        def part_of_both_tiers(c, n, q, count):
            product(first_tier, c, n, q, count)
            product(second_tier, c, n, q, count)

        def both_tiers(c, *tile_numbers):
            for n in tile_numbers:
                product(first_tier, c, n)
                product(second_tier, c, n)

        def quant_w_and_multiply(c, n):
            quant_w(c, n)
            both_tiers(c, n)

        def empty(copy, n, q=0, count=QUARTERS):
            copy(out=result[n][:, columns(q, count)], in_=acc[n, q >= SPLIT.get(n, QUARTERS)][:, columns(q, count)])

        def store(n, q=0, count=QUARTERS):
            nc.sync.dma_start(out=out[columns(n), columns(q, count)], in_=result[n][:, columns(q, count)])

        def finish(copy, n, q=0, count=QUARTERS):
            empty(copy, n, q, count)
            store(n, q, count)

        def load(x, label, where, c, first, count):
            raw = tile(label + str(c) + str(first), [P, PACK, count * P], F32)
            nc.sync.dma_start(out=raw[:], in_=pass_rows(x, c)[:, :, columns(first, count)])
            for i in range(first, first + count):
                where[c, i] = (raw, first)

        for name, c, first, count in LOADS:
            load(*{"g": (g, "g_raw", g_raw), "w": (w, "w_raw", w_raw)}[name], c, first, count)

        words = (K_PASS + PACK) // 2
        nc.gpsimd.iota(ramp[:].bitcast(F32), [[1, words]], base=0, channel_multiplier=-2, allow_small_or_imprecise_dtypes=True)
        unread = bank(TILES - 1, "unread")

        def warm_up(stationary, moving):
            nc.tensor.matmul_mx(
                out=unread[:],
                lhsT=stationary[0][:, columns(0)].bitcast(E4M3),
                lhsT_scale=stationary[1][:, columns(0)],
                rhs=moving[0].bitcast(E4M3),
                rhs_scale=moving[1],
                start=True,
                stop=True,
            )

        zeros = (gr_codes[1][:], gr_codes[1][:, columns(0)].bitcast(U8))
        eye = (eye_codes[:], eye_scales[:])
        nc.vector.memset(gr_codes[1][:], 0)
        warm_up(zeros, zeros)
        warm_up(zeros, zeros)
        eye_group(0)
        eye_group(1)
        quant_eye(0, 1)
        warm_up(eye, zeros)
        eye_group(2)
        eye_group(3)
        quant_eye(1, 1)
        quant_eye(2, 2)
        warm_up(eye, eye)

        cast_g(scalar_copy, 0, 1)
        cast_g(vector_copy, 0, 0)
        quant_and_dequant_g(0, 0)
        quant_and_dequant_g(0, 1)
        cast_g(scalar_copy, 0, 3)
        cast_g(vector_copy, 0, 2)
        quant_and_dequant_g(0, 2)

        for q in range(QUARTERS):
            cast_g(scalar_copy, 1, q)
        for n in range(6):
            cast_w(scalar_copy, 0, n)
        for n in range(3):
            cast_w(scalar_copy, 1, n)

        subtract(0, 0)
        quant_and_dequant_g(0, 3)
        subtract(0, 1)
        quant_and_dequant_g(1, 0)
        subtract(0, 2)
        quant_and_dequant_g(1, 1)
        quant_r(0, 0, 2)
        subtract(0, 3)
        quant_and_dequant_g(1, 2)
        quant_and_dequant_g(1, 3)
        quant_r(0, 2, 2)

        quant_w_and_multiply(0, 0)
        subtract(1, 0)
        quant_w_and_multiply(0, 1)
        subtract(1, 1)
        quant_w_and_multiply(0, 2)
        subtract(1, 2, first_half)
        quant_w_and_multiply(0, 3)
        subtract(1, 2, second_half)
        quant_w_and_multiply(0, 4)
        subtract(1, 3, first_half)
        quant_w_and_multiply(0, 5)
        subtract(1, 3, second_half)
        quant_r(1, 0, 2)
        quant_w(1, 0)
        quant_r(1, 2, 2)

        quant_w(1, 1)
        both_tiers(1, 0, 1)
        cast_w(vector_copy, 1, 3)
        quant_w(1, 2)
        cast_w(vector_copy, 1, 4)
        quant_w(1, 3)
        both_tiers(1, 2, 3)
        cast_w(vector_copy, 1, 5)
        quant_w(1, 4)
        cast_w(vector_copy, 0, 6)
        quant_w(1, 5)
        both_tiers(1, 4, 5)
        for q in (0, 2):
            finish(scalar_copy, 0, q, 2)
        for n in range(1, 6):
            finish(scalar_copy, n)

        cast_w(vector_copy, 1, 6)
        quant_w(0, 6)
        for q in (0, 2):
            part_of_both_tiers(0, 6, q, 2)
        cast_w(vector_copy, 0, 7)
        quant_w(1, 6)
        for q in (0, 2):
            part_of_both_tiers(1, 6, q, 2)
        cast_w(vector_copy, 1, 7)
        quant_w(0, 7)
        quant_w(1, 7)
        for q in (0, 2):
            for c in range(PASSES):
                part_of_both_tiers(c, 7, q, 2)
        empty(scalar_copy, 6, 0, 2)
        empty(vector_copy, 6, 2, 2)
        store(6)
        finish(scalar_copy, 7, 0, 2)
        finish(vector_copy, 7, 2, 2)
